import numpy as np
import ml_dtypes


def mxq(x, axis, fmt="e4m3"):
    dtype, down = {"e4m3": (ml_dtypes.float8_e4m3fn, 7), "e5m2": (ml_dtypes.float8_e5m2, 14)}[fmt]
    v = np.moveaxis(np.asarray(x, np.float32).astype(ml_dtypes.bfloat16).astype(np.float64), axis, -1)
    blocks = v.reshape(v.shape[:-1] + (-1, 32))
    amax = np.abs(blocks).max(-1, keepdims=True)
    byte = np.maximum(np.where(amax > 0, np.frexp(amax)[1] - 1 + 127, 0) - down, 1)
    scale = np.exp2(byte - 127.0)
    codes = (blocks / scale).astype(np.float32).astype(dtype).astype(np.float64)
    return np.moveaxis((codes * scale).reshape(v.shape), -1, axis)


WIDE = False


def mx_kscale(k):
    if not WIDE:
        return np.ones(k)
    levels = np.array([10, -10, 5, -5, 0])
    if k % 512:
        return np.exp2(np.random.permutation(np.resize(levels, k // 32))).repeat(32)
    a = np.empty((k // 512, 16))
    for p in range(k // 512):
        a[p, :8] = np.random.permutation(np.resize(levels, 8))
        for g in range(8):
            far = levels[np.abs(levels - a[p, g]) >= 10]
            a[p, g + 8] = far[np.random.randint(len(far))]
    return np.exp2(a.ravel()).repeat(32)


def f64(x):
    return np.asarray(x).astype(np.float64)


def striped(idx):
    return np.tile(idx.reshape(-1, 16).T, (8, 1)).astype(np.uint16)


def unstriped(offs):
    return offs[:16].T.reshape(-1).astype(np.int64)


E2M1 = np.array([0.0, 0.5, 1.0, 1.5, 2.0, 3.0, 4.0, 6.0, -0.0, -0.5, -1.0, -1.5, -2.0, -3.0, -4.0, -6.0])


def pack_weight(w, fmt):
    k, n = w.shape
    w = f64(np.asarray(w, np.float32).astype(ml_dtypes.bfloat16)).reshape(k // 32, 32, n)
    amax = np.abs(w).max(1)
    if fmt == "e4m3":
        byte = np.frexp(amax)[1] - 1 + 127 - 7
    else:
        mant, ex = np.frexp(amax / 6.0)
        byte = np.where(mant > 0.5, ex, ex - 1) + 127
    byte = np.clip(np.where(amax > 0, byte, 1), 1, 254)
    scaled = (w * np.exp2(127.0 - byte)[:, None, :]).reshape(k, n).astype(np.float32)
    by_word = np.ascontiguousarray(scaled.reshape(k // 512, 128, 4, n).transpose(0, 1, 3, 2))
    if fmt == "e4m3":
        words = by_word.astype(ml_dtypes.float8_e4m3fn).view(np.uint8)
    else:
        c = by_word.astype(ml_dtypes.float4_e2m1fn).view(np.uint8) & 0xF
        words = (c[..., 0::2] | (c[..., 1::2] << 4)).reshape(k // 512, 128, 2 * n)
    return np.ascontiguousarray(words), np.ascontiguousarray(byte.astype(np.uint8).reshape(k // 512, 16, n))


def unpack_weight(words, scales, fmt):
    g, _, n = scales.shape
    words = np.ascontiguousarray(words).reshape(g, 128, n, -1)
    if fmt == "e4m3":
        vals = words.view(ml_dtypes.float8_e4m3fn).astype(np.float64)
    else:
        nib = np.empty((g, 128, n, 4), np.uint8)
        nib[..., 0::2] = words & 0xF
        nib[..., 1::2] = words >> 4
        vals = E2M1[nib]
    vals = vals * np.repeat(np.exp2(scales.astype(np.float64) - 127.0), 8, axis=1)[..., None]
    return vals.transpose(0, 1, 3, 2).reshape(g * 512, n)


def gelu(v):
    return 0.5 * v * (1.0 + np.tanh(np.sqrt(2.0 / np.pi) * (v + 0.044715 * v**3)))


K, T, S, H, N = 1024, 2048, 1024, 512, 256

def setup_inputs():
    n = np.random.standard_normal
    s = mx_kscale(K)[:, None]
    u = mx_kscale(H)[:, None]
    tab_words, tab_scales = pack_weight(n((K, T)) * s, "e4m3")
    wp_words, wp_scales = pack_weight(0.5 * n((K, H)) / np.sqrt(K) / s, "e2m1")
    wk_words, wk_scales = pack_weight(0.5 * n((K, H)) / np.sqrt(K) / s, "e4m3")
    wt = (0.5 * n((K, H)) / np.sqrt(K) / s).astype(np.float32)
    gain = (np.exp(0.3 * n(H)) * u[:, 0]).astype(np.float32)
    wo = (2.0 * n((H, N)) / np.sqrt(H) / u).astype(np.float32)
    bo = (0.5 * n(N)).astype(np.float32)
    return dict(tab_words=tab_words, tab_scales=tab_scales,
                offs=striped(np.random.permutation(T)[:S]),
                offs2=striped(np.random.permutation(T)[:S]),
                offs3=striped(np.random.permutation(T)[:S]),
                wp_words=wp_words, wp_scales=wp_scales,
                wk_words=wk_words, wk_scales=wk_scales,
                wt=wt, gain=gain, wo=wo, bo=bo)

def reference(tab_words, tab_scales, offs, offs2, offs3, wp_words, wp_scales,
              wk_words, wk_scales, wt, gain, wo, bo):
    vp = unpack_weight(tab_words, tab_scales, "e4m3")[:, unstriped(offs)]
    vk = unpack_weight(tab_words, tab_scales, "e4m3")[:, unstriped(offs2)]
    vt = unpack_weight(tab_words, tab_scales, "e4m3")[:, unstriped(offs3)]
    wp = unpack_weight(wp_words, wp_scales, "e2m1")
    wk = unpack_weight(wk_words, wk_scales, "e4m3")
    a = wp.T @ vp + wk.T @ vk + mxq(f64(wt), 0, "e4m3").T @ vt
    c = np.minimum(np.maximum(a, 0.0), 1.0)
    h = np.square(c) * f64(gain)[:, None]
    y = mxq(f64(wo), 0, "e4m3").T @ mxq(h, 0, "e4m3")
    return y + f64(bo)[:, None]

@@ -1,0 +1,389 @@
+from contextlib import ExitStack
+
+import concourse.mybir as mybir
+from concourse.masks import make_identity
+
+K, T, S, H, N = 1024, 2048, 1024, 512, 256
+FLOPS = 2 * (3 * K * H * S + H * N * S)
+
+F32 = mybir.dt.float32
+BF16 = mybir.dt.bfloat16
+I32 = mybir.dt.int32
+U32 = mybir.dt.uint32
+U16 = mybir.dt.uint16
+U8 = mybir.dt.uint8
+FP8X4 = mybir.dt.float8_e4m3fn_x4
+FP4X4 = mybir.dt.float4_e2m1fn_x4
+ACT = mybir.ActivationFunctionType
+ALU = mybir.AluOpType
+
+P = 128
+PASSES = 2
+CH = 256
+RING = 4
+PIECE, KING, THREAT = 0, 1, 2
+
+
+def tile_list_chess_pattern_evaluation_kernel(
+    tc, tab_words, tab_scales, offs, offs2, offs3, wp_words, wp_scales, wk_words, wk_scales, wt, gain, wo, bo, out
+):
+    nc = tc.nc
+    with ExitStack() as ctx:
+        sb = ctx.enter_context(tc.tile_pool(name="sb", bufs=1))
+        ps = ctx.enter_context(tc.psum_pool(name="ps", bufs=1))
+
+        def tile(name, shape, dtype, tag=None):
+            return sb.tile(shape, dtype, name=name, tag=tag or name, align_bytes=64)
+
+        lists = [tile("list%d" % i, [P, S // 16], U16) for i in range(3)]
+        tab_sc = tile("tab_sc", [P, T], U8)
+        tab_w = [tile("tab_w%d" % a, [P, T], I32) for a in range(PASSES)]
+        wk_sc_raw = tile("wk_sc_raw", [P, H], U8)
+        wk_sc = tile("wk_sc", [P, H], U8)
+        wp_sc_raw = tile("wp_sc_raw", [P, 2 * H], U8)
+        wp_sc = tile("wp_sc", [P, 2 * H], U8)
+        piece_sc = tile("piece_sc", [P, S], U8)
+        piece_sc1 = tile("piece_sc1", [P, S], U8)
+        half_sc = {KING: tile("king_sc", [P, S // 2], U8), THREAT: tile("threat_sc", [P, S // 2], U8)}
+        wt_raw = [tile("wt_raw%d" % a, [P, 4, H], F32) for a in range(PASSES)]
+        wt_bf = [tile("wt_bf%d" % a, [P, 4 * H], BF16) for a in range(PASSES)]
+        wt_q = [tile("wt_q%d" % a, [P, H], U32) for a in range(PASSES)]
+        wt_sc = [tile("wt_sc%d" % a, [P, H], U8) for a in range(PASSES)]
+        wk_raw = tile("wk_raw", [P, PASSES, H], I32)
+        wk_q = tile("wk_q", [P, PASSES * H], I32)
+        wp_raw = tile("wp_raw", [P, PASSES, H // 2], I32)
+        wp_q = tile("wp_q", [P, PASSES * 2 * H], U8)
+        wo_raw = [tile("wo_raw%d" % j, [P, N], F32) for j in range(4)]
+        wo_sgn = tile("wo_sgn", [P, 4, N], BF16)
+        wo_bf = tile("wo_bf", [P, 4 * N], BF16)
+        wo_q = tile("wo_q", [P, N], U32)
+        wo_sc = tile("wo_sc", [P, N], U8)
+        rows = tile("rows", [P, P], F32)
+        ident = tile("ident", [P, P], F32)
+        banks = [ps.tile([P, 512], F32, name="bank%d" % b) for b in range(8)]
+
+        nc.vector.memset(tab_sc[:].bitcast(I32), 0)
+        nc.vector.memset(wk_sc_raw[:].bitcast(I32), 0)
+        nc.vector.memset(wp_sc_raw[:].bitcast(I32), 0)
+        nc.vector.memset(piece_sc1[:].bitcast(I32), 0)
+        nc.gpsimd.memset(rows[:], 0.0)
+
+        nc.sync.dma_start(lists[PIECE][:], offs)
+        for q in range(4):
+            nc.sync.dma_start(
+                out=tab_sc[32 * q : 32 * q + 8, :].bitcast(I32), in_=tab_scales[:, 4 * q : 4 * q + 4, :].bitcast(I32)
+            )
+        nc.sync.dma_start(lists[THREAT][:], offs3)
+        nc.sync.dma_start(lists[KING][:], offs2)
+        make_identity(nc, ident[:])
+
+        def load_wt(a):
+            nc.sync.dma_start(out=wt_raw[a][:], in_=wt[512 * a : 512 * (a + 1), :].rearrange("(p j) c -> p j c", j=4))
+
+        def load_tab(a):
+            nc.sync.dma_start(out=tab_w[a][:], in_=tab_words[a].rearrange("p t i -> p (t i)").bitcast(I32))
+
+        load_wt(0)
+        load_tab(0)
+        nc.sync.dma_start(out=rows[0:4, :], in_=gain.rearrange("(q t e) -> t q e", t=4, e=8))
+        for q in range(4):
+            nc.sync.dma_start(
+                out=wk_sc_raw[32 * q : 32 * q + 8, :].bitcast(I32), in_=wk_scales[:, 4 * q : 4 * q + 4, :].bitcast(I32)
+            )
+        nc.sync.dma_start(out=wk_raw[:], in_=wk_words.rearrange("a p c i -> p a (c i)").bitcast(I32))
+        for q in range(4):
+            nc.sync.dma_start(
+                out=wp_sc_raw[32 * q : 32 * q + 4, :].bitcast(I32).rearrange("r (a c) -> r a c", a=PASSES),
+                in_=wp_scales[:, 4 * q : 4 * q + 4, :].rearrange("a r c -> r a c").bitcast(I32),
+            )
+        nc.sync.dma_start(out=wp_raw[:], in_=wp_words.rearrange("a p c -> p a c").bitcast(I32))
+        load_wt(1)
+        load_tab(1)
+        wo_rows = wo.rearrange("(q j e) n -> j q e n", j=4, e=8)
+        for j in range(4):
+            nc.sync.dma_start(out=wo_raw[j][:], in_=wo_rows[j])
+        bias_sb = tile("bias_sb", [P, 2], F32)
+        with nc.allow_non_contiguous_dma(reason="one bias value a partition"):
+            nc.sync.dma_start(out=bias_sb[:], in_=bo.rearrange("(b p) -> p b", p=P))
+
+        nc.tensor.transpose(banks[7][:, 0:P], rows[:], ident[:])
+        cols = tile("cols", [P, 8], F32)
+        nc.scalar.copy(out=cols[:, 0:4], in_=banks[7][:, 0:4])
+        g = cols[:, 0:4]
+        mag = tile("mag", [P, 4], F32)
+        inv = tile("inv", [P, 4], F32)
+        root0 = tile("root0", [P, 4], F32)
+        sq = tile("sq", [P, 4], F32)
+        res = tile("res", [P, 4], F32)
+        root = tile("root", [P, 4], F32)
+        neg_root = tile("neg_root", [P, 4], F32)
+        sgn0 = tile("sgn0", [P, 4], F32)
+        sgn = tile("sgn", [P, 4], F32)
+        half_inv = tile("half_inv", [P, 4], F32)
+        nc.scalar.activation(out=mag[:], in_=g, func=ACT.Abs)
+        nc.scalar.activation(out=inv[:], in_=mag[:], func=ACT.Abs_reciprocal_sqrt, bias=2.0**-100)
+        for t in range(4):
+            nc.scalar.activation(out=root0[:, t : t + 1], in_=mag[:, t : t + 1], func=ACT.Copy, scale=inv[:, t : t + 1])
+        nc.scalar.activation(out=half_inv[:], in_=inv[:], func=ACT.Copy, scale=0.5)
+        nc.scalar.activation(out=sq[:], in_=root0[:], func=ACT.Square)
+        nc.scalar.activation(out=sgn0[:], in_=g, func=ACT.Sign)
+        for t in range(4):
+            nc.scalar.activation(
+                out=res[:, t : t + 1], in_=sq[:, t : t + 1], func=ACT.Identity, scale=-1.0, bias=mag[:, t : t + 1]
+            )
+        nc.scalar.activation(out=sgn[:], in_=sgn0[:], func=ACT.Sign, bias=0.5)
+        for t in range(4):
+            nc.scalar.activation(
+                out=root[:, t : t + 1],
+                in_=res[:, t : t + 1],
+                func=ACT.Identity,
+                scale=half_inv[:, t : t + 1],
+                bias=root0[:, t : t + 1],
+            )
+        nc.scalar.activation(out=neg_root[:], in_=root[:], func=ACT.Copy, scale=-1.0)
+
+        def offsets(kind, start, count):
+            return lists[kind][:, start // 16 : (start + count) // 16]
+
+        def gather_scales(kind, dst, start, count):
+            nc.vector.tensor_copy(out=dst, in_=tab_sc[:].indirect(offsets(kind, start, count)))
+
+        def gather_words(kind, a, dst, start, count):
+            nc.vector.tensor_copy(out=dst, in_=tab_w[a][:].bitcast(U32).indirect(offsets(kind, start, count)))
+
+        def cast_wt(a):
+            src = wt_raw[a][:].rearrange("p j (q t u i) -> p t q u j i", t=4, u=2, i=4)
+            for t in range(4):
+                dst = wt_bf[a][:, 512 * t : 512 * (t + 1)].rearrange("p (q u i j) -> p q u j i", u=2, i=4, j=4)
+                nc.scalar.copy(out=dst, in_=src[:, t])
+
+        def quantize_wt(a):
+            nc.vector.quantize_mx(out=wt_q[a][:].bitcast(FP8X4), scales=wt_sc[a][:], in_=wt_bf[a][:])
+
+        passes_done = {}
+
+        def multiply(kind, a, c, words):
+            base = 2 * (c % 3)
+            lo = c * CH
+            for t in range(4):
+                bank = banks[base + t // 2]
+                col = (t % 2) * CH
+                m = slice(128 * t, 128 * (t + 1))
+                if kind == PIECE:
+                    width = 128
+                    lhsT = wp_q[:, 256 * (4 * a + t) : 256 * (4 * a + t + 1)].bitcast(FP4X4)
+                    lhsT_sc = wp_sc[:, H * a + 128 * t : H * a + 128 * (t + 1)]
+                    plane = (piece_sc, piece_sc1)[a][:, lo : lo + CH]
+                elif kind == KING:
+                    width = CH
+                    lhsT = wk_q[:, H * a + 128 * t : H * a + 128 * (t + 1)].bitcast(FP8X4)
+                    lhsT_sc = wk_sc[4 * a : P, m]
+                    plane = half_sc[KING][4 * a : P, lo % 512 : lo % 512 + CH]
+                else:
+                    width = CH
+                    lhsT = wt_q[a][:, m].bitcast(FP8X4)
+                    lhsT_sc = wt_sc[a][:, m]
+                    plane = half_sc[THREAT][4 * a : P, lo % 512 : lo % 512 + CH]
+                for x in range(0, CH, width):
+                    done = passes_done.get((c, t // 2), 0)
+                    passes_done[(c, t // 2)] = done + width
+                    nc.tensor.matmul_mx(
+                        out=bank[:, col + x : col + x + width],
+                        lhsT=lhsT,
+                        lhsT_scale=lhsT_sc,
+                        rhs=words[:, x : x + width].bitcast(FP8X4),
+                        rhs_scale=plane[:, x : x + width],
+                        start=(done == 0),
+                        stop=(done + width == 6 * 512),
+                    )
+
+        def look_up(kind, a, c, words):
+            gather_words(kind, a, words, c * CH, CH)
+            multiply(kind, a, c, words)
+
+        w_t = [tile("w%d" % c, [P, 4, CH], F32) for c in range(4)]
+        v_t = [tile("v%d" % c, [P, 4 * CH], F32) for c in range(4)]
+        h_bf = [tile("h_bf%d" % c, [P, 4 * CH], BF16) for c in range(4)]
+        h_q = [tile("h_q%d" % c, [P, CH], U32) for c in range(4)]
+        h_sc = [tile("h_sc%d" % c, [P, CH], U8) for c in range(4)]
+        y_sb = [tile("y%d" % c, [P, 2, CH], F32) for c in range(3)]
+        y_last = [tile("y_last%d" % u, [P, 2, CH // 2], F32) for u in range(2)]
+        out_v = out.rearrange("(b p) s -> p b s", p=P)
+
+        def woven(c, lo, hi):
+            src = w_t[c][:, :, lo:hi].rearrange("p t (n i) -> p n t i", i=4)
+            dst = h_bf[c][:, 4 * lo : 4 * hi].rearrange("p (n i t) -> p n t i", i=4, t=4)
+            return dst, src
+
+        def leave_banks(c):
+            base = 2 * (c % 3)
+            for b in range(2):
+                v = v_t[c][:, 512 * b : 512 * (b + 1)]
+                nc.scalar.activation(out=v, in_=banks[base + b][:], func=ACT.Relu, scale=-1.0, bias=1.0)
+
+        def hidden(c):
+            for t in range(4):
+                nc.scalar.activation(
+                    out=w_t[c][:, t, :],
+                    in_=v_t[c][:, CH * t : CH * (t + 1)],
+                    func=ACT.Relu,
+                    scale=neg_root[:, t : t + 1],
+                    bias=root[:, t : t + 1],
+                )
+            dst, src = woven(c, 0, CH)
+            nc.scalar.activation(out=dst, in_=src, func=ACT.Square)
+
+        def evaluate(c):
+            bank = banks[6 + c % 2]
+            nc.vector.quantize_mx(out=h_q[c][:].bitcast(FP8X4), scales=h_sc[c][:], in_=h_bf[c][:])
+            for b in range(2):
+                nc.tensor.matmul_mx(
+                    out=bank[:, CH * b : CH * (b + 1)],
+                    lhsT=wo_q[:, 128 * b : 128 * (b + 1)].bitcast(FP8X4),
+                    lhsT_scale=wo_sc[:, 128 * b : 128 * (b + 1)],
+                    rhs=h_q[c][:].bitcast(FP8X4),
+                    rhs_scale=h_sc[c][:],
+                    start=True,
+                    stop=True,
+                )
+
+        def store(c):
+            bank = banks[6 + c % 2]
+            for b in range(2):
+                nc.scalar.activation(
+                    out=y_sb[c][:, b, :],
+                    in_=bank[:, CH * b : CH * (b + 1)],
+                    func=ACT.Identity,
+                    bias=bias_sb[:, b : b + 1],
+                )
+            nc.sync.dma_start(out=out_v[:, :, c * CH : (c + 1) * CH], in_=y_sb[c][:])
+
+        gather_scales(PIECE, piece_sc[:], 0, S)
+        for q in range(4):
+            nc.gpsimd.dma_start(
+                out=piece_sc1[32 * q : 32 * q + 4, :].bitcast(I32), in_=piece_sc[32 * q + 4 : 32 * q + 8, :].bitcast(I32)
+            )
+        gather_scales(THREAT, half_sc[THREAT][:], 0, 512)
+        gather_scales(KING, half_sc[KING][:], 0, 512)
+        cast_wt(0)
+        first_threat = tile("first_threat", [P, 2 * CH], U32)
+        gather_words(THREAT, 0, first_threat[:], 0, 512)
+        nc.vector.tensor_copy(
+            out=wk_sc[:].bitcast(I32).rearrange("p (t q e) -> p t q e", t=4, e=2),
+            in_=wk_sc_raw[:].bitcast(I32).rearrange("p (q t e) -> p t q e", t=4, e=2),
+        )
+        quantize_wt(0)
+        for c in range(2):
+            multiply(THREAT, 0, c, first_threat[:, CH * c : CH * (c + 1)])
+        nc.vector.tensor_copy(
+            out=wk_q[:].rearrange("p (a t q e) -> p a t q e", a=2, t=4, e=8),
+            in_=wk_raw[:].rearrange("p a (q t e) -> p a t q e", t=4, e=8),
+        )
+        first_king = tile("first_king", [P, 2 * CH], U32, tag="wk_raw")
+        gather_words(KING, 0, first_king[:], 0, 512)
+        for c in range(2):
+            multiply(KING, 0, c, first_king[:, CH * c : CH * (c + 1)])
+        nc.vector.tensor_copy(
+            out=wp_sc[:].bitcast(I32).rearrange("p (a t q e) -> p a t q e", a=2, t=4, e=2),
+            in_=wp_sc_raw[:].bitcast(I32).rearrange("p (a q t e) -> p a t q e", a=2, t=4, e=2),
+        )
+        nc.vector.tensor_copy(
+            out=wp_q[:].bitcast(I32).rearrange("p (a t q e) -> p a t q e", a=2, t=4, e=4),
+            in_=wp_raw[:].rearrange("p a (q t e) -> p a t q e", t=4, e=4),
+        )
+        first_piece = tile("first_piece", [P, 2 * CH], U32, tag="wp_raw")
+        gather_words(PIECE, 0, first_piece[:], 0, 512)
+        for c in range(2):
+            multiply(PIECE, 0, c, first_piece[:, CH * c : CH * (c + 1)])
+        cast_wt(1)
+        quantize_wt(1)
+        ring_a = tile("ring_a", [P, 2 * CH], U32)
+        ring_b = tile("ring_b", [P, 2 * CH], U32, tag="wt_bf1")
+        ring = [ring_a[:, 0:CH], ring_a[:, CH : 2 * CH], ring_b[:, 0:CH], ring_b[:, CH : 2 * CH]]
+        for i, (kind, c) in enumerate(((KING, 0), (PIECE, 0), (THREAT, 0), (KING, 1), (THREAT, 1), (PIECE, 1))):
+            look_up(kind, 1, c, ring[i % RING])
+        for j in range(4):
+            nc.scalar.activation(out=wo_sgn[:, j, :], in_=wo_raw[j][:], func=ACT.Copy, scale=sgn[:, j : j + 1])
+        nc.scalar.copy(
+            out=wo_bf[:].rearrange("p (n i j) -> p n j i", i=4, j=4),
+            in_=wo_sgn[:].rearrange("p j (n i) -> p n j i", i=4),
+        )
+        nc.vector.quantize_mx(out=wo_q[:].bitcast(FP8X4), scales=wo_sc[:], in_=wo_bf[:])
+        leave_banks(0)
+        hidden(0)
+        gather_scales(KING, half_sc[KING][:], 512, 512)
+        gather_scales(THREAT, half_sc[THREAT][:], 512, 512)
+        for a in range(PASSES):
+            look_up(PIECE, a, 2, ring[2 + a])
+        evaluate(0)
+        leave_banks(1)
+        hidden(1)
+        store(0)
+        later = ((THREAT, 0), (THREAT, 1), (KING, 0), (KING, 1))
+        words2 = tile("words2", [P, 4 * CH], U32, tag="h_bf0")
+        for i, (kind, a) in enumerate(later):
+            look_up(kind, a, 2, words2[:, CH * i : CH * (i + 1)])
+        for a in range(PASSES):
+            look_up(PIECE, a, 3, words2[:, CH * a : CH * (a + 1)])
+        evaluate(1)
+        leave_banks(2)
+        store(1)
+        hidden(2)
+        words3 = tile("words3", [P, 4 * CH], U32, tag="h_bf1")
+        for i, (kind, a) in enumerate(later):
+            look_up(kind, a, 3, words3[:, CH * i : CH * (i + 1)])
+        evaluate(2)
+
+        c = 3
+        nc.vector.tensor_scalar(
+            out=v_t[c][:, 0:512], in0=banks[0][:], scalar1=0.0, scalar2=1.0, op0=ALU.max, op1=ALU.min
+        )
+        for t in (2, 3):
+            nc.scalar.activation(
+                out=v_t[c][:, CH * t : CH * (t + 1)],
+                in_=banks[1][:, CH * (t - 2) : CH * (t - 1)],
+                func=ACT.Relu,
+                scale=root[:, t : t + 1],
+            )
+        for t in range(4):
+            nc.vector.tensor_scalar(
+                out=w_t[c][:, t, :],
+                in0=v_t[c][:, CH * t : CH * (t + 1)],
+                scalar1=root[:, t : t + 1],
+                scalar2=None,
+                op0=ALU.mult if t < 2 else ALU.min,
+            )
+        store(2)
+        half = CH // 2
+        dst, src = woven(c, 0, half)
+        nc.scalar.activation(out=dst, in_=src, func=ACT.Square)
+        dst, src = woven(c, half, CH)
+        nc.vector.tensor_tensor(out=dst, in0=src, in1=src, op=ALU.mult)
+        for u in range(2):
+            bank = banks[2 + u]
+            n = slice(half * u, half * (u + 1))
+            nc.vector.quantize_mx(
+                out=h_q[c][:, n].bitcast(FP8X4), scales=h_sc[c][:, n], in_=h_bf[c][:, 4 * half * u : 4 * half * (u + 1)]
+            )
+            for b in range(2):
+                nc.tensor.matmul_mx(
+                    out=bank[:, half * b : half * (b + 1)],
+                    lhsT=wo_q[:, 128 * b : 128 * (b + 1)].bitcast(FP8X4),
+                    lhsT_scale=wo_sc[:, 128 * b : 128 * (b + 1)],
+                    rhs=h_q[c][:, n].bitcast(FP8X4),
+                    rhs_scale=h_sc[c][:, n],
+                    start=True,
+                    stop=True,
+                )
+        for u in range(2):
+            bank = banks[2 + u]
+            for b in range(2):
+                src = bank[:, half * b : half * (b + 1)]
+                bias = bias_sb[:, b : b + 1]
+                if u == 0:
+                    nc.scalar.activation(out=y_last[u][:, b, :], in_=src, func=ACT.Identity, bias=bias)
+                else:
+                    nc.vector.tensor_scalar(
+                        out=y_last[u][:, b, :], in0=src, scalar1=bias, scalar2=None, op0=ALU.add
+                    )
+            nc.sync.dma_start(out=out_v[:, :, c * CH + half * u : c * CH + half * (u + 1)], in_=y_last[u][:])

@@ -20,7 +20,8 @@ ALU = mybir.AluOpType
 P = 128
 PASSES = 2
 CH = 256
-RING = 4
+HALF = CH // 2
+LAST = S // CH - 1
 PIECE, KING, THREAT = 0, 1, 2
 
 
@@ -30,26 +31,29 @@ def tile_list_chess_pattern_evaluation_kernel(
     nc = tc.nc
     with ExitStack() as ctx:
         sb = ctx.enter_context(tc.tile_pool(name="sb", bufs=1))
+        reused = ctx.enter_context(tc.tile_pool(name="reused", bufs=1))
         ps = ctx.enter_context(tc.psum_pool(name="ps", bufs=1))
 
         def tile(name, shape, dtype, tag=None):
             return sb.tile(shape, dtype, name=name, tag=tag or name, align_bytes=64)
+
+        def placed(name, shape, dtype, offset):
+            return reused.tile(shape, dtype, name=name, align_bytes=64, offset=offset)
 
         lists = [tile("list%d" % i, [P, S // 16], U16) for i in range(3)]
         tab_sc = tile("tab_sc", [P, T], U8)
         tab_w = [tile("tab_w%d" % a, [P, T], I32) for a in range(PASSES)]
         wk_sc_raw = tile("wk_sc_raw", [P, H], U8)
         wk_sc = tile("wk_sc", [P, H], U8)
-        wp_sc_raw = tile("wp_sc_raw", [P, 2 * H], U8)
-        wp_sc = tile("wp_sc", [P, 2 * H], U8)
+        wp_sc_raw = tile("wp_sc_raw", [P, PASSES * H], U8)
+        wp_sc = tile("wp_sc", [P, PASSES * H], U8)
         piece_sc = tile("piece_sc", [P, S], U8)
         piece_sc1 = tile("piece_sc1", [P, S], U8)
-        half_sc = {KING: tile("king_sc", [P, S // 2], U8), THREAT: tile("threat_sc", [P, S // 2], U8)}
         wt_raw = [tile("wt_raw%d" % a, [P, 4, H], F32) for a in range(PASSES)]
         wt_bf = [tile("wt_bf%d" % a, [P, 4 * H], BF16) for a in range(PASSES)]
         wt_q = [tile("wt_q%d" % a, [P, H], U32) for a in range(PASSES)]
         wt_sc = [tile("wt_sc%d" % a, [P, H], U8) for a in range(PASSES)]
-        wk_raw = tile("wk_raw", [P, PASSES, H], I32)
+        wk_raw = placed("wk_raw", [P, PASSES, H], I32, 0)
         wk_q = tile("wk_q", [P, PASSES * H], I32)
         wp_raw = tile("wp_raw", [P, PASSES, H // 2], I32)
         wp_q = tile("wp_q", [P, PASSES * 2 * H], U8)
@@ -58,24 +62,18 @@ def tile_list_chess_pattern_evaluation_kernel(
         wo_bf = tile("wo_bf", [P, 4 * N], BF16)
         wo_q = tile("wo_q", [P, N], U32)
         wo_sc = tile("wo_sc", [P, N], U8)
-        rows = tile("rows", [P, P], F32)
+        gain_rows = tile("gain_rows", [P, P], F32)
         ident = tile("ident", [P, P], F32)
+        bias_sb = tile("bias_sb", [P, 2], F32)
         banks = [ps.tile([P, 512], F32, name="bank%d" % b) for b in range(8)]
 
-        nc.vector.memset(tab_sc[:].bitcast(I32), 0)
-        nc.vector.memset(wk_sc_raw[:].bitcast(I32), 0)
-        nc.vector.memset(wp_sc_raw[:].bitcast(I32), 0)
-        nc.vector.memset(piece_sc1[:].bitcast(I32), 0)
-        nc.gpsimd.memset(rows[:], 0.0)
-
-        nc.sync.dma_start(lists[PIECE][:], offs)
-        for q in range(4):
-            nc.sync.dma_start(
-                out=tab_sc[32 * q : 32 * q + 8, :].bitcast(I32), in_=tab_scales[:, 4 * q : 4 * q + 4, :].bitcast(I32)
-            )
-        nc.sync.dma_start(lists[THREAT][:], offs3)
-        nc.sync.dma_start(lists[KING][:], offs2)
+        nc.vector.memset(tab_sc[:, 0 : T // 2].bitcast(I32), 0)
+        nc.gpsimd.memset(tab_sc[:, T // 2 : T].bitcast(I32), 0)
+        nc.gpsimd.memset(gain_rows[:], 0.0)
+        nc.gpsimd.memset(wk_sc_raw[:].bitcast(I32), 0)
+        nc.gpsimd.memset(wp_sc_raw[:].bitcast(I32), 0)
         make_identity(nc, ident[:])
+        nc.gpsimd.memset(piece_sc1[:].bitcast(I32), 0)
 
         def load_wt(a):
             nc.sync.dma_start(out=wt_raw[a][:], in_=wt[512 * a : 512 * (a + 1), :].rearrange("(p j) c -> p j c", j=4))
@@ -83,33 +81,38 @@ def tile_list_chess_pattern_evaluation_kernel(
         def load_tab(a):
             nc.sync.dma_start(out=tab_w[a][:], in_=tab_words[a].rearrange("p t i -> p (t i)").bitcast(I32))
 
-        load_wt(0)
-        load_tab(0)
-        nc.sync.dma_start(out=rows[0:4, :], in_=gain.rearrange("(q t e) -> t q e", t=4, e=8))
-        for q in range(4):
-            nc.sync.dma_start(
-                out=wk_sc_raw[32 * q : 32 * q + 8, :].bitcast(I32), in_=wk_scales[:, 4 * q : 4 * q + 4, :].bitcast(I32)
-            )
-        nc.sync.dma_start(out=wk_raw[:], in_=wk_words.rearrange("a p c i -> p a (c i)").bitcast(I32))
-        for q in range(4):
+        def load_packed_rows(dst, scales):
+            for q in range(4):
+                nc.sync.dma_start(
+                    out=dst[32 * q : 32 * q + 8, :].bitcast(I32), in_=scales[:, 4 * q : 4 * q + 4, :].bitcast(I32)
+                )
+
+        def load_wp_rows(q):
             nc.sync.dma_start(
                 out=wp_sc_raw[32 * q : 32 * q + 4, :].bitcast(I32).rearrange("r (a c) -> r a c", a=PASSES),
                 in_=wp_scales[:, 4 * q : 4 * q + 4, :].rearrange("a r c -> r a c").bitcast(I32),
             )
-        nc.sync.dma_start(out=wp_raw[:], in_=wp_words.rearrange("a p c -> p a c").bitcast(I32))
+
+        nc.sync.dma_start(lists[PIECE][:], offs)
+        nc.sync.dma_start(lists[KING][:], offs2)
+        nc.sync.dma_start(lists[THREAT][:], offs3)
+        load_packed_rows(tab_sc, tab_scales)
+        load_tab(0)
+        nc.sync.dma_start(out=gain_rows[0:4, :], in_=gain.rearrange("(q t e) -> t q e", t=4, e=8))
+        load_packed_rows(wk_sc_raw, wk_scales)
+        nc.sync.dma_start(out=wk_raw[:], in_=wk_words.rearrange("a p c i -> p a (c i)").bitcast(I32))
+        load_wt(0)
+        for q in range(4):
+            load_wp_rows(q)
         load_wt(1)
+        nc.sync.dma_start(out=wp_raw[:], in_=wp_words.rearrange("a p c -> p a c").bitcast(I32))
         load_tab(1)
         wo_rows = wo.rearrange("(q j e) n -> j q e n", j=4, e=8)
         for j in range(4):
             nc.sync.dma_start(out=wo_raw[j][:], in_=wo_rows[j])
-        bias_sb = tile("bias_sb", [P, 2], F32)
         with nc.allow_non_contiguous_dma(reason="one bias value a partition"):
             nc.sync.dma_start(out=bias_sb[:], in_=bo.rearrange("(b p) -> p b", p=P))
 
-        nc.tensor.transpose(banks[7][:, 0:P], rows[:], ident[:])
-        cols = tile("cols", [P, 8], F32)
-        nc.scalar.copy(out=cols[:, 0:4], in_=banks[7][:, 0:4])
-        g = cols[:, 0:4]
         mag = tile("mag", [P, 4], F32)
         inv = tile("inv", [P, 4], F32)
         root0 = tile("root0", [P, 4], F32)
@@ -120,18 +123,19 @@ def tile_list_chess_pattern_evaluation_kernel(
         sgn0 = tile("sgn0", [P, 4], F32)
         sgn = tile("sgn", [P, 4], F32)
         half_inv = tile("half_inv", [P, 4], F32)
-        nc.scalar.activation(out=mag[:], in_=g, func=ACT.Abs)
+        nc.tensor.transpose(banks[7][:, 0:P], gain_rows[:], ident[:])
+        nc.scalar.activation(out=mag[:], in_=banks[7][:, 0:4], func=ACT.Abs)
+        nc.scalar.activation(out=sgn0[:], in_=banks[7][:, 0:4], func=ACT.Sign)
         nc.scalar.activation(out=inv[:], in_=mag[:], func=ACT.Abs_reciprocal_sqrt, bias=2.0**-100)
         for t in range(4):
             nc.scalar.activation(out=root0[:, t : t + 1], in_=mag[:, t : t + 1], func=ACT.Copy, scale=inv[:, t : t + 1])
         nc.scalar.activation(out=half_inv[:], in_=inv[:], func=ACT.Copy, scale=0.5)
         nc.scalar.activation(out=sq[:], in_=root0[:], func=ACT.Square)
-        nc.scalar.activation(out=sgn0[:], in_=g, func=ACT.Sign)
+        nc.scalar.activation(out=sgn[:], in_=sgn0[:], func=ACT.Sign, bias=0.5)
         for t in range(4):
             nc.scalar.activation(
                 out=res[:, t : t + 1], in_=sq[:, t : t + 1], func=ACT.Identity, scale=-1.0, bias=mag[:, t : t + 1]
             )
-        nc.scalar.activation(out=sgn[:], in_=sgn0[:], func=ACT.Sign, bias=0.5)
         for t in range(4):
             nc.scalar.activation(
                 out=root[:, t : t + 1],
@@ -160,99 +164,116 @@ def tile_list_chess_pattern_evaluation_kernel(
         def quantize_wt(a):
             nc.vector.quantize_mx(out=wt_q[a][:].bitcast(FP8X4), scales=wt_sc[a][:], in_=wt_bf[a][:])
 
-        passes_done = {}
+        planes = {}
+        columns_done = {}
 
         def multiply(kind, a, c, words):
-            base = 2 * (c % 3)
             lo = c * CH
-            for t in range(4):
-                bank = banks[base + t // 2]
-                col = (t % 2) * CH
+            if kind == PIECE:
+                plane = (piece_sc, piece_sc1)[a][:, lo : lo + CH]
+            else:
+                plane = planes[(kind, c)][4 * a : P, :]
+            width = HALF if kind == PIECE or c == LAST else CH
+            if c == LAST:
+                steps = [(t, x, 2 * c + x // HALF, t * HALF) for x in (0, HALF) for t in range(4)]
+            else:
+                steps = [(t, x, 2 * c + t // 2, (t % 2) * CH + x) for t in range(4) for x in range(0, CH, width)]
+            for t, x, b, col in steps:
                 m = slice(128 * t, 128 * (t + 1))
+                am = slice(H * a + 128 * t, H * a + 128 * (t + 1))
                 if kind == PIECE:
-                    width = 128
                     lhsT = wp_q[:, 256 * (4 * a + t) : 256 * (4 * a + t + 1)].bitcast(FP4X4)
-                    lhsT_sc = wp_sc[:, H * a + 128 * t : H * a + 128 * (t + 1)]
-                    plane = (piece_sc, piece_sc1)[a][:, lo : lo + CH]
+                    lhsT_sc = wp_sc[:, am]
                 elif kind == KING:
-                    width = CH
-                    lhsT = wk_q[:, H * a + 128 * t : H * a + 128 * (t + 1)].bitcast(FP8X4)
+                    lhsT = wk_q[:, am].bitcast(FP8X4)
                     lhsT_sc = wk_sc[4 * a : P, m]
-                    plane = half_sc[KING][4 * a : P, lo % 512 : lo % 512 + CH]
                 else:
-                    width = CH
                     lhsT = wt_q[a][:, m].bitcast(FP8X4)
                     lhsT_sc = wt_sc[a][:, m]
-                    plane = half_sc[THREAT][4 * a : P, lo % 512 : lo % 512 + CH]
-                for x in range(0, CH, width):
-                    done = passes_done.get((c, t // 2), 0)
-                    passes_done[(c, t // 2)] = done + width
-                    nc.tensor.matmul_mx(
-                        out=bank[:, col + x : col + x + width],
-                        lhsT=lhsT,
-                        lhsT_scale=lhsT_sc,
-                        rhs=words[:, x : x + width].bitcast(FP8X4),
-                        rhs_scale=plane[:, x : x + width],
-                        start=(done == 0),
-                        stop=(done + width == 6 * 512),
-                    )
+                done = columns_done.get(b, 0)
+                columns_done[b] = done + width
+                nc.tensor.matmul_mx(
+                    out=banks[b][:, col : col + width],
+                    lhsT=lhsT,
+                    lhsT_scale=lhsT_sc,
+                    rhs=words[:, x : x + width].bitcast(FP8X4),
+                    rhs_scale=plane[:, x : x + width],
+                    start=(done == 0),
+                    stop=(done + width == 6 * 512),
+                )
 
         def look_up(kind, a, c, words):
             gather_words(kind, a, words, c * CH, CH)
             multiply(kind, a, c, words)
 
-        w_t = [tile("w%d" % c, [P, 4, CH], F32) for c in range(4)]
-        v_t = [tile("v%d" % c, [P, 4 * CH], F32) for c in range(4)]
-        h_bf = [tile("h_bf%d" % c, [P, 4 * CH], BF16) for c in range(4)]
-        h_q = [tile("h_q%d" % c, [P, CH], U32) for c in range(4)]
-        h_sc = [tile("h_sc%d" % c, [P, CH], U8) for c in range(4)]
-        y_sb = [tile("y%d" % c, [P, 2, CH], F32) for c in range(3)]
-        y_last = [tile("y_last%d" % u, [P, 2, CH // 2], F32) for u in range(2)]
+        def look_up_two(kind, words):
+            gather_words(kind, 0, words[:], 0, 2 * CH)
+            for c in range(2):
+                multiply(kind, 0, c, words[:, CH * c : CH * (c + 1)])
+
+        def look_up_group(name, tag, c, steps):
+            words = tile(name, [P, len(steps) * CH], U32, tag=tag)
+            for i, (kind, a) in enumerate(steps):
+                look_up(kind, a, c, words[:, CH * i : CH * (i + 1)])
+
+        def chunk_planes(c, tag):
+            both = tile("planes%d" % c, [P, 2 * CH], U8, tag=tag)
+            for i, kind in enumerate((KING, THREAT)):
+                plane = both[:, CH * i : CH * (i + 1)]
+                gather_scales(kind, plane, c * CH, CH)
+                planes[(kind, c)] = plane
+
+        h_bf = [tile("h_bf%d" % c, [P, 4 * CH], BF16) for c in range(LAST)]
+        h_sc = [tile("h_sc%d" % c, [P, CH], U8) for c in range(LAST)]
+        y_sb = [tile("y%d" % c, [P, 2, CH], F32) for c in range(LAST)]
         out_v = out.rearrange("(b p) s -> p b s", p=P)
 
-        def woven(c, lo, hi):
-            src = w_t[c][:, :, lo:hi].rearrange("p t (n i) -> p n t i", i=4)
-            dst = h_bf[c][:, 4 * lo : 4 * hi].rearrange("p (n i t) -> p n t i", i=4, t=4)
-            return dst, src
-
-        def leave_banks(c):
-            base = 2 * (c % 3)
-            for b in range(2):
-                v = v_t[c][:, 512 * b : 512 * (b + 1)]
-                nc.scalar.activation(out=v, in_=banks[base + b][:], func=ACT.Relu, scale=-1.0, bias=1.0)
-
-        def hidden(c):
+        def hidden(c, width, src_banks, dst):
+            v = tile("v%d" % c, [P, 4 * width], F32, tag="swap%d" % (c % 2))
+            w = tile("w%d" % c, [P, 4, width], F32, tag="swap%d" % ((c + 1) % 2))
+            for b, bank in enumerate(src_banks):
+                nc.scalar.activation(
+                    out=v[:, 512 * b : 512 * (b + 1)], in_=bank[:], func=ACT.Relu, scale=-1.0, bias=1.0
+                )
             for t in range(4):
                 nc.scalar.activation(
-                    out=w_t[c][:, t, :],
-                    in_=v_t[c][:, CH * t : CH * (t + 1)],
+                    out=w[:, t, :],
+                    in_=v[:, width * t : width * (t + 1)],
                     func=ACT.Relu,
                     scale=neg_root[:, t : t + 1],
                     bias=root[:, t : t + 1],
                 )
-            dst, src = woven(c, 0, CH)
-            nc.scalar.activation(out=dst, in_=src, func=ACT.Square)
+            nc.scalar.activation(
+                out=dst.rearrange("p (n i t) -> p n t i", i=4, t=4),
+                in_=w[:].rearrange("p t (n i) -> p n t i", i=4),
+                func=ACT.Square,
+            )
 
-        def evaluate(c):
-            bank = banks[6 + c % 2]
-            nc.vector.quantize_mx(out=h_q[c][:].bitcast(FP8X4), scales=h_sc[c][:], in_=h_bf[c][:])
+        def evaluate(src, codes, scales, bank, width):
+            nc.vector.quantize_mx(out=codes.bitcast(FP8X4), scales=scales, in_=src)
             for b in range(2):
                 nc.tensor.matmul_mx(
-                    out=bank[:, CH * b : CH * (b + 1)],
+                    out=bank[:, width * b : width * (b + 1)],
                     lhsT=wo_q[:, 128 * b : 128 * (b + 1)].bitcast(FP8X4),
                     lhsT_scale=wo_sc[:, 128 * b : 128 * (b + 1)],
-                    rhs=h_q[c][:].bitcast(FP8X4),
-                    rhs_scale=h_sc[c][:],
+                    rhs=codes.bitcast(FP8X4),
+                    rhs_scale=scales,
                     start=True,
                     stop=True,
                 )
 
-        def store(c):
-            bank = banks[6 + c % 2]
+        def hidden_chunk(c):
+            hidden(c, CH, banks[2 * c : 2 * c + 2], h_bf[c][:])
+
+        def evaluate_chunk(c, tag=None):
+            h_q = tile("h_q%d" % c, [P, CH], U32, tag=tag)
+            evaluate(h_bf[c][:], h_q[:], h_sc[c][:], banks[2 * c], CH)
+
+        def store_chunk(c):
             for b in range(2):
                 nc.scalar.activation(
                     out=y_sb[c][:, b, :],
-                    in_=bank[:, CH * b : CH * (b + 1)],
+                    in_=banks[2 * c][:, CH * b : CH * (b + 1)],
                     func=ACT.Identity,
                     bias=bias_sb[:, b : b + 1],
                 )
@@ -263,26 +284,32 @@ def tile_list_chess_pattern_evaluation_kernel(
             nc.gpsimd.dma_start(
                 out=piece_sc1[32 * q : 32 * q + 4, :].bitcast(I32), in_=piece_sc[32 * q + 4 : 32 * q + 8, :].bitcast(I32)
             )
-        gather_scales(THREAT, half_sc[THREAT][:], 0, 512)
-        gather_scales(KING, half_sc[KING][:], 0, 512)
-        cast_wt(0)
-        first_threat = tile("first_threat", [P, 2 * CH], U32)
-        gather_words(THREAT, 0, first_threat[:], 0, 512)
+
+        def first_planes(kind, plane):
+            gather_scales(kind, plane[:], 0, 2 * CH)
+            for c in range(2):
+                planes[(kind, c)] = plane[:, CH * c : CH * (c + 1)]
+
+        first_planes(KING, tile("king_first", [P, 2 * CH], U8))
+        first_king = tile("first_king", [P, 2 * CH], U32)
+        gather_words(KING, 0, first_king[:], 0, 2 * CH)
         nc.vector.tensor_copy(
             out=wk_sc[:].bitcast(I32).rearrange("p (t q e) -> p t q e", t=4, e=2),
             in_=wk_sc_raw[:].bitcast(I32).rearrange("p (q t e) -> p t q e", t=4, e=2),
         )
-        quantize_wt(0)
-        for c in range(2):
-            multiply(THREAT, 0, c, first_threat[:, CH * c : CH * (c + 1)])
         nc.vector.tensor_copy(
             out=wk_q[:].rearrange("p (a t q e) -> p a t q e", a=2, t=4, e=8),
             in_=wk_raw[:].rearrange("p a (q t e) -> p a t q e", t=4, e=8),
         )
-        first_king = tile("first_king", [P, 2 * CH], U32, tag="wk_raw")
-        gather_words(KING, 0, first_king[:], 0, 512)
         for c in range(2):
             multiply(KING, 0, c, first_king[:, CH * c : CH * (c + 1)])
+        cast_wt(0)
+        first_planes(THREAT, placed("threat_first", [P, 2 * CH], U8, 8 * CH))
+        first_threat = placed("first_threat", [P, 2 * CH], U32, 0)
+        gather_words(THREAT, 0, first_threat[:], 0, 2 * CH)
+        quantize_wt(0)
+        for c in range(2):
+            multiply(THREAT, 0, c, first_threat[:, CH * c : CH * (c + 1)])
         nc.vector.tensor_copy(
             out=wp_sc[:].bitcast(I32).rearrange("p (a t q e) -> p a t q e", a=2, t=4, e=2),
             in_=wp_sc_raw[:].bitcast(I32).rearrange("p (a q t e) -> p a t q e", a=2, t=4, e=2),
@@ -291,17 +318,14 @@ def tile_list_chess_pattern_evaluation_kernel(
             out=wp_q[:].bitcast(I32).rearrange("p (a t q e) -> p a t q e", a=2, t=4, e=4),
             in_=wp_raw[:].rearrange("p a (q t e) -> p a t q e", t=4, e=4),
         )
-        first_piece = tile("first_piece", [P, 2 * CH], U32, tag="wp_raw")
-        gather_words(PIECE, 0, first_piece[:], 0, 512)
-        for c in range(2):
-            multiply(PIECE, 0, c, first_piece[:, CH * c : CH * (c + 1)])
+        look_up_two(PIECE, tile("first_piece", [P, 2 * CH], U32, tag="wp_raw"))
         cast_wt(1)
         quantize_wt(1)
-        ring_a = tile("ring_a", [P, 2 * CH], U32)
-        ring_b = tile("ring_b", [P, 2 * CH], U32, tag="wt_bf1")
-        ring = [ring_a[:, 0:CH], ring_a[:, CH : 2 * CH], ring_b[:, 0:CH], ring_b[:, CH : 2 * CH]]
-        for i, (kind, c) in enumerate(((KING, 0), (PIECE, 0), (THREAT, 0), (KING, 1), (THREAT, 1), (PIECE, 1))):
-            look_up(kind, 1, c, ring[i % RING])
+        second = ((KING, 1), (THREAT, 1), (PIECE, 1))
+        second_words = tile("second_words", [P, 6 * CH], U32, tag="wt_bf1")
+        for c in range(2):
+            for i, (kind, a) in enumerate(second):
+                look_up(kind, a, c, second_words[:, CH * (3 * c + i) : CH * (3 * c + i + 1)])
         for j in range(4):
             nc.scalar.activation(out=wo_sgn[:, j, :], in_=wo_raw[j][:], func=ACT.Copy, scale=sgn[:, j : j + 1])
         nc.scalar.copy(
@@ -309,81 +333,51 @@ def tile_list_chess_pattern_evaluation_kernel(
             in_=wo_sgn[:].rearrange("p j (n i) -> p n j i", i=4),
         )
         nc.vector.quantize_mx(out=wo_q[:].bitcast(FP8X4), scales=wo_sc[:], in_=wo_bf[:])
-        leave_banks(0)
-        hidden(0)
-        gather_scales(KING, half_sc[KING][:], 512, 512)
-        gather_scales(THREAT, half_sc[THREAT][:], 512, 512)
-        for a in range(PASSES):
-            look_up(PIECE, a, 2, ring[2 + a])
-        evaluate(0)
-        leave_banks(1)
-        hidden(1)
-        store(0)
-        later = ((THREAT, 0), (THREAT, 1), (KING, 0), (KING, 1))
-        words2 = tile("words2", [P, 4 * CH], U32, tag="h_bf0")
-        for i, (kind, a) in enumerate(later):
-            look_up(kind, a, 2, words2[:, CH * i : CH * (i + 1)])
-        for a in range(PASSES):
-            look_up(PIECE, a, 3, words2[:, CH * a : CH * (a + 1)])
-        evaluate(1)
-        leave_banks(2)
-        store(1)
-        hidden(2)
-        words3 = tile("words3", [P, 4 * CH], U32, tag="h_bf1")
-        for i, (kind, a) in enumerate(later):
-            look_up(kind, a, 3, words3[:, CH * i : CH * (i + 1)])
-        evaluate(2)
+        hidden_chunk(0)
 
-        c = 3
-        nc.vector.tensor_scalar(
-            out=v_t[c][:, 0:512], in0=banks[0][:], scalar1=0.0, scalar2=1.0, op0=ALU.max, op1=ALU.min
+        chunk_planes(2, "king_first")
+        look_up_group("words2a", "wo_bf", 2, ((KING, 0),))
+        look_up_group("words2b", "wo_sgn", 2, ((THREAT, 0),))
+        evaluate_chunk(0, "wo_bf")
+        hidden_chunk(1)
+        store_chunk(0)
+        look_up_group("words2c", "h_bf0", 2, ((PIECE, 0), (PIECE, 1), (THREAT, 1), (KING, 1)))
+
+        chunk_planes(3, "h_sc0")
+        evaluate_chunk(1)
+        hidden_chunk(2)
+        store_chunk(1)
+        look_up_group(
+            "words3", "h_bf1", 3, ((PIECE, 0), (PIECE, 1), (THREAT, 0), (KING, 0), (THREAT, 1), (KING, 1))
         )
-        for t in (2, 3):
-            nc.scalar.activation(
-                out=v_t[c][:, CH * t : CH * (t + 1)],
-                in_=banks[1][:, CH * (t - 2) : CH * (t - 1)],
-                func=ACT.Relu,
-                scale=root[:, t : t + 1],
-            )
-        for t in range(4):
-            nc.vector.tensor_scalar(
-                out=w_t[c][:, t, :],
-                in0=v_t[c][:, CH * t : CH * (t + 1)],
-                scalar1=root[:, t : t + 1],
-                scalar2=None,
-                op0=ALU.mult if t < 2 else ALU.min,
-            )
-        store(2)
-        half = CH // 2
-        dst, src = woven(c, 0, half)
-        nc.scalar.activation(out=dst, in_=src, func=ACT.Square)
-        dst, src = woven(c, half, CH)
-        nc.vector.tensor_tensor(out=dst, in0=src, in1=src, op=ALU.mult)
-        for u in range(2):
-            bank = banks[2 + u]
-            n = slice(half * u, half * (u + 1))
-            nc.vector.quantize_mx(
-                out=h_q[c][:, n].bitcast(FP8X4), scales=h_sc[c][:, n], in_=h_bf[c][:, 4 * half * u : 4 * half * (u + 1)]
-            )
+        evaluate_chunk(2)
+
+        last_bf = [tile("last_bf%d" % u, [P, 4 * HALF], BF16) for u in range(2)]
+        last_q = [tile("last_q%d" % u, [P, HALF], U32) for u in range(2)]
+        last_sc = [tile("last_sc%d" % u, [P, HALF], U8) for u in range(2)]
+        last_y = [tile("last_y%d" % u, [P, 2, HALF], F32) for u in range(2)]
+        hidden(LAST, HALF, banks[2 * LAST : 2 * LAST + 1], last_bf[0][:])
+        capped = tile("capped", [P, HALF, 4], F32)
+        nc.vector.scalar_tensor_tensor(
+            out=capped[:],
+            in0=banks[2 * LAST + 1][:].rearrange("p (t n) -> p n t", t=4),
+            scalar=1.0,
+            in1=root[:].unsqueeze(1).to_broadcast([P, HALF, 4]),
+            op0=ALU.min,
+            op1=ALU.mult,
+        )
+        flat = capped[:].rearrange("p n t -> p (n t)")
+        nc.vector.scalar_tensor_tensor(out=last_bf[1][:], in0=flat, scalar=0.0, in1=flat, op0=ALU.max, op1=ALU.mult)
+        store_chunk(2)
+        for u in (1, 0):
+            evaluate(last_bf[u][:], last_q[u][:], last_sc[u][:], banks[1 + 2 * u], HALF)
+        for u in (1, 0):
             for b in range(2):
-                nc.tensor.matmul_mx(
-                    out=bank[:, half * b : half * (b + 1)],
-                    lhsT=wo_q[:, 128 * b : 128 * (b + 1)].bitcast(FP8X4),
-                    lhsT_scale=wo_sc[:, 128 * b : 128 * (b + 1)],
-                    rhs=h_q[c][:, n].bitcast(FP8X4),
-                    rhs_scale=h_sc[c][:, n],
-                    start=True,
-                    stop=True,
-                )
-        for u in range(2):
-            bank = banks[2 + u]
-            for b in range(2):
-                src = bank[:, half * b : half * (b + 1)]
+                src = banks[1 + 2 * u][:, HALF * b : HALF * (b + 1)]
                 bias = bias_sb[:, b : b + 1]
                 if u == 0:
-                    nc.scalar.activation(out=y_last[u][:, b, :], in_=src, func=ACT.Identity, bias=bias)
+                    nc.scalar.activation(out=last_y[u][:, b, :], in_=src, func=ACT.Identity, bias=bias)
                 else:
-                    nc.vector.tensor_scalar(
-                        out=y_last[u][:, b, :], in0=src, scalar1=bias, scalar2=None, op0=ALU.add
-                    )
-            nc.sync.dma_start(out=out_v[:, :, c * CH + half * u : c * CH + half * (u + 1)], in_=y_last[u][:])
+                    nc.vector.tensor_scalar(out=last_y[u][:, b, :], in0=src, scalar1=bias, scalar2=None, op0=ALU.add)
+            lo = LAST * CH + HALF * u
+            nc.sync.dma_start(out=out_v[:, :, lo : lo + HALF], in_=last_y[u][:])

@@ -173,11 +173,8 @@ def tile_list_chess_pattern_evaluation_kernel(
                 plane = (piece_sc, piece_sc1)[a][:, lo : lo + CH]
             else:
                 plane = planes[(kind, c)][4 * a : P, :]
-            width = HALF if kind == PIECE or c == LAST else CH
-            if c == LAST:
-                steps = [(t, x, 2 * c + x // HALF, t * HALF) for x in (0, HALF) for t in range(4)]
-            else:
-                steps = [(t, x, 2 * c + t // 2, (t % 2) * CH + x) for t in range(4) for x in range(0, CH, width)]
+            width = HALF if kind == PIECE else CH
+            steps = [(t, x, 2 * c + t // 2, (t % 2) * CH + x) for t in range(4) for x in range(0, CH, width)]
             for t, x, b, col in steps:
                 m = slice(128 * t, 128 * (t + 1))
                 am = slice(H * a + 128 * t, H * a + 128 * (t + 1))
@@ -211,19 +208,19 @@ def tile_list_chess_pattern_evaluation_kernel(
             for c in range(2):
                 multiply(kind, 0, c, words[:, CH * c : CH * (c + 1)])
 
-        def look_up_group(name, tag, c, steps):
-            words = tile(name, [P, len(steps) * CH], U32, tag=tag)
+        def look_up_group(name, tag, c, steps, offset=None):
+            shape = [P, len(steps) * CH]
+            words = tile(name, shape, U32, tag=tag) if offset is None else placed(name, shape, U32, offset)
             for i, (kind, a) in enumerate(steps):
                 look_up(kind, a, c, words[:, CH * i : CH * (i + 1)])
 
-        def chunk_planes(c, tag):
-            both = tile("planes%d" % c, [P, 2 * CH], U8, tag=tag)
-            for i, kind in enumerate((KING, THREAT)):
-                plane = both[:, CH * i : CH * (i + 1)]
-                gather_scales(kind, plane, c * CH, CH)
-                planes[(kind, c)] = plane
+        def chunk_plane(kind, c, tag, offset=None):
+            name = "plane%d_%d" % (kind, c)
+            plane = tile(name, [P, CH], U8, tag=tag) if offset is None else placed(name, [P, CH], U8, offset)
+            gather_scales(kind, plane[:], c * CH, CH)
+            planes[(kind, c)] = plane[:]
 
-        h_bf = [tile("h_bf%d" % c, [P, 4 * CH], BF16) for c in range(LAST)]
+        h_bf = [placed("h_bf%d" % c, [P, 4 * CH], BF16, 8192 * (c + 1)) for c in range(LAST)]
         h_sc = [tile("h_sc%d" % c, [P, CH], U8) for c in range(LAST)]
         y_sb = [tile("y%d" % c, [P, 2, CH], F32) for c in range(LAST)]
         out_v = out.rearrange("(b p) s -> p b s", p=P)
@@ -335,43 +332,67 @@ def tile_list_chess_pattern_evaluation_kernel(
         nc.vector.quantize_mx(out=wo_q[:].bitcast(FP8X4), scales=wo_sc[:], in_=wo_bf[:])
         hidden_chunk(0)
 
-        chunk_planes(2, "king_first")
-        look_up_group("words2a", "wo_bf", 2, ((KING, 0),))
-        look_up_group("words2b", "wo_sgn", 2, ((THREAT, 0),))
+        look_up_group("words2a", "wo_bf", 2, ((PIECE, 0),))
+        look_up_group("words2b", "wo_sgn", 2, ((PIECE, 1),))
+        chunk_plane(THREAT, 2, "king_first")
+        look_up_group("words2c", "wt_bf1", 2, ((THREAT, 0),))
         evaluate_chunk(0, "wo_bf")
         hidden_chunk(1)
         store_chunk(0)
-        look_up_group("words2c", "h_bf0", 2, ((PIECE, 0), (PIECE, 1), (THREAT, 1), (KING, 1)))
+        look_up_group("words2d", None, 2, ((THREAT, 1),), 8192 - 896)
+        chunk_plane(KING, 2, None, 8192 + 128)
+        look_up_group("words2e", None, 2, ((KING, 0),), 8192 + 384)
+        look_up_group("words2f", None, 2, ((KING, 1),), 8192 + 1408)
 
-        chunk_planes(3, "h_sc0")
+        look_up_group("words3a", "wo_bf", 3, ((PIECE, 0),))
+        look_up_group("words3b", "h_sc0", 3, ((PIECE, 1),))
         evaluate_chunk(1)
         hidden_chunk(2)
         store_chunk(1)
-        look_up_group(
-            "words3", "h_bf1", 3, ((PIECE, 0), (PIECE, 1), (THREAT, 0), (KING, 0), (THREAT, 1), (KING, 1))
-        )
+        chunk_plane(THREAT, 3, None, 16384 + 128)
+        look_up_group("words3c", None, 3, ((THREAT, 0), (THREAT, 1)), 16384 - 1920)
+        chunk_plane(KING, 3, None, 16384 + 384)
+        look_up_group("words3d", None, 3, ((KING, 0), (KING, 1)), 16384 + 640)
         evaluate_chunk(2)
 
+        first_bank, second_bank = banks[2 * LAST], banks[2 * LAST + 1]
+        v = tile("v_last", [P, 4 * CH], F32, tag="swap1")
+        w = tile("w_last", [P, 4, CH], F32)
         last_bf = [tile("last_bf%d" % u, [P, 4 * HALF], BF16) for u in range(2)]
         last_q = [tile("last_q%d" % u, [P, HALF], U32) for u in range(2)]
         last_sc = [tile("last_sc%d" % u, [P, HALF], U8) for u in range(2)]
         last_y = [tile("last_y%d" % u, [P, 2, HALF], F32) for u in range(2)]
-        hidden(LAST, HALF, banks[2 * LAST : 2 * LAST + 1], last_bf[0][:])
-        capped = tile("capped", [P, HALF, 4], F32)
-        nc.vector.scalar_tensor_tensor(
-            out=capped[:],
-            in0=banks[2 * LAST + 1][:].rearrange("p (t n) -> p n t", t=4),
-            scalar=1.0,
-            in1=root[:].unsqueeze(1).to_broadcast([P, HALF, 4]),
-            op0=ALU.min,
-            op1=ALU.mult,
+        nc.vector.tensor_scalar(
+            out=v[:, 0:512], in0=first_bank[:], scalar1=0.0, scalar2=1.0, op0=ALU.max, op1=ALU.min
         )
-        flat = capped[:].rearrange("p n t -> p (n t)")
-        nc.vector.scalar_tensor_tensor(out=last_bf[1][:], in0=flat, scalar=0.0, in1=flat, op0=ALU.max, op1=ALU.mult)
+        for t in (2, 3):
+            nc.scalar.activation(
+                out=v[:, CH * t : CH * (t + 1)],
+                in_=second_bank[:, CH * (t - 2) : CH * (t - 1)],
+                func=ACT.Relu,
+                scale=root[:, t : t + 1],
+            )
+        for t in range(4):
+            nc.vector.tensor_scalar(
+                out=w[:, t, :],
+                in0=v[:, CH * t : CH * (t + 1)],
+                scalar1=root[:, t : t + 1],
+                scalar2=None,
+                op0=ALU.mult if t < 2 else ALU.min,
+            )
         store_chunk(2)
-        for u in (1, 0):
+        woven = [
+            (
+                last_bf[u][:].rearrange("p (n i t) -> p n t i", i=4, t=4),
+                w[:, :, HALF * u : HALF * (u + 1)].rearrange("p t (n i) -> p n t i", i=4),
+            )
+            for u in range(2)
+        ]
+        nc.scalar.activation(out=woven[0][0], in_=woven[0][1], func=ACT.Square)
+        nc.vector.tensor_tensor(out=woven[1][0], in0=woven[1][1], in1=woven[1][1], op=ALU.mult)
+        for u in range(2):
             evaluate(last_bf[u][:], last_q[u][:], last_sc[u][:], banks[1 + 2 * u], HALF)
-        for u in (1, 0):
+        for u in range(2):
             for b in range(2):
                 src = banks[1 + 2 * u][:, HALF * b : HALF * (b + 1)]
                 bias = bias_sb[:, b : b + 1]

@@ -50,7 +50,7 @@ def tile_list_chess_pattern_evaluation_kernel(
         piece_sc = tile("piece_sc", [P, S], U8)
         piece_sc1 = tile("piece_sc1", [P, S], U8)
         wt_raw = [tile("wt_raw%d" % a, [P, 4, H], F32) for a in range(PASSES)]
-        wt_bf = [tile("wt_bf%d" % a, [P, 4 * H], BF16) for a in range(PASSES)]
+        wt_bf = [tile("wt_bf0", [P, 4 * H], BF16), placed("wt_bf1", [P, 4 * H], BF16, 69632)]
         wt_q = [tile("wt_q%d" % a, [P, H], U32) for a in range(PASSES)]
         wt_sc = [tile("wt_sc%d" % a, [P, H], U8) for a in range(PASSES)]
         wk_raw = placed("wk_raw", [P, PASSES, H], I32, 0)
@@ -59,21 +59,20 @@ def tile_list_chess_pattern_evaluation_kernel(
         wp_q = tile("wp_q", [P, PASSES * 2 * H], U8)
         wo_raw = [tile("wo_raw%d" % j, [P, N], F32) for j in range(4)]
         wo_sgn = tile("wo_sgn", [P, 4, N], BF16)
-        wo_bf = tile("wo_bf", [P, 4 * N], BF16)
-        wo_q = tile("wo_q", [P, N], U32)
+        wo_bf = placed("wo_bf", [P, 4 * N], BF16, 61440)
+        wo_q = placed("wo_q", [P, N], U32, 69632)
         wo_sc = tile("wo_sc", [P, N], U8)
         gain_rows = tile("gain_rows", [P, P], F32)
         ident = tile("ident", [P, P], F32)
         bias_sb = tile("bias_sb", [P, 2], F32)
         banks = [ps.tile([P, 512], F32, name="bank%d" % b) for b in range(8)]
 
-        nc.vector.memset(tab_sc[:, 0 : T // 2].bitcast(I32), 0)
-        nc.gpsimd.memset(tab_sc[:, T // 2 : T].bitcast(I32), 0)
+        nc.vector.memset(tab_sc[:].bitcast(I32), 0)
+        nc.vector.memset(wk_sc_raw[:].bitcast(I32), 0)
+        nc.vector.memset(wp_sc_raw[:].bitcast(I32), 0)
+        nc.vector.memset(piece_sc1[:].bitcast(I32), 0)
         nc.gpsimd.memset(gain_rows[:], 0.0)
-        nc.gpsimd.memset(wk_sc_raw[:].bitcast(I32), 0)
-        nc.gpsimd.memset(wp_sc_raw[:].bitcast(I32), 0)
         make_identity(nc, ident[:])
-        nc.gpsimd.memset(piece_sc1[:].bitcast(I32), 0)
 
         def load_wt(a):
             nc.sync.dma_start(out=wt_raw[a][:], in_=wt[512 * a : 512 * (a + 1), :].rearrange("(p j) c -> p j c", j=4))
@@ -97,19 +96,19 @@ def tile_list_chess_pattern_evaluation_kernel(
         nc.sync.dma_start(lists[KING][:], offs2)
         nc.sync.dma_start(lists[THREAT][:], offs3)
         load_packed_rows(tab_sc, tab_scales)
+        load_wt(0)
         load_tab(0)
         nc.sync.dma_start(out=gain_rows[0:4, :], in_=gain.rearrange("(q t e) -> t q e", t=4, e=8))
         load_packed_rows(wk_sc_raw, wk_scales)
         nc.sync.dma_start(out=wk_raw[:], in_=wk_words.rearrange("a p c i -> p a (c i)").bitcast(I32))
-        load_wt(0)
         for q in range(4):
             load_wp_rows(q)
-        load_wt(1)
         nc.sync.dma_start(out=wp_raw[:], in_=wp_words.rearrange("a p c -> p a c").bitcast(I32))
-        load_tab(1)
+        load_wt(1)
         wo_rows = wo.rearrange("(q j e) n -> j q e n", j=4, e=8)
         for j in range(4):
             nc.sync.dma_start(out=wo_raw[j][:], in_=wo_rows[j])
+        load_tab(1)
         with nc.allow_non_contiguous_dma(reason="one bias value a partition"):
             nc.sync.dma_start(out=bias_sb[:], in_=bo.rearrange("(b p) -> p b", p=P))
 
@@ -222,12 +221,14 @@ def tile_list_chess_pattern_evaluation_kernel(
 
         h_bf = [placed("h_bf%d" % c, [P, 4 * CH], BF16, 8192 * (c + 1)) for c in range(LAST)]
         h_sc = [tile("h_sc%d" % c, [P, CH], U8) for c in range(LAST)]
-        y_sb = [tile("y%d" % c, [P, 2, CH], F32) for c in range(LAST)]
+        w_at = [32768 + 8192 * c for c in range(LAST)]
+        y_sb = [placed("y%d" % c, [P, 2, CH], F32, w_at[c + 1] - 1984) for c in range(LAST - 1)]
+        y_sb.append(tile("y%d" % (LAST - 1), [P, 2, CH], F32))
         out_v = out.rearrange("(b p) s -> p b s", p=P)
 
         def hidden(c, width, src_banks, dst):
-            v = tile("v%d" % c, [P, 4 * width], F32, tag="swap%d" % (c % 2))
-            w = tile("w%d" % c, [P, 4, width], F32, tag="swap%d" % ((c + 1) % 2))
+            v = placed("v%d" % c, [P, 4 * width], F32, w_at[c] - 8192 + 64)
+            w = placed("w%d" % c, [P, 4, width], F32, w_at[c])
             for b, bank in enumerate(src_banks):
                 nc.scalar.activation(
                     out=v[:, 512 * b : 512 * (b + 1)], in_=bank[:], func=ACT.Relu, scale=-1.0, bias=1.0
@@ -287,9 +288,14 @@ def tile_list_chess_pattern_evaluation_kernel(
             for c in range(2):
                 planes[(kind, c)] = plane[:, CH * c : CH * (c + 1)]
 
+        first_planes(THREAT, tile("threat_first", [P, 2 * CH], U8))
         first_planes(KING, tile("king_first", [P, 2 * CH], U8))
-        first_king = tile("first_king", [P, 2 * CH], U32)
-        gather_words(KING, 0, first_king[:], 0, 2 * CH)
+        cast_wt(0)
+        first_threat = tile("first_threat", [P, 2 * CH], U32)
+        gather_words(THREAT, 0, first_threat[:], 0, 2 * CH)
+        quantize_wt(0)
+        for c in range(2):
+            multiply(THREAT, 0, c, first_threat[:, CH * c : CH * (c + 1)])
         nc.vector.tensor_copy(
             out=wk_sc[:].bitcast(I32).rearrange("p (t q e) -> p t q e", t=4, e=2),
             in_=wk_sc_raw[:].bitcast(I32).rearrange("p (q t e) -> p t q e", t=4, e=2),
@@ -298,15 +304,7 @@ def tile_list_chess_pattern_evaluation_kernel(
             out=wk_q[:].rearrange("p (a t q e) -> p a t q e", a=2, t=4, e=8),
             in_=wk_raw[:].rearrange("p a (q t e) -> p a t q e", t=4, e=8),
         )
-        for c in range(2):
-            multiply(KING, 0, c, first_king[:, CH * c : CH * (c + 1)])
-        cast_wt(0)
-        first_planes(THREAT, placed("threat_first", [P, 2 * CH], U8, 8 * CH))
-        first_threat = placed("first_threat", [P, 2 * CH], U32, 0)
-        gather_words(THREAT, 0, first_threat[:], 0, 2 * CH)
-        quantize_wt(0)
-        for c in range(2):
-            multiply(THREAT, 0, c, first_threat[:, CH * c : CH * (c + 1)])
+        look_up_two(KING, placed("first_king", [P, 2 * CH], U32, 0))
         nc.vector.tensor_copy(
             out=wp_sc[:].bitcast(I32).rearrange("p (a t q e) -> p a t q e", a=2, t=4, e=2),
             in_=wp_sc_raw[:].bitcast(I32).rearrange("p (a q t e) -> p a t q e", a=2, t=4, e=2),
@@ -319,10 +317,8 @@ def tile_list_chess_pattern_evaluation_kernel(
         cast_wt(1)
         quantize_wt(1)
         second = ((KING, 1), (THREAT, 1), (PIECE, 1))
-        second_words = tile("second_words", [P, 6 * CH], U32, tag="wt_bf1")
         for c in range(2):
-            for i, (kind, a) in enumerate(second):
-                look_up(kind, a, c, second_words[:, CH * (3 * c + i) : CH * (3 * c + i + 1)])
+            look_up_group("second%d" % c, None, c, second, 69632 + 3072 * c)
         for j in range(4):
             nc.scalar.activation(out=wo_sgn[:, j, :], in_=wo_raw[j][:], func=ACT.Copy, scale=sgn[:, j : j + 1])
         nc.scalar.copy(
@@ -332,31 +328,29 @@ def tile_list_chess_pattern_evaluation_kernel(
         nc.vector.quantize_mx(out=wo_q[:].bitcast(FP8X4), scales=wo_sc[:], in_=wo_bf[:])
         hidden_chunk(0)
 
-        look_up_group("words2a", "wo_bf", 2, ((PIECE, 0),))
-        look_up_group("words2b", "wo_sgn", 2, ((PIECE, 1),))
-        chunk_plane(THREAT, 2, "king_first")
-        look_up_group("words2c", "wt_bf1", 2, ((THREAT, 0),))
-        evaluate_chunk(0, "wo_bf")
+        def later_planes(kind, offset):
+            plane = placed("later_plane%d" % kind, [P, 2 * CH], U8, offset)
+            gather_scales(kind, plane[:], 2 * CH, 2 * CH)
+            for c in (2, 3):
+                planes[(kind, c)] = plane[:, CH * (c - 2) : CH * (c - 1)]
+
+        look_up_group("words2a", None, 2, ((PIECE, 0), (PIECE, 1)), 61440 - 1920)
+        later_planes(THREAT, 61440 + 128)
+        later_planes(KING, 61440 + 640)
+        look_up_group("words2b", None, 2, ((THREAT, 0), (THREAT, 1), (KING, 0), (KING, 1)), 61440 + 1152)
+        evaluate_chunk(0)
         hidden_chunk(1)
         store_chunk(0)
-        look_up_group("words2d", None, 2, ((THREAT, 1),), 8192 - 896)
-        chunk_plane(KING, 2, None, 8192 + 128)
-        look_up_group("words2e", None, 2, ((KING, 0),), 8192 + 384)
-        look_up_group("words2f", None, 2, ((KING, 1),), 8192 + 1408)
 
-        look_up_group("words3a", "wo_bf", 3, ((PIECE, 0),))
-        look_up_group("words3b", "h_sc0", 3, ((PIECE, 1),))
+        look_up_group("words3a", None, 3, ((PIECE, 0), (PIECE, 1), (THREAT, 0), (THREAT, 1)), 8192)
         evaluate_chunk(1)
         hidden_chunk(2)
         store_chunk(1)
-        chunk_plane(THREAT, 3, None, 16384 + 128)
-        look_up_group("words3c", None, 3, ((THREAT, 0), (THREAT, 1)), 16384 - 1920)
-        chunk_plane(KING, 3, None, 16384 + 384)
-        look_up_group("words3d", None, 3, ((KING, 0), (KING, 1)), 16384 + 640)
+        look_up_group("words3b", None, 3, ((KING, 0), (KING, 1)), 16384)
         evaluate_chunk(2)
 
         first_bank, second_bank = banks[2 * LAST], banks[2 * LAST + 1]
-        v = tile("v_last", [P, 4 * CH], F32, tag="swap1")
+        v = placed("v_last", [P, 4 * CH], F32, w_at[LAST - 1] + 64)
         w = tile("w_last", [P, 4, CH], F32)
         last_bf = [tile("last_bf%d" % u, [P, 4 * HALF], BF16) for u in range(2)]
         last_q = [tile("last_q%d" % u, [P, HALF], U32) for u in range(2)]

@@ -60,7 +60,7 @@ def tile_list_chess_pattern_evaluation_kernel(
         wo_raw = [tile("wo_raw%d" % j, [P, N], F32) for j in range(4)]
         wo_sgn = tile("wo_sgn", [P, 4, N], BF16)
         wo_bf = placed("wo_bf", [P, 4 * N], BF16, 61440)
-        wo_q = placed("wo_q", [P, N], U32, 69632)
+        wo_q = tile("wo_q", [P, N], U32)
         wo_sc = tile("wo_sc", [P, N], U8)
         gain_rows = tile("gain_rows", [P, P], F32)
         ident = tile("ident", [P, P], F32)
@@ -68,10 +68,10 @@ def tile_list_chess_pattern_evaluation_kernel(
         banks = [ps.tile([P, 512], F32, name="bank%d" % b) for b in range(8)]
 
         nc.vector.memset(tab_sc[:].bitcast(I32), 0)
+        nc.vector.memset(gain_rows[:], 0.0)
         nc.vector.memset(wk_sc_raw[:].bitcast(I32), 0)
         nc.vector.memset(wp_sc_raw[:].bitcast(I32), 0)
         nc.vector.memset(piece_sc1[:].bitcast(I32), 0)
-        nc.gpsimd.memset(gain_rows[:], 0.0)
         make_identity(nc, ident[:])
 
         def load_wt(a):
@@ -93,8 +93,9 @@ def tile_list_chess_pattern_evaluation_kernel(
             )
 
         nc.sync.dma_start(lists[PIECE][:], offs)
-        nc.sync.dma_start(lists[KING][:], offs2)
         nc.sync.dma_start(lists[THREAT][:], offs3)
+        nc.sync.dma_start(lists[KING][:], offs2)
+        nc.sync.dma_start(out=wp_raw[:], in_=wp_words.rearrange("a p c -> p a c").bitcast(I32))
         load_packed_rows(tab_sc, tab_scales)
         load_wt(0)
         load_tab(0)
@@ -103,12 +104,16 @@ def tile_list_chess_pattern_evaluation_kernel(
         nc.sync.dma_start(out=wk_raw[:], in_=wk_words.rearrange("a p c i -> p a (c i)").bitcast(I32))
         for q in range(4):
             load_wp_rows(q)
-        nc.sync.dma_start(out=wp_raw[:], in_=wp_words.rearrange("a p c -> p a c").bitcast(I32))
         load_wt(1)
+        nc.vector.tensor_copy(out=piece_sc[:], in_=tab_sc[:].indirect(lists[PIECE][:]))
+        for q in range(4):
+            nc.sync.dma_start(
+                out=piece_sc1[32 * q : 32 * q + 4, :].bitcast(I32), in_=piece_sc[32 * q + 4 : 32 * q + 8, :].bitcast(I32)
+            )
+        load_tab(1)
         wo_rows = wo.rearrange("(q j e) n -> j q e n", j=4, e=8)
         for j in range(4):
             nc.sync.dma_start(out=wo_raw[j][:], in_=wo_rows[j])
-        load_tab(1)
         with nc.allow_non_contiguous_dma(reason="one bias value a partition"):
             nc.sync.dma_start(out=bias_sb[:], in_=bo.rearrange("(b p) -> p b", p=P))
 
@@ -172,8 +177,11 @@ def tile_list_chess_pattern_evaluation_kernel(
                 plane = (piece_sc, piece_sc1)[a][:, lo : lo + CH]
             else:
                 plane = planes[(kind, c)][4 * a : P, :]
-            width = HALF if kind == PIECE else CH
-            steps = [(t, x, 2 * c + t // 2, (t % 2) * CH + x) for t in range(4) for x in range(0, CH, width)]
+            width = HALF if kind == PIECE or c == LAST else CH
+            if c == LAST:
+                steps = [(t, x, 2 * c + x // HALF, t * HALF) for x in (0, HALF) for t in range(4)]
+            else:
+                steps = [(t, x, 2 * c + t // 2, (t % 2) * CH + x) for t in range(4) for x in range(0, CH, width)]
             for t, x, b, col in steps:
                 m = slice(128 * t, 128 * (t + 1))
                 am = slice(H * a + 128 * t, H * a + 128 * (t + 1))
@@ -277,12 +285,6 @@ def tile_list_chess_pattern_evaluation_kernel(
                 )
             nc.sync.dma_start(out=out_v[:, :, c * CH : (c + 1) * CH], in_=y_sb[c][:])
 
-        gather_scales(PIECE, piece_sc[:], 0, S)
-        for q in range(4):
-            nc.gpsimd.dma_start(
-                out=piece_sc1[32 * q : 32 * q + 4, :].bitcast(I32), in_=piece_sc[32 * q + 4 : 32 * q + 8, :].bitcast(I32)
-            )
-
         def first_planes(kind, plane):
             gather_scales(kind, plane[:], 0, 2 * CH)
             for c in range(2):
@@ -313,7 +315,7 @@ def tile_list_chess_pattern_evaluation_kernel(
             out=wp_q[:].bitcast(I32).rearrange("p (a t q e) -> p a t q e", a=2, t=4, e=4),
             in_=wp_raw[:].rearrange("p a (q t e) -> p a t q e", t=4, e=4),
         )
-        look_up_two(PIECE, tile("first_piece", [P, 2 * CH], U32, tag="wp_raw"))
+        look_up_two(PIECE, tile("first_piece", [P, 2 * CH], U32, tag="wp_sc_raw"))
         cast_wt(1)
         quantize_wt(1)
         second = ((KING, 1), (THREAT, 1), (PIECE, 1))
@@ -325,7 +327,6 @@ def tile_list_chess_pattern_evaluation_kernel(
             out=wo_bf[:].rearrange("p (n i j) -> p n j i", i=4, j=4),
             in_=wo_sgn[:].rearrange("p j (n i) -> p n j i", i=4),
         )
-        nc.vector.quantize_mx(out=wo_q[:].bitcast(FP8X4), scales=wo_sc[:], in_=wo_bf[:])
         hidden_chunk(0)
 
         def later_planes(kind, offset):
@@ -334,10 +335,11 @@ def tile_list_chess_pattern_evaluation_kernel(
             for c in (2, 3):
                 planes[(kind, c)] = plane[:, CH * (c - 2) : CH * (c - 1)]
 
-        look_up_group("words2a", None, 2, ((PIECE, 0), (PIECE, 1)), 61440 - 1920)
-        later_planes(THREAT, 61440 + 128)
-        later_planes(KING, 61440 + 640)
-        look_up_group("words2b", None, 2, ((THREAT, 0), (THREAT, 1), (KING, 0), (KING, 1)), 61440 + 1152)
+        look_up_group("words2a", None, 2, ((PIECE, 0), (PIECE, 1)), 69632)
+        later_planes(THREAT, 69632 + 2048)
+        later_planes(KING, 69632 + 2560)
+        nc.vector.quantize_mx(out=wo_q[:].bitcast(FP8X4), scales=wo_sc[:], in_=wo_bf[:])
+        look_up_group("words2b", None, 2, ((THREAT, 0), (THREAT, 1), (KING, 0), (KING, 1)), 61440)
         evaluate_chunk(0)
         hidden_chunk(1)
         store_chunk(0)
@@ -347,43 +349,26 @@ def tile_list_chess_pattern_evaluation_kernel(
         hidden_chunk(2)
         store_chunk(1)
         look_up_group("words3b", None, 3, ((KING, 0), (KING, 1)), 16384)
-        evaluate_chunk(2)
 
-        first_bank, second_bank = banks[2 * LAST], banks[2 * LAST + 1]
-        v = placed("v_last", [P, 4 * CH], F32, w_at[LAST - 1] + 64)
-        w = tile("w_last", [P, 4, CH], F32)
-        last_bf = [tile("last_bf%d" % u, [P, 4 * HALF], BF16) for u in range(2)]
+        last_bf = [placed("last_bf%d" % u, [P, 4 * HALF], BF16, 8192 * LAST + 1024 * u) for u in range(2)]
         last_q = [tile("last_q%d" % u, [P, HALF], U32) for u in range(2)]
         last_sc = [tile("last_sc%d" % u, [P, HALF], U8) for u in range(2)]
         last_y = [tile("last_y%d" % u, [P, 2, HALF], F32) for u in range(2)]
-        nc.vector.tensor_scalar(
-            out=v[:, 0:512], in0=first_bank[:], scalar1=0.0, scalar2=1.0, op0=ALU.max, op1=ALU.min
-        )
-        for t in (2, 3):
-            nc.scalar.activation(
-                out=v[:, CH * t : CH * (t + 1)],
-                in_=second_bank[:, CH * (t - 2) : CH * (t - 1)],
-                func=ACT.Relu,
-                scale=root[:, t : t + 1],
+        capped = [tile("capped%d" % u, [P, HALF, 4], F32) for u in range(2)]
+        for u in range(2):
+            nc.vector.scalar_tensor_tensor(
+                out=capped[u][:],
+                in0=banks[2 * LAST + u][:].rearrange("p (t n) -> p n t", t=4),
+                scalar=1.0,
+                in1=root[:].unsqueeze(1).to_broadcast([P, HALF, 4]),
+                op0=ALU.min,
+                op1=ALU.mult,
             )
-        for t in range(4):
-            nc.vector.tensor_scalar(
-                out=w[:, t, :],
-                in0=v[:, CH * t : CH * (t + 1)],
-                scalar1=root[:, t : t + 1],
-                scalar2=None,
-                op0=ALU.mult if t < 2 else ALU.min,
-            )
+        evaluate_chunk(2)
         store_chunk(2)
-        woven = [
-            (
-                last_bf[u][:].rearrange("p (n i t) -> p n t i", i=4, t=4),
-                w[:, :, HALF * u : HALF * (u + 1)].rearrange("p t (n i) -> p n t i", i=4),
-            )
-            for u in range(2)
-        ]
-        nc.scalar.activation(out=woven[0][0], in_=woven[0][1], func=ACT.Square)
-        nc.vector.tensor_tensor(out=woven[1][0], in0=woven[1][1], in1=woven[1][1], op=ALU.mult)
+        for u in range(2):
+            flat = capped[u][:].rearrange("p n t -> p (n t)")
+            nc.vector.scalar_tensor_tensor(out=last_bf[u][:], in0=flat, scalar=0.0, in1=flat, op0=ALU.max, op1=ALU.mult)
         for u in range(2):
             evaluate(last_bf[u][:], last_q[u][:], last_sc[u][:], banks[1 + 2 * u], HALF)
         for u in range(2):

@@ -50,7 +50,10 @@ def tile_list_chess_pattern_evaluation_kernel(
         piece_sc = tile("piece_sc", [P, S], U8)
         piece_sc1 = tile("piece_sc1", [P, S], U8)
         wt_raw = [tile("wt_raw%d" % a, [P, 4, H], F32) for a in range(PASSES)]
-        wt_bf = [tile("wt_bf0", [P, 4 * H], BF16), placed("wt_bf1", [P, 4 * H], BF16, 69632)]
+        wt_bf = [
+            [tile("wt_bf0", [P, 4 * H], BF16)],
+            [placed("wt_bf1", [P, 2 * H], BF16, 69632), tile("wt_bf2", [P, 2 * H], BF16)],
+        ]
         wt_q = [tile("wt_q%d" % a, [P, H], U32) for a in range(PASSES)]
         wt_sc = [tile("wt_sc%d" % a, [P, H], U8) for a in range(PASSES)]
         wk_raw = placed("wk_raw", [P, PASSES, H], I32, 0)
@@ -58,8 +61,8 @@ def tile_list_chess_pattern_evaluation_kernel(
         wp_raw = tile("wp_raw", [P, PASSES, H // 2], I32)
         wp_q = tile("wp_q", [P, PASSES * 2 * H], U8)
         wo_raw = [tile("wo_raw%d" % j, [P, N], F32) for j in range(4)]
-        wo_sgn = tile("wo_sgn", [P, 4, N], BF16)
-        wo_bf = placed("wo_bf", [P, 4 * N], BF16, 61440)
+        wo_sgn = placed("wo_sgn", [P, 4, N], BF16, 24576)
+        wo_bf = tile("wo_bf", [P, 4 * N], BF16)
         wo_q = tile("wo_q", [P, N], U32)
         wo_sc = tile("wo_sc", [P, N], U8)
         gain_rows = tile("gain_rows", [P, P], F32)
@@ -93,23 +96,18 @@ def tile_list_chess_pattern_evaluation_kernel(
             )
 
         nc.sync.dma_start(lists[PIECE][:], offs)
-        nc.sync.dma_start(lists[THREAT][:], offs3)
         nc.sync.dma_start(lists[KING][:], offs2)
+        nc.sync.dma_start(lists[THREAT][:], offs3)
         nc.sync.dma_start(out=wp_raw[:], in_=wp_words.rearrange("a p c -> p a c").bitcast(I32))
         load_packed_rows(tab_sc, tab_scales)
-        load_wt(0)
         load_tab(0)
         nc.sync.dma_start(out=gain_rows[0:4, :], in_=gain.rearrange("(q t e) -> t q e", t=4, e=8))
-        load_packed_rows(wk_sc_raw, wk_scales)
         nc.sync.dma_start(out=wk_raw[:], in_=wk_words.rearrange("a p c i -> p a (c i)").bitcast(I32))
+        load_packed_rows(wk_sc_raw, wk_scales)
+        load_wt(0)
+        load_wt(1)
         for q in range(4):
             load_wp_rows(q)
-        load_wt(1)
-        nc.vector.tensor_copy(out=piece_sc[:], in_=tab_sc[:].indirect(lists[PIECE][:]))
-        for q in range(4):
-            nc.sync.dma_start(
-                out=piece_sc1[32 * q : 32 * q + 4, :].bitcast(I32), in_=piece_sc[32 * q + 4 : 32 * q + 8, :].bitcast(I32)
-            )
         load_tab(1)
         wo_rows = wo.rearrange("(q j e) n -> j q e n", j=4, e=8)
         for j in range(4):
@@ -118,36 +116,15 @@ def tile_list_chess_pattern_evaluation_kernel(
             nc.sync.dma_start(out=bias_sb[:], in_=bo.rearrange("(b p) -> p b", p=P))
 
         mag = tile("mag", [P, 4], F32)
-        inv = tile("inv", [P, 4], F32)
-        root0 = tile("root0", [P, 4], F32)
-        sq = tile("sq", [P, 4], F32)
-        res = tile("res", [P, 4], F32)
         root = tile("root", [P, 4], F32)
         neg_root = tile("neg_root", [P, 4], F32)
         sgn0 = tile("sgn0", [P, 4], F32)
         sgn = tile("sgn", [P, 4], F32)
-        half_inv = tile("half_inv", [P, 4], F32)
         nc.tensor.transpose(banks[7][:, 0:P], gain_rows[:], ident[:])
-        nc.scalar.activation(out=mag[:], in_=banks[7][:, 0:4], func=ACT.Abs)
         nc.scalar.activation(out=sgn0[:], in_=banks[7][:, 0:4], func=ACT.Sign)
-        nc.scalar.activation(out=inv[:], in_=mag[:], func=ACT.Abs_reciprocal_sqrt, bias=2.0**-100)
-        for t in range(4):
-            nc.scalar.activation(out=root0[:, t : t + 1], in_=mag[:, t : t + 1], func=ACT.Copy, scale=inv[:, t : t + 1])
-        nc.scalar.activation(out=half_inv[:], in_=inv[:], func=ACT.Copy, scale=0.5)
-        nc.scalar.activation(out=sq[:], in_=root0[:], func=ACT.Square)
+        nc.scalar.activation(out=mag[:], in_=banks[7][:, 0:4], func=ACT.Abs)
         nc.scalar.activation(out=sgn[:], in_=sgn0[:], func=ACT.Sign, bias=0.5)
-        for t in range(4):
-            nc.scalar.activation(
-                out=res[:, t : t + 1], in_=sq[:, t : t + 1], func=ACT.Identity, scale=-1.0, bias=mag[:, t : t + 1]
-            )
-        for t in range(4):
-            nc.scalar.activation(
-                out=root[:, t : t + 1],
-                in_=res[:, t : t + 1],
-                func=ACT.Identity,
-                scale=half_inv[:, t : t + 1],
-                bias=root0[:, t : t + 1],
-            )
+        nc.scalar.activation(out=root[:], in_=mag[:], func=ACT.Sqrt)
         nc.scalar.activation(out=neg_root[:], in_=root[:], func=ACT.Copy, scale=-1.0)
 
         def offsets(kind, start, count):
@@ -162,11 +139,18 @@ def tile_list_chess_pattern_evaluation_kernel(
         def cast_wt(a):
             src = wt_raw[a][:].rearrange("p j (q t u i) -> p t q u j i", t=4, u=2, i=4)
             for t in range(4):
-                dst = wt_bf[a][:, 512 * t : 512 * (t + 1)].rearrange("p (q u i j) -> p q u j i", u=2, i=4, j=4)
+                part, first = divmod(512 * t, wt_bf[a][0].shape[1])
+                dst = wt_bf[a][part][:, first : first + 512].rearrange("p (q u i j) -> p q u j i", u=2, i=4, j=4)
                 nc.scalar.copy(out=dst, in_=src[:, t])
 
+        def quantize(codes, scales, parts):
+            width = codes.shape[1] // len(parts)
+            for i, part in enumerate(parts):
+                cols = slice(width * i, width * (i + 1))
+                nc.vector.quantize_mx(out=codes[:, cols].bitcast(FP8X4), scales=scales[:, cols], in_=part[:])
+
         def quantize_wt(a):
-            nc.vector.quantize_mx(out=wt_q[a][:].bitcast(FP8X4), scales=wt_sc[a][:], in_=wt_bf[a][:])
+            quantize(wt_q[a][:], wt_sc[a][:], wt_bf[a])
 
         planes = {}
         columns_done = {}
@@ -210,11 +194,6 @@ def tile_list_chess_pattern_evaluation_kernel(
             gather_words(kind, a, words, c * CH, CH)
             multiply(kind, a, c, words)
 
-        def look_up_two(kind, words):
-            gather_words(kind, 0, words[:], 0, 2 * CH)
-            for c in range(2):
-                multiply(kind, 0, c, words[:, CH * c : CH * (c + 1)])
-
         def look_up_group(name, tag, c, steps, offset=None):
             shape = [P, len(steps) * CH]
             words = tile(name, shape, U32, tag=tag) if offset is None else placed(name, shape, U32, offset)
@@ -227,14 +206,18 @@ def tile_list_chess_pattern_evaluation_kernel(
             gather_scales(kind, plane[:], c * CH, CH)
             planes[(kind, c)] = plane[:]
 
-        h_bf = [placed("h_bf%d" % c, [P, 4 * CH], BF16, 8192 * (c + 1)) for c in range(LAST)]
+        h_bf = [
+            [placed("h_bf%d" % c, [P, 2 * CH], BF16, 8192 * (c + 1)), tile("h_rest%d" % c, [P, 2 * CH], BF16)]
+            for c in range(LAST - 1)
+        ]
+        h_bf.append([placed("h_bf%d" % (LAST - 1), [P, 4 * CH], BF16, 8192 * LAST)])
         h_sc = [tile("h_sc%d" % c, [P, CH], U8) for c in range(LAST)]
-        w_at = [32768 + 8192 * c for c in range(LAST)]
-        y_sb = [placed("y%d" % c, [P, 2, CH], F32, w_at[c + 1] - 1984) for c in range(LAST - 1)]
-        y_sb.append(tile("y%d" % (LAST - 1), [P, 2, CH], F32))
+        w_at = [32768 + 8192 * c for c in range(LAST + 1)]
+        y_at = (w_at[2] - 1984, w_at[2] + 64, w_at[3] - 1984)
+        y_sb = [placed("y%d" % c, [P, 2, CH], F32, y_at[c]) for c in range(LAST)]
         out_v = out.rearrange("(b p) s -> p b s", p=P)
 
-        def hidden(c, width, src_banks, dst):
+        def hidden(c, width, src_banks, parts):
             v = placed("v%d" % c, [P, 4 * width], F32, w_at[c] - 8192 + 64)
             w = placed("w%d" % c, [P, 4, width], F32, w_at[c])
             for b, bank in enumerate(src_banks):
@@ -249,14 +232,16 @@ def tile_list_chess_pattern_evaluation_kernel(
                     scale=neg_root[:, t : t + 1],
                     bias=root[:, t : t + 1],
                 )
-            nc.scalar.activation(
-                out=dst.rearrange("p (n i t) -> p n t i", i=4, t=4),
-                in_=w[:].rearrange("p t (n i) -> p n t i", i=4),
-                func=ACT.Square,
-            )
+            step = width // len(parts)
+            for i, part in enumerate(parts):
+                nc.scalar.activation(
+                    out=part[:].rearrange("p (n i t) -> p n t i", i=4, t=4),
+                    in_=w[:, :, step * i : step * (i + 1)].rearrange("p t (n i) -> p n t i", i=4),
+                    func=ACT.Square,
+                )
 
-        def evaluate(src, codes, scales, bank, width):
-            nc.vector.quantize_mx(out=codes.bitcast(FP8X4), scales=scales, in_=src)
+        def evaluate(parts, codes, scales, bank, width):
+            quantize(codes, scales, parts)
             for b in range(2):
                 nc.tensor.matmul_mx(
                     out=bank[:, width * b : width * (b + 1)],
@@ -269,11 +254,11 @@ def tile_list_chess_pattern_evaluation_kernel(
                 )
 
         def hidden_chunk(c):
-            hidden(c, CH, banks[2 * c : 2 * c + 2], h_bf[c][:])
+            hidden(c, CH, banks[2 * c : 2 * c + 2], h_bf[c])
 
         def evaluate_chunk(c, tag=None):
             h_q = tile("h_q%d" % c, [P, CH], U32, tag=tag)
-            evaluate(h_bf[c][:], h_q[:], h_sc[c][:], banks[2 * c], CH)
+            evaluate(h_bf[c], h_q[:], h_sc[c][:], banks[2 * c], CH)
 
         def store_chunk(c):
             for b in range(2):
@@ -285,28 +270,39 @@ def tile_list_chess_pattern_evaluation_kernel(
                 )
             nc.sync.dma_start(out=out_v[:, :, c * CH : (c + 1) * CH], in_=y_sb[c][:])
 
+        gather_scales(PIECE, piece_sc[:], 0, S)
+        for q in range(4):
+            nc.gpsimd.dma_start(
+                out=piece_sc1[32 * q : 32 * q + 4, :].bitcast(I32), in_=piece_sc[32 * q + 4 : 32 * q + 8, :].bitcast(I32)
+            )
+
         def first_planes(kind, plane):
             gather_scales(kind, plane[:], 0, 2 * CH)
             for c in range(2):
                 planes[(kind, c)] = plane[:, CH * c : CH * (c + 1)]
 
-        first_planes(THREAT, tile("threat_first", [P, 2 * CH], U8))
+        def multiply_two(kind, words):
+            for c in range(2):
+                multiply(kind, 0, c, words[:, CH * c : CH * (c + 1)])
+
         first_planes(KING, tile("king_first", [P, 2 * CH], U8))
-        cast_wt(0)
-        first_threat = tile("first_threat", [P, 2 * CH], U32)
-        gather_words(THREAT, 0, first_threat[:], 0, 2 * CH)
-        quantize_wt(0)
-        for c in range(2):
-            multiply(THREAT, 0, c, first_threat[:, CH * c : CH * (c + 1)])
-        nc.vector.tensor_copy(
-            out=wk_sc[:].bitcast(I32).rearrange("p (t q e) -> p t q e", t=4, e=2),
-            in_=wk_sc_raw[:].bitcast(I32).rearrange("p (q t e) -> p t q e", t=4, e=2),
-        )
+        first_king = tile("first_king", [P, 2 * CH], U32)
+        gather_words(KING, 0, first_king[:], 0, 2 * CH)
         nc.vector.tensor_copy(
             out=wk_q[:].rearrange("p (a t q e) -> p a t q e", a=2, t=4, e=8),
             in_=wk_raw[:].rearrange("p a (q t e) -> p a t q e", t=4, e=8),
         )
-        look_up_two(KING, placed("first_king", [P, 2 * CH], U32, 0))
+        nc.vector.tensor_copy(
+            out=wk_sc[:].bitcast(I32).rearrange("p (t q e) -> p t q e", t=4, e=2),
+            in_=wk_sc_raw[:].bitcast(I32).rearrange("p (q t e) -> p t q e", t=4, e=2),
+        )
+        multiply_two(KING, first_king)
+        first_planes(THREAT, placed("threat_first", [P, 2 * CH], U8, 2048))
+        first_threat = placed("first_threat", [P, 2 * CH], U32, 0)
+        gather_words(THREAT, 0, first_threat[:], 0, 2 * CH)
+        cast_wt(0)
+        quantize_wt(0)
+        multiply_two(THREAT, first_threat)
         nc.vector.tensor_copy(
             out=wp_sc[:].bitcast(I32).rearrange("p (a t q e) -> p a t q e", a=2, t=4, e=2),
             in_=wp_sc_raw[:].bitcast(I32).rearrange("p (a q t e) -> p a t q e", a=2, t=4, e=2),
@@ -315,12 +311,12 @@ def tile_list_chess_pattern_evaluation_kernel(
             out=wp_q[:].bitcast(I32).rearrange("p (a t q e) -> p a t q e", a=2, t=4, e=4),
             in_=wp_raw[:].rearrange("p a (q t e) -> p a t q e", t=4, e=4),
         )
-        look_up_two(PIECE, tile("first_piece", [P, 2 * CH], U32, tag="wp_sc_raw"))
+        look_up_group("first_piece", "wp_sc_raw", 0, ((PIECE, 0),))
         cast_wt(1)
         quantize_wt(1)
         second = ((KING, 1), (THREAT, 1), (PIECE, 1))
-        for c in range(2):
-            look_up_group("second%d" % c, None, c, second, 69632 + 3072 * c)
+        look_up_group("second0", None, 0, second, 66688)
+        look_up_group("second1", None, 1, ((PIECE, 0),) + second, 71616)
         for j in range(4):
             nc.scalar.activation(out=wo_sgn[:, j, :], in_=wo_raw[j][:], func=ACT.Copy, scale=sgn[:, j : j + 1])
         nc.scalar.copy(
@@ -329,32 +325,30 @@ def tile_list_chess_pattern_evaluation_kernel(
         )
         hidden_chunk(0)
 
-        def later_planes(kind, offset):
-            plane = placed("later_plane%d" % kind, [P, 2 * CH], U8, offset)
-            gather_scales(kind, plane[:], 2 * CH, 2 * CH)
-            for c in (2, 3):
-                planes[(kind, c)] = plane[:, CH * (c - 2) : CH * (c - 1)]
-
-        look_up_group("words2a", None, 2, ((PIECE, 0), (PIECE, 1)), 69632)
-        later_planes(THREAT, 69632 + 2048)
-        later_planes(KING, 69632 + 2560)
+        chunk_plane(THREAT, 2, None, 66688 + 64)
+        chunk_plane(KING, 2, None, 66688 + 320)
+        look_up_group("words2a", None, 2, ((PIECE, 0), (PIECE, 1)), 66688 + 576)
+        look_up_group("words2b", None, 2, ((THREAT, 0), (THREAT, 1), (KING, 0), (KING, 1)), 66688 + 64 - 4096)
         nc.vector.quantize_mx(out=wo_q[:].bitcast(FP8X4), scales=wo_sc[:], in_=wo_bf[:])
-        look_up_group("words2b", None, 2, ((THREAT, 0), (THREAT, 1), (KING, 0), (KING, 1)), 61440)
         evaluate_chunk(0)
         hidden_chunk(1)
-        store_chunk(0)
 
-        look_up_group("words3a", None, 3, ((PIECE, 0), (PIECE, 1), (THREAT, 0), (THREAT, 1)), 8192)
+        look_up_group("words3a", None, 3, ((PIECE, 0), (PIECE, 1)), 8192 + 320)
+        chunk_plane(THREAT, 3, None, 8192 + 64)
         evaluate_chunk(1)
         hidden_chunk(2)
+        store_chunk(0)
         store_chunk(1)
-        look_up_group("words3b", None, 3, ((KING, 0), (KING, 1)), 16384)
+        look_up_group("words3b", None, 3, ((THREAT, 0), (THREAT, 1)), 16384 + 64 - 2048)
+        chunk_plane(KING, 3, None, 16384 + 64)
+        look_up_group("words3c", None, 3, ((KING, 0), (KING, 1)), 16384 + 320)
 
-        last_bf = [placed("last_bf%d" % u, [P, 4 * HALF], BF16, 8192 * LAST + 1024 * u) for u in range(2)]
+        evaluate_chunk(2)
+        last_bf = [tile("last_bf%d" % u, [P, 4 * HALF], BF16) for u in range(2)]
         last_q = [tile("last_q%d" % u, [P, HALF], U32) for u in range(2)]
         last_sc = [tile("last_sc%d" % u, [P, HALF], U8) for u in range(2)]
         last_y = [tile("last_y%d" % u, [P, 2, HALF], F32) for u in range(2)]
-        capped = [tile("capped%d" % u, [P, HALF, 4], F32) for u in range(2)]
+        capped = [placed("capped%d" % u, [P, HALF, 4], F32, 8192 * LAST - 1024 + 2048 * u) for u in range(2)]
         for u in range(2):
             nc.vector.scalar_tensor_tensor(
                 out=capped[u][:],
@@ -364,13 +358,16 @@ def tile_list_chess_pattern_evaluation_kernel(
                 op0=ALU.min,
                 op1=ALU.mult,
             )
-        evaluate_chunk(2)
+        flat = [capped[u][:].rearrange("p n t -> p (n t)") for u in range(2)]
+        floored = placed("floored", [P, 4 * HALF], F32, w_at[LAST])
+        nc.scalar.activation(out=floored[:], in_=flat[0], func=ACT.Relu)
+        nc.scalar.activation(out=last_bf[0][:], in_=floored[:], func=ACT.Square)
+        nc.vector.scalar_tensor_tensor(
+            out=last_bf[1][:], in0=flat[1], scalar=0.0, in1=flat[1], op0=ALU.max, op1=ALU.mult
+        )
         store_chunk(2)
         for u in range(2):
-            flat = capped[u][:].rearrange("p n t -> p (n t)")
-            nc.vector.scalar_tensor_tensor(out=last_bf[u][:], in0=flat, scalar=0.0, in1=flat, op0=ALU.max, op1=ALU.mult)
-        for u in range(2):
-            evaluate(last_bf[u][:], last_q[u][:], last_sc[u][:], banks[1 + 2 * u], HALF)
+            evaluate(last_bf[u : u + 1], last_q[u][:], last_sc[u][:], banks[1 + 2 * u], HALF)
         for u in range(2):
             for b in range(2):
                 src = banks[1 + 2 * u][:, HALF * b : HALF * (b + 1)]

@@ -102,8 +102,8 @@ def tile_list_chess_pattern_evaluation_kernel(
         load_packed_rows(tab_sc, tab_scales)
         load_tab(0)
         nc.sync.dma_start(out=gain_rows[0:4, :], in_=gain.rearrange("(q t e) -> t q e", t=4, e=8))
-        nc.sync.dma_start(out=wk_raw[:], in_=wk_words.rearrange("a p c i -> p a (c i)").bitcast(I32))
         load_packed_rows(wk_sc_raw, wk_scales)
+        nc.sync.dma_start(out=wk_raw[:], in_=wk_words.rearrange("a p c i -> p a (c i)").bitcast(I32))
         load_wt(0)
         load_wt(1)
         for q in range(4):
@@ -200,12 +200,6 @@ def tile_list_chess_pattern_evaluation_kernel(
             for i, (kind, a) in enumerate(steps):
                 look_up(kind, a, c, words[:, CH * i : CH * (i + 1)])
 
-        def chunk_plane(kind, c, tag, offset=None):
-            name = "plane%d_%d" % (kind, c)
-            plane = tile(name, [P, CH], U8, tag=tag) if offset is None else placed(name, [P, CH], U8, offset)
-            gather_scales(kind, plane[:], c * CH, CH)
-            planes[(kind, c)] = plane[:]
-
         h_bf = [
             [placed("h_bf%d" % c, [P, 2 * CH], BF16, 8192 * (c + 1)), tile("h_rest%d" % c, [P, 2 * CH], BF16)]
             for c in range(LAST - 1)
@@ -276,28 +270,28 @@ def tile_list_chess_pattern_evaluation_kernel(
                 out=piece_sc1[32 * q : 32 * q + 4, :].bitcast(I32), in_=piece_sc[32 * q + 4 : 32 * q + 8, :].bitcast(I32)
             )
 
-        def first_planes(kind, plane):
-            gather_scales(kind, plane[:], 0, 2 * CH)
-            for c in range(2):
+        def whole_plane(kind, plane):
+            gather_scales(kind, plane[:], 0, S)
+            for c in range(LAST + 1):
                 planes[(kind, c)] = plane[:, CH * c : CH * (c + 1)]
 
         def multiply_two(kind, words):
             for c in range(2):
                 multiply(kind, 0, c, words[:, CH * c : CH * (c + 1)])
 
-        first_planes(KING, tile("king_first", [P, 2 * CH], U8))
+        whole_plane(KING, tile("king_plane", [P, S], U8))
         first_king = tile("first_king", [P, 2 * CH], U32)
         gather_words(KING, 0, first_king[:], 0, 2 * CH)
-        nc.vector.tensor_copy(
-            out=wk_q[:].rearrange("p (a t q e) -> p a t q e", a=2, t=4, e=8),
-            in_=wk_raw[:].rearrange("p a (q t e) -> p a t q e", t=4, e=8),
-        )
         nc.vector.tensor_copy(
             out=wk_sc[:].bitcast(I32).rearrange("p (t q e) -> p t q e", t=4, e=2),
             in_=wk_sc_raw[:].bitcast(I32).rearrange("p (q t e) -> p t q e", t=4, e=2),
         )
+        nc.vector.tensor_copy(
+            out=wk_q[:].rearrange("p (a t q e) -> p a t q e", a=2, t=4, e=8),
+            in_=wk_raw[:].rearrange("p a (q t e) -> p a t q e", t=4, e=8),
+        )
         multiply_two(KING, first_king)
-        first_planes(THREAT, placed("threat_first", [P, 2 * CH], U8, 2048))
+        whole_plane(THREAT, placed("threat_plane", [P, S], U8, 2048))
         first_threat = placed("first_threat", [P, 2 * CH], U32, 0)
         gather_words(THREAT, 0, first_threat[:], 0, 2 * CH)
         cast_wt(0)
@@ -311,12 +305,14 @@ def tile_list_chess_pattern_evaluation_kernel(
             out=wp_q[:].bitcast(I32).rearrange("p (a t q e) -> p a t q e", a=2, t=4, e=4),
             in_=wp_raw[:].rearrange("p a (q t e) -> p a t q e", t=4, e=4),
         )
-        look_up_group("first_piece", "wp_sc_raw", 0, ((PIECE, 0),))
+        first_piece = tile("first_piece", [P, 2 * CH], U32, tag="wt_bf0")
+        gather_words(PIECE, 0, first_piece[:], 0, 2 * CH)
+        multiply_two(PIECE, first_piece)
         cast_wt(1)
         quantize_wt(1)
         second = ((KING, 1), (THREAT, 1), (PIECE, 1))
         look_up_group("second0", None, 0, second, 66688)
-        look_up_group("second1", None, 1, ((PIECE, 0),) + second, 71616)
+        look_up_group("second1", None, 1, second, 71616)
         for j in range(4):
             nc.scalar.activation(out=wo_sgn[:, j, :], in_=wo_raw[j][:], func=ACT.Copy, scale=sgn[:, j : j + 1])
         nc.scalar.copy(
@@ -325,30 +321,24 @@ def tile_list_chess_pattern_evaluation_kernel(
         )
         hidden_chunk(0)
 
-        chunk_plane(THREAT, 2, None, 66688 + 64)
-        chunk_plane(KING, 2, None, 66688 + 320)
         look_up_group("words2a", None, 2, ((PIECE, 0), (PIECE, 1)), 66688 + 576)
         look_up_group("words2b", None, 2, ((THREAT, 0), (THREAT, 1), (KING, 0), (KING, 1)), 66688 + 64 - 4096)
         nc.vector.quantize_mx(out=wo_q[:].bitcast(FP8X4), scales=wo_sc[:], in_=wo_bf[:])
         evaluate_chunk(0)
         hidden_chunk(1)
 
-        look_up_group("words3a", None, 3, ((PIECE, 0), (PIECE, 1)), 8192 + 320)
-        chunk_plane(THREAT, 3, None, 8192 + 64)
+        look_up_group("words3a", None, 3, ((PIECE, 0), (PIECE, 1), (THREAT, 0), (THREAT, 1)), 8192)
         evaluate_chunk(1)
         hidden_chunk(2)
         store_chunk(0)
         store_chunk(1)
-        look_up_group("words3b", None, 3, ((THREAT, 0), (THREAT, 1)), 16384 + 64 - 2048)
-        chunk_plane(KING, 3, None, 16384 + 64)
-        look_up_group("words3c", None, 3, ((KING, 0), (KING, 1)), 16384 + 320)
+        look_up_group("words3c", None, 3, ((KING, 0), (KING, 1)), 16384)
 
-        evaluate_chunk(2)
         last_bf = [tile("last_bf%d" % u, [P, 4 * HALF], BF16) for u in range(2)]
         last_q = [tile("last_q%d" % u, [P, HALF], U32) for u in range(2)]
         last_sc = [tile("last_sc%d" % u, [P, HALF], U8) for u in range(2)]
-        last_y = [tile("last_y%d" % u, [P, 2, HALF], F32) for u in range(2)]
-        capped = [placed("capped%d" % u, [P, HALF, 4], F32, 8192 * LAST - 1024 + 2048 * u) for u in range(2)]
+        last_y = [tile("last_y0", [P, 2, HALF], F32), placed("last_y1", [P, 2, HALF], F32, 8192 * LAST)]
+        capped = [tile("capped%d" % u, [P, HALF, 4], F32) for u in range(2)]
         for u in range(2):
             nc.vector.scalar_tensor_tensor(
                 out=capped[u][:],
@@ -358,16 +348,12 @@ def tile_list_chess_pattern_evaluation_kernel(
                 op0=ALU.min,
                 op1=ALU.mult,
             )
-        flat = [capped[u][:].rearrange("p n t -> p (n t)") for u in range(2)]
-        floored = placed("floored", [P, 4 * HALF], F32, w_at[LAST])
-        nc.scalar.activation(out=floored[:], in_=flat[0], func=ACT.Relu)
-        nc.scalar.activation(out=last_bf[0][:], in_=floored[:], func=ACT.Square)
-        nc.vector.scalar_tensor_tensor(
-            out=last_bf[1][:], in0=flat[1], scalar=0.0, in1=flat[1], op0=ALU.max, op1=ALU.mult
-        )
-        store_chunk(2)
+        for u in range(2):
+            flat = capped[u][:].rearrange("p n t -> p (n t)")
+            nc.vector.scalar_tensor_tensor(out=last_bf[u][:], in0=flat, scalar=0.0, in1=flat, op0=ALU.max, op1=ALU.mult)
         for u in range(2):
             evaluate(last_bf[u : u + 1], last_q[u][:], last_sc[u][:], banks[1 + 2 * u], HALF)
+        evaluate_chunk(2)
         for u in range(2):
             for b in range(2):
                 src = banks[1 + 2 * u][:, HALF * b : HALF * (b + 1)]
@@ -378,3 +364,4 @@ def tile_list_chess_pattern_evaluation_kernel(
                     nc.vector.tensor_scalar(out=last_y[u][:, b, :], in0=src, scalar1=bias, scalar2=None, op0=ALU.add)
             lo = LAST * CH + HALF * u
             nc.sync.dma_start(out=out_v[:, :, lo : lo + HALF], in_=last_y[u][:])
+        store_chunk(2)

@@ -22,6 +22,8 @@ PASSES = 2
 CH = 256
 HALF = CH // 2
 LAST = S // CH - 1
+EARLY = 2
+RING = 6
 PIECE, KING, THREAT = 0, 1, 2
 
 
@@ -31,37 +33,36 @@ def tile_list_chess_pattern_evaluation_kernel(
     nc = tc.nc
     with ExitStack() as ctx:
         sb = ctx.enter_context(tc.tile_pool(name="sb", bufs=1))
-        reused = ctx.enter_context(tc.tile_pool(name="reused", bufs=1))
+        ring = ctx.enter_context(tc.tile_pool(name="ring", bufs=1))
+        early = ctx.enter_context(tc.tile_pool(name="early", bufs=1))
+        scratch = ctx.enter_context(tc.tile_pool(name="scratch", bufs=1))
+        rounded = ctx.enter_context(tc.tile_pool(name="rounded", bufs=1))
         ps = ctx.enter_context(tc.psum_pool(name="ps", bufs=1))
 
-        def tile(name, shape, dtype, tag=None):
-            return sb.tile(shape, dtype, name=name, tag=tag or name, align_bytes=64)
+        def tile(name, shape, dtype):
+            return sb.tile(shape, dtype, name=name, align_bytes=64)
 
-        def placed(name, shape, dtype, offset):
-            return reused.tile(shape, dtype, name=name, align_bytes=64, offset=offset)
+        def placed(pool, name, shape, dtype, offset):
+            return pool.tile(shape, dtype, name=name, align_bytes=64, offset=offset)
 
         lists = [tile("list%d" % i, [P, S // 16], U16) for i in range(3)]
         tab_sc = tile("tab_sc", [P, T], U8)
         tab_w = [tile("tab_w%d" % a, [P, T], I32) for a in range(PASSES)]
         wk_sc_raw = tile("wk_sc_raw", [P, H], U8)
         wk_sc = tile("wk_sc", [P, H], U8)
-        wp_sc_raw = tile("wp_sc_raw", [P, PASSES * H], U8)
+        wp_sc_raw = placed(early, "wp_sc_raw", [P, PASSES * H], U8, 0)
         wp_sc = tile("wp_sc", [P, PASSES * H], U8)
         piece_sc = tile("piece_sc", [P, S], U8)
         piece_sc1 = tile("piece_sc1", [P, S], U8)
         wt_raw = [tile("wt_raw%d" % a, [P, 4, H], F32) for a in range(PASSES)]
-        wt_bf = [
-            [tile("wt_bf0", [P, 4 * H], BF16)],
-            [placed("wt_bf1", [P, 2 * H], BF16, 69632), tile("wt_bf2", [P, 2 * H], BF16)],
-        ]
+        wt_bf = [tile("wt_bf%d" % a, [P, 4 * H], BF16) for a in range(PASSES)]
         wt_q = [tile("wt_q%d" % a, [P, H], U32) for a in range(PASSES)]
         wt_sc = [tile("wt_sc%d" % a, [P, H], U8) for a in range(PASSES)]
-        wk_raw = placed("wk_raw", [P, PASSES, H], I32, 0)
+        wk_raw = tile("wk_raw", [P, PASSES, H], I32)
         wk_q = tile("wk_q", [P, PASSES * H], I32)
         wp_raw = tile("wp_raw", [P, PASSES, H // 2], I32)
         wp_q = tile("wp_q", [P, PASSES * 2 * H], U8)
         wo_raw = [tile("wo_raw%d" % j, [P, N], F32) for j in range(4)]
-        wo_sgn = placed("wo_sgn", [P, 4, N], BF16, 24576)
         wo_bf = tile("wo_bf", [P, 4 * N], BF16)
         wo_q = tile("wo_q", [P, N], U32)
         wo_sc = tile("wo_sc", [P, N], U8)
@@ -72,8 +73,8 @@ def tile_list_chess_pattern_evaluation_kernel(
 
         nc.vector.memset(tab_sc[:].bitcast(I32), 0)
         nc.vector.memset(gain_rows[:], 0.0)
-        nc.vector.memset(wk_sc_raw[:].bitcast(I32), 0)
         nc.vector.memset(wp_sc_raw[:].bitcast(I32), 0)
+        nc.vector.memset(wk_sc_raw[:].bitcast(I32), 0)
         nc.vector.memset(piece_sc1[:].bitcast(I32), 0)
         make_identity(nc, ident[:])
 
@@ -89,31 +90,29 @@ def tile_list_chess_pattern_evaluation_kernel(
                     out=dst[32 * q : 32 * q + 8, :].bitcast(I32), in_=scales[:, 4 * q : 4 * q + 4, :].bitcast(I32)
                 )
 
-        def load_wp_rows(q):
-            nc.sync.dma_start(
-                out=wp_sc_raw[32 * q : 32 * q + 4, :].bitcast(I32).rearrange("r (a c) -> r a c", a=PASSES),
-                in_=wp_scales[:, 4 * q : 4 * q + 4, :].rearrange("a r c -> r a c").bitcast(I32),
-            )
-
         nc.sync.dma_start(lists[PIECE][:], offs)
-        nc.sync.dma_start(lists[KING][:], offs2)
         nc.sync.dma_start(lists[THREAT][:], offs3)
+        nc.sync.dma_start(lists[KING][:], offs2)
         nc.sync.dma_start(out=wp_raw[:], in_=wp_words.rearrange("a p c -> p a c").bitcast(I32))
         load_packed_rows(tab_sc, tab_scales)
         load_tab(0)
         nc.sync.dma_start(out=gain_rows[0:4, :], in_=gain.rearrange("(q t e) -> t q e", t=4, e=8))
-        load_packed_rows(wk_sc_raw, wk_scales)
-        nc.sync.dma_start(out=wk_raw[:], in_=wk_words.rearrange("a p c i -> p a (c i)").bitcast(I32))
+        for q in range(4):
+            nc.sync.dma_start(
+                out=wp_sc_raw[32 * q : 32 * q + 4, :].bitcast(I32).rearrange("r (a c) -> r a c", a=PASSES),
+                in_=wp_scales[:, 4 * q : 4 * q + 4, :].rearrange("a r c -> r a c").bitcast(I32),
+            )
         load_wt(0)
         load_wt(1)
-        for q in range(4):
-            load_wp_rows(q)
-        load_tab(1)
-        wo_rows = wo.rearrange("(q j e) n -> j q e n", j=4, e=8)
-        for j in range(4):
-            nc.sync.dma_start(out=wo_raw[j][:], in_=wo_rows[j])
+        nc.sync.dma_start(out=wk_raw[:], in_=wk_words.rearrange("a p c i -> p a (c i)").bitcast(I32))
+        load_packed_rows(wk_sc_raw, wk_scales)
         with nc.allow_non_contiguous_dma(reason="one bias value a partition"):
             nc.sync.dma_start(out=bias_sb[:], in_=bo.rearrange("(b p) -> p b", p=P))
+        wo_rows = wo.rearrange("(q j e) n -> j q e n", j=4, e=8)
+        nc.sync.dma_start(out=wo_raw[0][:], in_=wo_rows[0])
+        load_tab(1)
+        for j in range(1, 4):
+            nc.sync.dma_start(out=wo_raw[j][:], in_=wo_rows[j])
 
         mag = tile("mag", [P, 4], F32)
         root = tile("root", [P, 4], F32)
@@ -136,21 +135,15 @@ def tile_list_chess_pattern_evaluation_kernel(
         def gather_words(kind, a, dst, start, count):
             nc.vector.tensor_copy(out=dst, in_=tab_w[a][:].bitcast(U32).indirect(offsets(kind, start, count)))
 
-        def cast_wt(a):
+        def quantize(codes, scales, src):
+            nc.vector.quantize_mx(out=codes.bitcast(FP8X4), scales=scales, in_=src)
+
+        def prepare_wt(a):
             src = wt_raw[a][:].rearrange("p j (q t u i) -> p t q u j i", t=4, u=2, i=4)
             for t in range(4):
-                part, first = divmod(512 * t, wt_bf[a][0].shape[1])
-                dst = wt_bf[a][part][:, first : first + 512].rearrange("p (q u i j) -> p q u j i", u=2, i=4, j=4)
+                dst = wt_bf[a][:, 512 * t : 512 * (t + 1)].rearrange("p (q u i j) -> p q u j i", u=2, i=4, j=4)
                 nc.scalar.copy(out=dst, in_=src[:, t])
-
-        def quantize(codes, scales, parts):
-            width = codes.shape[1] // len(parts)
-            for i, part in enumerate(parts):
-                cols = slice(width * i, width * (i + 1))
-                nc.vector.quantize_mx(out=codes[:, cols].bitcast(FP8X4), scales=scales[:, cols], in_=part[:])
-
-        def quantize_wt(a):
-            quantize(wt_q[a][:], wt_sc[a][:], wt_bf[a])
+            quantize(wt_q[a][:], wt_sc[a][:], wt_bf[a][:])
 
         planes = {}
         columns_done = {}
@@ -190,52 +183,78 @@ def tile_list_chess_pattern_evaluation_kernel(
                     stop=(done + width == 6 * 512),
                 )
 
-        def look_up(kind, a, c, words):
-            gather_words(kind, a, words, c * CH, CH)
-            multiply(kind, a, c, words)
+        def early_plane(kind):
+            plane = tile("early_plane%d" % kind, [P, EARLY * CH], U8)
+            gather_scales(kind, plane[:], 0, EARLY * CH)
+            for c in range(EARLY):
+                planes[(kind, c)] = plane[:, CH * c : CH * (c + 1)]
 
-        def look_up_group(name, tag, c, steps, offset=None):
-            shape = [P, len(steps) * CH]
-            words = tile(name, shape, U32, tag=tag) if offset is None else placed(name, shape, U32, offset)
-            for i, (kind, a) in enumerate(steps):
-                look_up(kind, a, c, words[:, CH * i : CH * (i + 1)])
+        def early_words(kind, first, words):
+            gather_words(kind, 0, words, first * CH, EARLY * CH)
+            return words
+
+        def multiply_early(kind, first, words):
+            for i in range(EARLY):
+                multiply(kind, 0, first + i, words[:, CH * i : CH * (i + 1)])
+
+        taken = []
+
+        def ring_tile(dtype):
+            taken.append(dtype)
+            n = len(taken) - 1
+            return placed(ring, "ring%d" % n, [P, CH], dtype, 4 * CH * (n % RING))
+
+        def late_plane(kind, c):
+            plane = ring_tile(U8)
+            gather_scales(kind, plane[:], c * CH, CH)
+            planes[(kind, c)] = plane[:]
+
+        def late_words(kind, a, c):
+            words = ring_tile(U32)
+            gather_words(kind, a, words[:], c * CH, CH)
+            multiply(kind, a, c, words[:])
 
         h_bf = [
-            [placed("h_bf%d" % c, [P, 2 * CH], BF16, 8192 * (c + 1)), tile("h_rest%d" % c, [P, 2 * CH], BF16)]
-            for c in range(LAST - 1)
+            [placed(rounded, "h_bf%d_%d" % (c, u), [P, 4 * HALF], BF16, 16 * HALF * (2 * c + u)) for u in range(2)]
+            for c in range(LAST)
         ]
-        h_bf.append([placed("h_bf%d" % (LAST - 1), [P, 4 * CH], BF16, 8192 * LAST)])
+        h_q = [tile("h_q%d" % c, [P, CH], U32) for c in range(LAST)]
         h_sc = [tile("h_sc%d" % c, [P, CH], U8) for c in range(LAST)]
-        w_at = [32768 + 8192 * c for c in range(LAST + 1)]
-        y_at = (w_at[2] - 1984, w_at[2] + 64, w_at[3] - 1984)
-        y_sb = [placed("y%d" % c, [P, 2, CH], F32, y_at[c]) for c in range(LAST)]
         out_v = out.rearrange("(b p) s -> p b s", p=P)
 
-        def hidden(c, width, src_banks, parts):
-            v = placed("v%d" % c, [P, 4 * width], F32, w_at[c] - 8192 + 64)
-            w = placed("w%d" % c, [P, 4, width], F32, w_at[c])
-            for b, bank in enumerate(src_banks):
+        def hidden(c):
+            v = placed(scratch, "v%d" % c, [P, 4, CH], F32, 0)
+            w = placed(scratch, "w%d" % c, [P, 4, CH], F32, 16 * CH)
+            for b in range(2):
                 nc.scalar.activation(
-                    out=v[:, 512 * b : 512 * (b + 1)], in_=bank[:], func=ACT.Relu, scale=-1.0, bias=1.0
-                )
-            for t in range(4):
-                nc.scalar.activation(
-                    out=w[:, t, :],
-                    in_=v[:, width * t : width * (t + 1)],
+                    out=v[:, 2 * b : 2 * b + 2, :].rearrange("p t n -> p (t n)"),
+                    in_=banks[2 * c + b][:],
                     func=ACT.Relu,
-                    scale=neg_root[:, t : t + 1],
-                    bias=root[:, t : t + 1],
+                    scale=-1.0,
+                    bias=1.0,
                 )
-            step = width // len(parts)
-            for i, part in enumerate(parts):
+            for x in (0, HALF):
+                for t in range(4):
+                    nc.scalar.activation(
+                        out=w[:, t, x : x + HALF],
+                        in_=v[:, t, x : x + HALF],
+                        func=ACT.Relu,
+                        scale=neg_root[:, t : t + 1],
+                        bias=root[:, t : t + 1],
+                    )
+            for u in range(2):
                 nc.scalar.activation(
-                    out=part[:].rearrange("p (n i t) -> p n t i", i=4, t=4),
-                    in_=w[:, :, step * i : step * (i + 1)].rearrange("p t (n i) -> p n t i", i=4),
+                    out=h_bf[c][u][:].rearrange("p (n i t) -> p n t i", i=4, t=4),
+                    in_=w[:, :, HALF * u : HALF * (u + 1)].rearrange("p t (n i) -> p n t i", i=4),
                     func=ACT.Square,
                 )
 
-        def evaluate(parts, codes, scales, bank, width):
-            quantize(codes, scales, parts)
+        def quantize_hidden(c):
+            for u in range(2):
+                cols = slice(HALF * u, HALF * (u + 1))
+                quantize(h_q[c][:, cols], h_sc[c][:, cols], h_bf[c][u][:])
+
+        def evaluate(codes, scales, bank, width):
             for b in range(2):
                 nc.tensor.matmul_mx(
                     out=bank[:, width * b : width * (b + 1)],
@@ -247,98 +266,82 @@ def tile_list_chess_pattern_evaluation_kernel(
                     stop=True,
                 )
 
-        def hidden_chunk(c):
-            hidden(c, CH, banks[2 * c : 2 * c + 2], h_bf[c])
-
-        def evaluate_chunk(c, tag=None):
-            h_q = tile("h_q%d" % c, [P, CH], U32, tag=tag)
-            evaluate(h_bf[c], h_q[:], h_sc[c][:], banks[2 * c], CH)
-
-        def store_chunk(c):
+        def add_bias(dst, bank, width):
             for b in range(2):
                 nc.scalar.activation(
-                    out=y_sb[c][:, b, :],
-                    in_=banks[2 * c][:, CH * b : CH * (b + 1)],
+                    out=dst[:, b, :],
+                    in_=bank[:, width * b : width * (b + 1)],
                     func=ACT.Identity,
                     bias=bias_sb[:, b : b + 1],
                 )
-            nc.sync.dma_start(out=out_v[:, :, c * CH : (c + 1) * CH], in_=y_sb[c][:])
 
+        nc.vector.tensor_copy(
+            out=wp_q[:].bitcast(I32).rearrange("p (a t q e) -> p a t q e", a=2, t=4, e=4),
+            in_=wp_raw[:].rearrange("p a (q t e) -> p a t q e", t=4, e=4),
+        )
         gather_scales(PIECE, piece_sc[:], 0, S)
         for q in range(4):
             nc.gpsimd.dma_start(
                 out=piece_sc1[32 * q : 32 * q + 4, :].bitcast(I32), in_=piece_sc[32 * q + 4 : 32 * q + 8, :].bitcast(I32)
             )
-
-        def whole_plane(kind, plane):
-            gather_scales(kind, plane[:], 0, S)
-            for c in range(LAST + 1):
-                planes[(kind, c)] = plane[:, CH * c : CH * (c + 1)]
-
-        def multiply_two(kind, words):
-            for c in range(2):
-                multiply(kind, 0, c, words[:, CH * c : CH * (c + 1)])
-
-        whole_plane(KING, tile("king_plane", [P, S], U8))
-        first_king = tile("first_king", [P, 2 * CH], U32)
-        gather_words(KING, 0, first_king[:], 0, 2 * CH)
-        nc.vector.tensor_copy(
-            out=wk_sc[:].bitcast(I32).rearrange("p (t q e) -> p t q e", t=4, e=2),
-            in_=wk_sc_raw[:].bitcast(I32).rearrange("p (q t e) -> p t q e", t=4, e=2),
-        )
-        nc.vector.tensor_copy(
-            out=wk_q[:].rearrange("p (a t q e) -> p a t q e", a=2, t=4, e=8),
-            in_=wk_raw[:].rearrange("p a (q t e) -> p a t q e", t=4, e=8),
-        )
-        multiply_two(KING, first_king)
-        whole_plane(THREAT, placed("threat_plane", [P, S], U8, 2048))
-        first_threat = placed("first_threat", [P, 2 * CH], U32, 0)
-        gather_words(THREAT, 0, first_threat[:], 0, 2 * CH)
-        cast_wt(0)
-        quantize_wt(0)
-        multiply_two(THREAT, first_threat)
+        early_plane(THREAT)
+        early_plane(KING)
         nc.vector.tensor_copy(
             out=wp_sc[:].bitcast(I32).rearrange("p (a t q e) -> p a t q e", a=2, t=4, e=2),
             in_=wp_sc_raw[:].bitcast(I32).rearrange("p (a q t e) -> p a t q e", a=2, t=4, e=2),
         )
+        first_piece = tile("first_piece", [P, EARLY * CH], U32)
+        multiply_early(PIECE, 0, early_words(PIECE, 0, first_piece[:]))
+        held = placed(early, "held", [P, 3, EARLY * CH], U32, 0)
+        multiply_early(PIECE, EARLY, early_words(PIECE, EARLY, held[:, 0, :]))
+        first_threat = early_words(THREAT, 0, held[:, 1, :])
+        first_king = early_words(KING, 0, held[:, 2, :])
+        prepare_wt(0)
+        multiply_early(THREAT, 0, first_threat)
         nc.vector.tensor_copy(
-            out=wp_q[:].bitcast(I32).rearrange("p (a t q e) -> p a t q e", a=2, t=4, e=4),
-            in_=wp_raw[:].rearrange("p a (q t e) -> p a t q e", t=4, e=4),
+            out=wk_q[:].rearrange("p (a t q e) -> p a t q e", a=2, t=4, e=8),
+            in_=wk_raw[:].rearrange("p a (q t e) -> p a t q e", t=4, e=8),
         )
-        first_piece = tile("first_piece", [P, 2 * CH], U32, tag="wt_bf0")
-        gather_words(PIECE, 0, first_piece[:], 0, 2 * CH)
-        multiply_two(PIECE, first_piece)
-        cast_wt(1)
-        quantize_wt(1)
-        second = ((KING, 1), (THREAT, 1), (PIECE, 1))
-        look_up_group("second0", None, 0, second, 66688)
-        look_up_group("second1", None, 1, second, 71616)
+        nc.vector.tensor_copy(
+            out=wk_sc[:].bitcast(I32).rearrange("p (t q e) -> p t q e", t=4, e=2),
+            in_=wk_sc_raw[:].bitcast(I32).rearrange("p (q t e) -> p t q e", t=4, e=2),
+        )
+        multiply_early(KING, 0, first_king)
+        prepare_wt(1)
+
+        for c in range(EARLY):
+            for kind in (PIECE, KING, THREAT):
+                late_words(kind, 1, c)
+        wo_sgn = placed(scratch, "wo_sgn", [P, 4, N], BF16, 0)
         for j in range(4):
             nc.scalar.activation(out=wo_sgn[:, j, :], in_=wo_raw[j][:], func=ACT.Copy, scale=sgn[:, j : j + 1])
         nc.scalar.copy(
             out=wo_bf[:].rearrange("p (n i j) -> p n j i", i=4, j=4),
             in_=wo_sgn[:].rearrange("p j (n i) -> p n j i", i=4),
         )
-        hidden_chunk(0)
+        quantize(wo_q[:], wo_sc[:], wo_bf[:])
+        for c in range(EARLY):
+            hidden(c)
 
-        look_up_group("words2a", None, 2, ((PIECE, 0), (PIECE, 1)), 66688 + 576)
-        look_up_group("words2b", None, 2, ((THREAT, 0), (THREAT, 1), (KING, 0), (KING, 1)), 66688 + 64 - 4096)
-        nc.vector.quantize_mx(out=wo_q[:].bitcast(FP8X4), scales=wo_sc[:], in_=wo_bf[:])
-        evaluate_chunk(0)
-        hidden_chunk(1)
+        for c in range(EARLY, LAST + 1):
+            late_words(PIECE, 1, c)
+            for kind in (THREAT, KING):
+                late_plane(kind, c)
+                for a in range(PASSES):
+                    late_words(kind, a, c)
+        hidden(EARLY)
 
-        look_up_group("words3a", None, 3, ((PIECE, 0), (PIECE, 1), (THREAT, 0), (THREAT, 1)), 8192)
-        evaluate_chunk(1)
-        hidden_chunk(2)
-        store_chunk(0)
-        store_chunk(1)
-        look_up_group("words3c", None, 3, ((KING, 0), (KING, 1)), 16384)
+        early_y = placed(scratch, "early_y", [P, 2, EARLY * CH], F32, 0)
+        for c in range(EARLY):
+            quantize_hidden(c)
+            evaluate(h_q[c][:], h_sc[c][:], banks[2 * c], CH)
+            add_bias(early_y[:, :, CH * c : CH * (c + 1)], banks[2 * c], CH)
+        nc.sync.dma_start(out=out_v[:, :, 0 : EARLY * CH], in_=early_y[:])
 
-        last_bf = [tile("last_bf%d" % u, [P, 4 * HALF], BF16) for u in range(2)]
-        last_q = [tile("last_q%d" % u, [P, HALF], U32) for u in range(2)]
-        last_sc = [tile("last_sc%d" % u, [P, HALF], U8) for u in range(2)]
-        last_y = [tile("last_y0", [P, 2, HALF], F32), placed("last_y1", [P, 2, HALF], F32, 8192 * LAST)]
-        capped = [tile("capped%d" % u, [P, HALF, 4], F32) for u in range(2)]
+        capped = [
+            placed(rounded, "capped0", [P, HALF, 4], F32, 32 * HALF * (EARLY - 1)),
+            tile("capped1", [P, HALF, 4], F32),
+        ]
         for u in range(2):
             nc.vector.scalar_tensor_tensor(
                 out=capped[u][:],
@@ -348,20 +351,33 @@ def tile_list_chess_pattern_evaluation_kernel(
                 op0=ALU.min,
                 op1=ALU.mult,
             )
+        quantize_hidden(EARLY)
+        evaluate(h_q[EARLY][:], h_sc[EARLY][:], banks[2 * EARLY], CH)
+        mid_y = tile("mid_y", [P, 2, CH], F32)
+        add_bias(mid_y, banks[2 * EARLY], CH)
+        nc.sync.dma_start(out=out_v[:, :, EARLY * CH : LAST * CH], in_=mid_y[:])
+
+        last_bf = placed(rounded, "last_bf", [P, 2, 4 * HALF], BF16, 32 * HALF * EARLY)
+        last_q = [tile("last_q%d" % u, [P, HALF], U32) for u in range(2)]
+        last_sc = [tile("last_sc%d" % u, [P, HALF], U8) for u in range(2)]
+        last_y = [tile("last_y%d" % u, [P, 2, HALF], F32) for u in range(2)]
         for u in range(2):
             flat = capped[u][:].rearrange("p n t -> p (n t)")
-            nc.vector.scalar_tensor_tensor(out=last_bf[u][:], in0=flat, scalar=0.0, in1=flat, op0=ALU.max, op1=ALU.mult)
+            nc.vector.scalar_tensor_tensor(out=last_bf[:, u, :], in0=flat, scalar=0.0, in1=flat, op0=ALU.max, op1=ALU.mult)
         for u in range(2):
-            evaluate(last_bf[u : u + 1], last_q[u][:], last_sc[u][:], banks[1 + 2 * u], HALF)
-        evaluate_chunk(2)
+            quantize(last_q[u][:], last_sc[u][:], last_bf[:, u, :])
+            evaluate(last_q[u][:], last_sc[u][:], banks[1 + 2 * u], HALF)
         for u in range(2):
-            for b in range(2):
-                src = banks[1 + 2 * u][:, HALF * b : HALF * (b + 1)]
-                bias = bias_sb[:, b : b + 1]
-                if u == 0:
-                    nc.scalar.activation(out=last_y[u][:, b, :], in_=src, func=ACT.Identity, bias=bias)
-                else:
-                    nc.vector.tensor_scalar(out=last_y[u][:, b, :], in0=src, scalar1=bias, scalar2=None, op0=ALU.add)
+            if u == 0:
+                add_bias(last_y[u], banks[1], HALF)
+            else:
+                for b in range(2):
+                    nc.vector.tensor_scalar(
+                        out=last_y[u][:, b, :],
+                        in0=banks[3][:, HALF * b : HALF * (b + 1)],
+                        scalar1=bias_sb[:, b : b + 1],
+                        scalar2=None,
+                        op0=ALU.add,
+                    )
             lo = LAST * CH + HALF * u
             nc.sync.dma_start(out=out_v[:, :, lo : lo + HALF], in_=last_y[u][:])
-        store_chunk(2)

@@ -183,10 +183,12 @@ def tile_list_chess_pattern_evaluation_kernel(
                     stop=(done + width == 6 * 512),
                 )
 
+        early_planes = {THREAT: EARLY + 1, KING: EARLY}
+
         def early_plane(kind):
-            plane = tile("early_plane%d" % kind, [P, EARLY * CH], U8)
-            gather_scales(kind, plane[:], 0, EARLY * CH)
-            for c in range(EARLY):
+            plane = tile("early_plane%d" % kind, [P, early_planes[kind] * CH], U8)
+            gather_scales(kind, plane[:], 0, early_planes[kind] * CH)
+            for c in range(early_planes[kind]):
                 planes[(kind, c)] = plane[:, CH * c : CH * (c + 1)]
 
         def early_words(kind, first, words):
@@ -298,11 +300,11 @@ def tile_list_chess_pattern_evaluation_kernel(
         first_king = early_words(KING, 0, held[:, 2, :])
         prepare_wt(0)
         multiply_early(THREAT, 0, first_threat)
-        nc.vector.tensor_copy(
+        nc.gpsimd.tensor_copy(
             out=wk_q[:].rearrange("p (a t q e) -> p a t q e", a=2, t=4, e=8),
             in_=wk_raw[:].rearrange("p a (q t e) -> p a t q e", t=4, e=8),
         )
-        nc.vector.tensor_copy(
+        nc.gpsimd.tensor_copy(
             out=wk_sc[:].bitcast(I32).rearrange("p (t q e) -> p t q e", t=4, e=2),
             in_=wk_sc_raw[:].bitcast(I32).rearrange("p (q t e) -> p t q e", t=4, e=2),
         )
@@ -326,7 +328,8 @@ def tile_list_chess_pattern_evaluation_kernel(
         for c in range(EARLY, LAST + 1):
             late_words(PIECE, 1, c)
             for kind in (THREAT, KING):
-                late_plane(kind, c)
+                if c >= early_planes[kind]:
+                    late_plane(kind, c)
                 for a in range(PASSES):
                     late_words(kind, a, c)
         hidden(EARLY)

@@ -23,7 +23,7 @@ CH = 256
 HALF = CH // 2
 LAST = S // CH - 1
 EARLY = 2
-RING = 6
+RING = 7
 PIECE, KING, THREAT = 0, 1, 2
 
 
@@ -34,7 +34,6 @@ def tile_list_chess_pattern_evaluation_kernel(
     with ExitStack() as ctx:
         sb = ctx.enter_context(tc.tile_pool(name="sb", bufs=1))
         ring = ctx.enter_context(tc.tile_pool(name="ring", bufs=1))
-        early = ctx.enter_context(tc.tile_pool(name="early", bufs=1))
         scratch = ctx.enter_context(tc.tile_pool(name="scratch", bufs=1))
         rounded = ctx.enter_context(tc.tile_pool(name="rounded", bufs=1))
         ps = ctx.enter_context(tc.psum_pool(name="ps", bufs=1))
@@ -50,7 +49,7 @@ def tile_list_chess_pattern_evaluation_kernel(
         tab_w = [tile("tab_w%d" % a, [P, T], I32) for a in range(PASSES)]
         wk_sc_raw = tile("wk_sc_raw", [P, H], U8)
         wk_sc = tile("wk_sc", [P, H], U8)
-        wp_sc_raw = placed(early, "wp_sc_raw", [P, PASSES * H], U8, 0)
+        wp_sc_raw = tile("wp_sc_raw", [P, PASSES * H], U8)
         wp_sc = tile("wp_sc", [P, PASSES * H], U8)
         piece_sc = tile("piece_sc", [P, S], U8)
         piece_sc1 = tile("piece_sc1", [P, S], U8)
@@ -183,7 +182,7 @@ def tile_list_chess_pattern_evaluation_kernel(
                     stop=(done + width == 6 * 512),
                 )
 
-        early_planes = {THREAT: EARLY + 1, KING: EARLY}
+        early_planes = {THREAT: EARLY, KING: EARLY}
 
         def early_plane(kind):
             plane = tile("early_plane%d" % kind, [P, early_planes[kind] * CH], U8)
@@ -282,19 +281,16 @@ def tile_list_chess_pattern_evaluation_kernel(
             in_=wp_raw[:].rearrange("p a (q t e) -> p a t q e", t=4, e=4),
         )
         gather_scales(PIECE, piece_sc[:], 0, S)
-        for q in range(4):
-            nc.gpsimd.dma_start(
-                out=piece_sc1[32 * q : 32 * q + 4, :].bitcast(I32), in_=piece_sc[32 * q + 4 : 32 * q + 8, :].bitcast(I32)
-            )
+        nc.gpsimd.dma_start(out=piece_sc1[0:100, :].bitcast(I32), in_=piece_sc[4:104, :].bitcast(I32))
         early_plane(THREAT)
         early_plane(KING)
-        nc.vector.tensor_copy(
+        nc.gpsimd.tensor_copy(
             out=wp_sc[:].bitcast(I32).rearrange("p (a t q e) -> p a t q e", a=2, t=4, e=2),
             in_=wp_sc_raw[:].bitcast(I32).rearrange("p (a q t e) -> p a t q e", a=2, t=4, e=2),
         )
         first_piece = tile("first_piece", [P, EARLY * CH], U32)
         multiply_early(PIECE, 0, early_words(PIECE, 0, first_piece[:]))
-        held = placed(early, "held", [P, 3, EARLY * CH], U32, 0)
+        held = tile("held", [P, 3, EARLY * CH], U32)
         multiply_early(PIECE, EARLY, early_words(PIECE, EARLY, held[:, 0, :]))
         first_threat = early_words(THREAT, 0, held[:, 1, :])
         first_king = early_words(KING, 0, held[:, 2, :])
@@ -314,10 +310,12 @@ def tile_list_chess_pattern_evaluation_kernel(
         for c in range(EARLY):
             for kind in (PIECE, KING, THREAT):
                 late_words(kind, 1, c)
-        wo_sgn = placed(scratch, "wo_sgn", [P, 4, N], BF16, 0)
+        wo_sgn = tile("wo_sgn", [P, 4, N], BF16)
         for j in range(4):
-            nc.scalar.activation(out=wo_sgn[:, j, :], in_=wo_raw[j][:], func=ACT.Copy, scale=sgn[:, j : j + 1])
-        nc.scalar.copy(
+            nc.gpsimd.tensor_scalar(
+                out=wo_sgn[:, j, :], in0=wo_raw[j][:], scalar1=sgn[:, j : j + 1], scalar2=0.0, op0=ALU.mult, op1=ALU.add
+            )
+        nc.gpsimd.tensor_copy(
             out=wo_bf[:].rearrange("p (n i j) -> p n j i", i=4, j=4),
             in_=wo_sgn[:].rearrange("p j (n i) -> p n j i", i=4),
         )

@@ -34,6 +34,8 @@ def tile_list_chess_pattern_evaluation_kernel(
     with ExitStack() as ctx:
         sb = ctx.enter_context(tc.tile_pool(name="sb", bufs=1))
         ring = ctx.enter_context(tc.tile_pool(name="ring", bufs=1))
+        early = ctx.enter_context(tc.tile_pool(name="early", bufs=1))
+        cast = ctx.enter_context(tc.tile_pool(name="cast", bufs=1))
         scratch = ctx.enter_context(tc.tile_pool(name="scratch", bufs=1))
         rounded = ctx.enter_context(tc.tile_pool(name="rounded", bufs=1))
         ps = ctx.enter_context(tc.psum_pool(name="ps", bufs=1))
@@ -49,21 +51,19 @@ def tile_list_chess_pattern_evaluation_kernel(
         tab_w = [tile("tab_w%d" % a, [P, T], I32) for a in range(PASSES)]
         wk_sc_raw = tile("wk_sc_raw", [P, H], U8)
         wk_sc = tile("wk_sc", [P, H], U8)
-        wp_sc_raw = tile("wp_sc_raw", [P, PASSES * H], U8)
+        wp_sc_raw = placed(early, "wp_sc_raw", [P, PASSES * H], U8, 4 * CH * KING)
         wp_sc = tile("wp_sc", [P, PASSES * H], U8)
         piece_sc = tile("piece_sc", [P, S], U8)
         piece_sc1 = tile("piece_sc1", [P, S], U8)
         wt_raw = [tile("wt_raw%d" % a, [P, 4, H], F32) for a in range(PASSES)]
-        wt_bf = [tile("wt_bf%d" % a, [P, 4 * H], BF16) for a in range(PASSES)]
+        wt_bf = [placed(cast, "wt_bf%d" % a, [P, 4 * H], BF16, 12 * H * a) for a in range(PASSES)]
         wt_q = [tile("wt_q%d" % a, [P, H], U32) for a in range(PASSES)]
         wt_sc = [tile("wt_sc%d" % a, [P, H], U8) for a in range(PASSES)]
         wk_raw = tile("wk_raw", [P, PASSES, H], I32)
-        wk_q = tile("wk_q", [P, PASSES * H], I32)
         wp_raw = tile("wp_raw", [P, PASSES, H // 2], I32)
         wp_q = tile("wp_q", [P, PASSES * 2 * H], U8)
         wo_raw = [tile("wo_raw%d" % j, [P, N], F32) for j in range(4)]
         wo_bf = tile("wo_bf", [P, 4 * N], BF16)
-        wo_q = tile("wo_q", [P, N], U32)
         wo_sc = tile("wo_sc", [P, N], U8)
         gain_rows = tile("gain_rows", [P, P], F32)
         ident = tile("ident", [P, P], F32)
@@ -103,15 +103,14 @@ def tile_list_chess_pattern_evaluation_kernel(
             )
         load_wt(0)
         load_wt(1)
-        nc.sync.dma_start(out=wk_raw[:], in_=wk_words.rearrange("a p c i -> p a (c i)").bitcast(I32))
         load_packed_rows(wk_sc_raw, wk_scales)
+        nc.sync.dma_start(out=wk_raw[:], in_=wk_words.rearrange("a p c i -> p a (c i)").bitcast(I32))
+        wo_rows = wo.rearrange("(q j e) n -> j q e n", j=4, e=8)
+        load_tab(1)
+        for j in range(4):
+            nc.sync.dma_start(out=wo_raw[j][:], in_=wo_rows[j])
         with nc.allow_non_contiguous_dma(reason="one bias value a partition"):
             nc.sync.dma_start(out=bias_sb[:], in_=bo.rearrange("(b p) -> p b", p=P))
-        wo_rows = wo.rearrange("(q j e) n -> j q e n", j=4, e=8)
-        nc.sync.dma_start(out=wo_raw[0][:], in_=wo_rows[0])
-        load_tab(1)
-        for j in range(1, 4):
-            nc.sync.dma_start(out=wo_raw[j][:], in_=wo_rows[j])
 
         mag = tile("mag", [P, 4], F32)
         root = tile("root", [P, 4], F32)
@@ -182,16 +181,17 @@ def tile_list_chess_pattern_evaluation_kernel(
                     stop=(done + width == 6 * 512),
                 )
 
-        early_planes = {THREAT: EARLY, KING: EARLY}
+        early_planes = {THREAT: EARLY + 1, KING: EARLY}
 
         def early_plane(kind):
-            plane = tile("early_plane%d" % kind, [P, early_planes[kind] * CH], U8)
+            plane = placed(early, "early_plane%d" % kind, [P, early_planes[kind] * CH], U8, 4 * CH * kind)
             gather_scales(kind, plane[:], 0, early_planes[kind] * CH)
             for c in range(early_planes[kind]):
                 planes[(kind, c)] = plane[:, CH * c : CH * (c + 1)]
 
-        def early_words(kind, first, words):
-            gather_words(kind, 0, words, first * CH, EARLY * CH)
+        def early_words(kind, first):
+            words = tile("early_words%d_%d" % (kind, first), [P, EARLY * CH], U32)
+            gather_words(kind, 0, words[:], first * CH, EARLY * CH)
             return words
 
         def multiply_early(kind, first, words):
@@ -283,34 +283,35 @@ def tile_list_chess_pattern_evaluation_kernel(
         gather_scales(PIECE, piece_sc[:], 0, S)
         nc.gpsimd.dma_start(out=piece_sc1[0:100, :].bitcast(I32), in_=piece_sc[4:104, :].bitcast(I32))
         early_plane(THREAT)
-        early_plane(KING)
         nc.gpsimd.tensor_copy(
             out=wp_sc[:].bitcast(I32).rearrange("p (a t q e) -> p a t q e", a=2, t=4, e=2),
             in_=wp_sc_raw[:].bitcast(I32).rearrange("p (a q t e) -> p a t q e", a=2, t=4, e=2),
         )
-        first_piece = tile("first_piece", [P, EARLY * CH], U32)
-        multiply_early(PIECE, 0, early_words(PIECE, 0, first_piece[:]))
-        held = tile("held", [P, 3, EARLY * CH], U32)
-        multiply_early(PIECE, EARLY, early_words(PIECE, EARLY, held[:, 0, :]))
-        first_threat = early_words(THREAT, 0, held[:, 1, :])
-        first_king = early_words(KING, 0, held[:, 2, :])
+        multiply_early(PIECE, 0, early_words(PIECE, 0))
+        first_threat = early_words(THREAT, 0)
+        multiply_early(PIECE, EARLY, early_words(PIECE, EARLY))
+        early_plane(KING)
         prepare_wt(0)
+        first_king = placed(cast, "king_words", [P, EARLY * CH], U32, 0)
+        gather_words(KING, 0, first_king[:], 0, EARLY * CH)
         multiply_early(THREAT, 0, first_threat)
-        nc.gpsimd.tensor_copy(
-            out=wk_q[:].rearrange("p (a t q e) -> p a t q e", a=2, t=4, e=8),
-            in_=wk_raw[:].rearrange("p a (q t e) -> p a t q e", t=4, e=8),
-        )
         nc.gpsimd.tensor_copy(
             out=wk_sc[:].bitcast(I32).rearrange("p (t q e) -> p t q e", t=4, e=2),
             in_=wk_sc_raw[:].bitcast(I32).rearrange("p (q t e) -> p t q e", t=4, e=2),
         )
-        multiply_early(KING, 0, first_king)
+        wk_q = placed(cast, "wk_q", [P, PASSES * H], I32, 4 * H)
+        nc.gpsimd.tensor_copy(
+            out=wk_q[:].rearrange("p (a t q e) -> p a t q e", a=2, t=4, e=8),
+            in_=wk_raw[:].rearrange("p a (q t e) -> p a t q e", t=4, e=8),
+        )
         prepare_wt(1)
 
         for c in range(EARLY):
-            for kind in (PIECE, KING, THREAT):
-                late_words(kind, 1, c)
-        wo_sgn = tile("wo_sgn", [P, 4, N], BF16)
+            late_words(PIECE, 1, c)
+            multiply(KING, 0, c, first_king[:, CH * c : CH * (c + 1)])
+            late_words(THREAT, 1, c)
+            late_words(KING, 1, c)
+        wo_sgn = placed(cast, "wo_sgn", [P, 4, N], BF16, 12 * H)
         for j in range(4):
             nc.gpsimd.tensor_scalar(
                 out=wo_sgn[:, j, :], in0=wo_raw[j][:], scalar1=sgn[:, j : j + 1], scalar2=0.0, op0=ALU.mult, op1=ALU.add
@@ -319,7 +320,6 @@ def tile_list_chess_pattern_evaluation_kernel(
             out=wo_bf[:].rearrange("p (n i j) -> p n j i", i=4, j=4),
             in_=wo_sgn[:].rearrange("p j (n i) -> p n j i", i=4),
         )
-        quantize(wo_q[:], wo_sc[:], wo_bf[:])
         for c in range(EARLY):
             hidden(c)
 
@@ -331,6 +331,8 @@ def tile_list_chess_pattern_evaluation_kernel(
                 for a in range(PASSES):
                     late_words(kind, a, c)
         hidden(EARLY)
+        wo_q = placed(early, "wo_q", [P, N], U32, 4 * CH * THREAT)
+        quantize(wo_q[:], wo_sc[:], wo_bf[:])
 
         early_y = placed(scratch, "early_y", [P, 2, EARLY * CH], F32, 0)
         for c in range(EARLY):

@@ -55,8 +55,11 @@ def tile_list_chess_pattern_evaluation_kernel(
         wp_sc = tile("wp_sc", [P, PASSES * H], U8)
         piece_sc = tile("piece_sc", [P, S], U8)
         piece_sc1 = tile("piece_sc1", [P, S], U8)
-        wt_raw = [tile("wt_raw%d" % a, [P, 4, H], F32) for a in range(PASSES)]
-        wt_bf = [placed(cast, "wt_bf%d" % a, [P, 4 * H], BF16, 12 * H * a) for a in range(PASSES)]
+        wt_raw = [
+            [tile("wt_raw0", [P, 4, H], F32)],
+            [tile("wt_raw1", [P, 4, H // 2], F32), placed(cast, "wt_raw2", [P, 4, H // 2], F32, 0)],
+        ]
+        wt_bf = [tile("wt_bf0", [P, 4 * H], BF16), placed(ring, "wt_bf1", [P, 4 * H], BF16, 2 * CH)]
         wt_q = [tile("wt_q%d" % a, [P, H], U32) for a in range(PASSES)]
         wt_sc = [tile("wt_sc%d" % a, [P, H], U8) for a in range(PASSES)]
         wk_raw = tile("wk_raw", [P, PASSES, H], I32)
@@ -78,7 +81,10 @@ def tile_list_chess_pattern_evaluation_kernel(
         make_identity(nc, ident[:])
 
         def load_wt(a):
-            nc.sync.dma_start(out=wt_raw[a][:], in_=wt[512 * a : 512 * (a + 1), :].rearrange("(p j) c -> p j c", j=4))
+            rows = wt[512 * a : 512 * (a + 1), :].rearrange("(p j) c -> p j c", j=4)
+            width = H // len(wt_raw[a])
+            for i, part in enumerate(wt_raw[a]):
+                nc.sync.dma_start(out=part[:], in_=rows[:, :, width * i : width * (i + 1)])
 
         def load_tab(a):
             nc.sync.dma_start(out=tab_w[a][:], in_=tab_words[a].rearrange("p t i -> p (t i)").bitcast(I32))
@@ -102,11 +108,11 @@ def tile_list_chess_pattern_evaluation_kernel(
                 in_=wp_scales[:, 4 * q : 4 * q + 4, :].rearrange("a r c -> r a c").bitcast(I32),
             )
         load_wt(0)
-        load_wt(1)
         load_packed_rows(wk_sc_raw, wk_scales)
         nc.sync.dma_start(out=wk_raw[:], in_=wk_words.rearrange("a p c i -> p a (c i)").bitcast(I32))
         wo_rows = wo.rearrange("(q j e) n -> j q e n", j=4, e=8)
         load_tab(1)
+        load_wt(1)
         for j in range(4):
             nc.sync.dma_start(out=wo_raw[j][:], in_=wo_rows[j])
         with nc.allow_non_contiguous_dma(reason="one bias value a partition"):
@@ -137,10 +143,13 @@ def tile_list_chess_pattern_evaluation_kernel(
             nc.vector.quantize_mx(out=codes.bitcast(FP8X4), scales=scales, in_=src)
 
         def prepare_wt(a):
-            src = wt_raw[a][:].rearrange("p j (q t u i) -> p t q u j i", t=4, u=2, i=4)
-            for t in range(4):
-                dst = wt_bf[a][:, 512 * t : 512 * (t + 1)].rearrange("p (q u i j) -> p q u j i", u=2, i=4, j=4)
-                nc.scalar.copy(out=dst, in_=src[:, t])
+            width = H // len(wt_raw[a])
+            for i, part in enumerate(wt_raw[a]):
+                src = part[:].rearrange("p j (q t u i) -> p t q u j i", t=4, u=2, i=4)
+                for t in range(4):
+                    first = 512 * t + width * i
+                    dst = wt_bf[a][:, first : first + width].rearrange("p (q u i j) -> p q u j i", u=2, i=4, j=4)
+                    nc.scalar.copy(out=dst, in_=src[:, t])
             quantize(wt_q[a][:], wt_sc[a][:], wt_bf[a][:])
 
         planes = {}
@@ -181,7 +190,7 @@ def tile_list_chess_pattern_evaluation_kernel(
                     stop=(done + width == 6 * 512),
                 )
 
-        early_planes = {THREAT: EARLY + 1, KING: EARLY}
+        early_planes = {THREAT: LAST, KING: EARLY}
 
         def early_plane(kind):
             plane = placed(early, "early_plane%d" % kind, [P, early_planes[kind] * CH], U8, 4 * CH * kind)
@@ -210,8 +219,8 @@ def tile_list_chess_pattern_evaluation_kernel(
             gather_scales(kind, plane[:], c * CH, CH)
             planes[(kind, c)] = plane[:]
 
-        def late_words(kind, a, c):
-            words = ring_tile(U32)
+        def late_words(kind, a, c, words=None):
+            words = ring_tile(U32) if words is None else words
             gather_words(kind, a, words[:], c * CH, CH)
             multiply(kind, a, c, words[:])
 
@@ -219,7 +228,7 @@ def tile_list_chess_pattern_evaluation_kernel(
             [placed(rounded, "h_bf%d_%d" % (c, u), [P, 4 * HALF], BF16, 16 * HALF * (2 * c + u)) for u in range(2)]
             for c in range(LAST)
         ]
-        h_q = [tile("h_q%d" % c, [P, CH], U32) for c in range(LAST)]
+        h_q = {c: tile("h_q%d" % c, [P, CH], U32) for c in range(1, LAST)}
         h_sc = [tile("h_sc%d" % c, [P, CH], U8) for c in range(LAST)]
         out_v = out.rearrange("(b p) s -> p b s", p=P)
 
@@ -289,29 +298,32 @@ def tile_list_chess_pattern_evaluation_kernel(
         )
         multiply_early(PIECE, 0, early_words(PIECE, 0))
         first_threat = early_words(THREAT, 0)
-        multiply_early(PIECE, EARLY, early_words(PIECE, EARLY))
+        first_king = early_words(KING, 0)
         early_plane(KING)
-        prepare_wt(0)
-        first_king = placed(cast, "king_words", [P, EARLY * CH], U32, 0)
-        gather_words(KING, 0, first_king[:], 0, EARLY * CH)
-        multiply_early(THREAT, 0, first_threat)
         nc.gpsimd.tensor_copy(
             out=wk_sc[:].bitcast(I32).rearrange("p (t q e) -> p t q e", t=4, e=2),
             in_=wk_sc_raw[:].bitcast(I32).rearrange("p (q t e) -> p t q e", t=4, e=2),
         )
-        wk_q = placed(cast, "wk_q", [P, PASSES * H], I32, 4 * H)
+        wk_q = tile("wk_q", [P, PASSES * H], I32)
         nc.gpsimd.tensor_copy(
             out=wk_q[:].rearrange("p (a t q e) -> p a t q e", a=2, t=4, e=8),
             in_=wk_raw[:].rearrange("p a (q t e) -> p a t q e", t=4, e=8),
         )
+        multiply_early(KING, 0, first_king)
+        prepare_wt(0)
+        multiply_early(THREAT, 0, first_threat)
         prepare_wt(1)
 
-        for c in range(EARLY):
-            late_words(PIECE, 1, c)
-            multiply(KING, 0, c, first_king[:, CH * c : CH * (c + 1)])
-            late_words(THREAT, 1, c)
-            late_words(KING, 1, c)
-        wo_sgn = placed(cast, "wo_sgn", [P, 4, N], BF16, 12 * H)
+        late_words(PIECE, 1, 0, tile("piece_second0", [P, CH], U32))
+        late_words(KING, 1, 0, tile("king_second0", [P, CH], U32))
+        late_words(THREAT, 1, 0, placed(ring, "threat_second0", [P, CH], U32, 4 * CH * (RING - 2)))
+        late_words(PIECE, 1, 1, placed(early, "piece_second1", [P, CH], U32, 12 * CH))
+        late_words(THREAT, 1, 1, placed(ring, "threat_second1", [P, CH], U32, 4 * CH * (RING - 1)))
+        mid_plane = placed(cast, "mid_plane", [P, CH], U8, 0)
+        gather_scales(KING, mid_plane[:], EARLY * CH, CH)
+        planes[(KING, EARLY)] = mid_plane[:]
+        late_words(KING, 1, 1)
+        wo_sgn = placed(early, "wo_sgn", [P, 4, N], BF16, 12 * CH)
         for j in range(4):
             nc.gpsimd.tensor_scalar(
                 out=wo_sgn[:, j, :], in0=wo_raw[j][:], scalar1=sgn[:, j : j + 1], scalar2=0.0, op0=ALU.mult, op1=ALU.add
@@ -324,16 +336,18 @@ def tile_list_chess_pattern_evaluation_kernel(
             hidden(c)
 
         for c in range(EARLY, LAST + 1):
-            late_words(PIECE, 1, c)
+            for a in range(PASSES):
+                late_words(PIECE, a, c)
             for kind in (THREAT, KING):
-                if c >= early_planes[kind]:
+                if (kind, c) not in planes:
                     late_plane(kind, c)
                 for a in range(PASSES):
                     late_words(kind, a, c)
         hidden(EARLY)
-        wo_q = placed(early, "wo_q", [P, N], U32, 4 * CH * THREAT)
+        wo_q = placed(cast, "wo_q", [P, N], U32, 0)
         quantize(wo_q[:], wo_sc[:], wo_bf[:])
 
+        h_q[0] = ring_tile(U32)
         early_y = placed(scratch, "early_y", [P, 2, EARLY * CH], F32, 0)
         for c in range(EARLY):
             quantize_hidden(c)

@@ -98,8 +98,8 @@ def tile_list_chess_pattern_evaluation_kernel(
         nc.sync.dma_start(lists[PIECE][:], offs)
         nc.sync.dma_start(lists[THREAT][:], offs3)
         nc.sync.dma_start(lists[KING][:], offs2)
-        nc.sync.dma_start(out=wp_raw[:], in_=wp_words.rearrange("a p c -> p a c").bitcast(I32))
         load_packed_rows(tab_sc, tab_scales)
+        nc.sync.dma_start(out=wp_raw[:], in_=wp_words.rearrange("a p c -> p a c").bitcast(I32))
         load_tab(0)
         nc.sync.dma_start(out=gain_rows[0:4, :], in_=gain.rearrange("(q t e) -> t q e", t=4, e=8))
         for q in range(4):
@@ -209,10 +209,10 @@ def tile_list_chess_pattern_evaluation_kernel(
 
         taken = []
 
-        def ring_tile(dtype):
-            taken.append(dtype)
-            n = len(taken) - 1
-            return placed(ring, "ring%d" % n, [P, CH], dtype, 4 * CH * (n % RING))
+        def ring_tile(dtype, buffers=1):
+            n = len(taken)
+            taken.extend([dtype] * buffers)
+            return placed(ring, "ring%d" % n, [P, buffers * CH], dtype, 4 * CH * (n % RING))
 
         def late_plane(kind, c):
             plane = ring_tile(U8)
@@ -224,12 +224,9 @@ def tile_list_chess_pattern_evaluation_kernel(
             gather_words(kind, a, words[:], c * CH, CH)
             multiply(kind, a, c, words[:])
 
-        h_bf = [
-            [placed(rounded, "h_bf%d_%d" % (c, u), [P, 4 * HALF], BF16, 16 * HALF * (2 * c + u)) for u in range(2)]
-            for c in range(LAST)
-        ]
-        h_q = {c: tile("h_q%d" % c, [P, CH], U32) for c in range(1, LAST)}
-        h_sc = [tile("h_sc%d" % c, [P, CH], U8) for c in range(LAST)]
+        early_bf = placed(rounded, "early_bf", [P, EARLY, 2, 4 * HALF], BF16, 0)
+        h_bf = [[early_bf[:, c, u, :] for u in range(2)] for c in range(EARLY)]
+        h_bf.append([placed(rounded, "mid_bf%d" % u, [P, 4 * HALF], BF16, 16 * HALF * (2 * EARLY + u))[:] for u in range(2)])
         out_v = out.rearrange("(b p) s -> p b s", p=P)
 
         def hidden(c):
@@ -254,20 +251,18 @@ def tile_list_chess_pattern_evaluation_kernel(
                     )
             for u in range(2):
                 nc.scalar.activation(
-                    out=h_bf[c][u][:].rearrange("p (n i t) -> p n t i", i=4, t=4),
+                    out=h_bf[c][u].rearrange("p (n i t) -> p n t i", i=4, t=4),
                     in_=w[:, :, HALF * u : HALF * (u + 1)].rearrange("p t (n i) -> p n t i", i=4),
                     func=ACT.Square,
                 )
 
-        def quantize_hidden(c):
-            for u in range(2):
-                cols = slice(HALF * u, HALF * (u + 1))
-                quantize(h_q[c][:, cols], h_sc[c][:, cols], h_bf[c][u][:])
+        def halves(bank, width):
+            return [bank[:, width * b : width * (b + 1)] for b in range(2)]
 
-        def evaluate(codes, scales, bank, width):
+        def evaluate(codes, scales, sums):
             for b in range(2):
                 nc.tensor.matmul_mx(
-                    out=bank[:, width * b : width * (b + 1)],
+                    out=sums[b],
                     lhsT=wo_q[:, 128 * b : 128 * (b + 1)].bitcast(FP8X4),
                     lhsT_scale=wo_sc[:, 128 * b : 128 * (b + 1)],
                     rhs=codes.bitcast(FP8X4),
@@ -276,16 +271,16 @@ def tile_list_chess_pattern_evaluation_kernel(
                     stop=True,
                 )
 
-        def add_bias(dst, bank, width):
+        def add_bias(dst, sums):
             for b in range(2):
                 nc.scalar.activation(
                     out=dst[:, b, :],
-                    in_=bank[:, width * b : width * (b + 1)],
+                    in_=sums[b],
                     func=ACT.Identity,
                     bias=bias_sb[:, b : b + 1],
                 )
 
-        nc.vector.tensor_copy(
+        nc.gpsimd.tensor_copy(
             out=wp_q[:].bitcast(I32).rearrange("p (a t q e) -> p a t q e", a=2, t=4, e=4),
             in_=wp_raw[:].rearrange("p a (q t e) -> p a t q e", t=4, e=4),
         )
@@ -344,21 +339,19 @@ def tile_list_chess_pattern_evaluation_kernel(
                 for a in range(PASSES):
                     late_words(kind, a, c)
         hidden(EARLY)
-        wo_q = placed(cast, "wo_q", [P, N], U32, 0)
-        quantize(wo_q[:], wo_sc[:], wo_bf[:])
 
-        h_q[0] = ring_tile(U32)
+        early_q = ring_tile(U32, EARLY)
+        early_sc = tile("early_sc", [P, EARLY * CH], U8)
         early_y = placed(scratch, "early_y", [P, 2, EARLY * CH], F32, 0)
-        for c in range(EARLY):
-            quantize_hidden(c)
-            evaluate(h_q[c][:], h_sc[c][:], banks[2 * c], CH)
-            add_bias(early_y[:, :, CH * c : CH * (c + 1)], banks[2 * c], CH)
+        quantize(early_q[:], early_sc[:], early_bf[:].rearrange("p c u x -> p (c u x)"))
+        wo_q = ring_tile(U32)
+        quantize(wo_q[:], wo_sc[:], wo_bf[:])
+        early_sums = [banks[0][:], banks[2][:]]
+        evaluate(early_q[:], early_sc[:], early_sums)
+        add_bias(early_y, early_sums)
         nc.sync.dma_start(out=out_v[:, :, 0 : EARLY * CH], in_=early_y[:])
 
-        capped = [
-            placed(rounded, "capped0", [P, HALF, 4], F32, 32 * HALF * (EARLY - 1)),
-            tile("capped1", [P, HALF, 4], F32),
-        ]
+        capped = [tile("capped%d" % u, [P, HALF, 4], F32) for u in range(2)]
         for u in range(2):
             nc.vector.scalar_tensor_tensor(
                 out=capped[u][:],
@@ -368,10 +361,14 @@ def tile_list_chess_pattern_evaluation_kernel(
                 op0=ALU.min,
                 op1=ALU.mult,
             )
-        quantize_hidden(EARLY)
-        evaluate(h_q[EARLY][:], h_sc[EARLY][:], banks[2 * EARLY], CH)
+        mid_q = tile("mid_q", [P, CH], U32)
+        mid_sc = tile("mid_sc", [P, CH], U8)
+        for u in range(2):
+            cols = slice(HALF * u, HALF * (u + 1))
+            quantize(mid_q[:, cols], mid_sc[:, cols], h_bf[EARLY][u])
+        evaluate(mid_q[:], mid_sc[:], halves(banks[2 * EARLY], CH))
         mid_y = tile("mid_y", [P, 2, CH], F32)
-        add_bias(mid_y, banks[2 * EARLY], CH)
+        add_bias(mid_y, halves(banks[2 * EARLY], CH))
         nc.sync.dma_start(out=out_v[:, :, EARLY * CH : LAST * CH], in_=mid_y[:])
 
         last_bf = placed(rounded, "last_bf", [P, 2, 4 * HALF], BF16, 32 * HALF * EARLY)
@@ -383,10 +380,10 @@ def tile_list_chess_pattern_evaluation_kernel(
             nc.vector.scalar_tensor_tensor(out=last_bf[:, u, :], in0=flat, scalar=0.0, in1=flat, op0=ALU.max, op1=ALU.mult)
         for u in range(2):
             quantize(last_q[u][:], last_sc[u][:], last_bf[:, u, :])
-            evaluate(last_q[u][:], last_sc[u][:], banks[1 + 2 * u], HALF)
+            evaluate(last_q[u][:], last_sc[u][:], halves(banks[1 + 2 * u], HALF))
         for u in range(2):
             if u == 0:
-                add_bias(last_y[u], banks[1], HALF)
+                add_bias(last_y[u], halves(banks[1], HALF))
             else:
                 for b in range(2):
                     nc.vector.tensor_scalar(

@@ -78,7 +78,8 @@ def tile_list_chess_pattern_evaluation_kernel(
         nc.vector.memset(wp_sc_raw[:].bitcast(I32), 0)
         nc.vector.memset(wk_sc_raw[:].bitcast(I32), 0)
         nc.vector.memset(piece_sc1[:].bitcast(I32), 0)
-        make_identity(nc, ident[:])
+        nc.vector.memset(ident[:], 0.0)
+        make_identity(nc, ident[:], nomemset=True)
 
         def load_wt(a):
             rows = wt[512 * a : 512 * (a + 1), :].rearrange("(p j) c -> p j c", j=4)
@@ -190,7 +191,7 @@ def tile_list_chess_pattern_evaluation_kernel(
                     stop=(done + width == 6 * 512),
                 )
 
-        early_planes = {THREAT: LAST, KING: EARLY}
+        early_planes = {THREAT: EARLY, KING: EARLY}
 
         def early_plane(kind):
             plane = placed(early, "early_plane%d" % kind, [P, early_planes[kind] * CH], U8, 4 * CH * kind)
@@ -219,8 +220,8 @@ def tile_list_chess_pattern_evaluation_kernel(
             gather_scales(kind, plane[:], c * CH, CH)
             planes[(kind, c)] = plane[:]
 
-        def late_words(kind, a, c, words=None):
-            words = ring_tile(U32) if words is None else words
+        def late_words(kind, a, c):
+            words = ring_tile(U32)
             gather_words(kind, a, words[:], c * CH, CH)
             multiply(kind, a, c, words[:])
 
@@ -309,15 +310,19 @@ def tile_list_chess_pattern_evaluation_kernel(
         multiply_early(THREAT, 0, first_threat)
         prepare_wt(1)
 
-        late_words(PIECE, 1, 0, tile("piece_second0", [P, CH], U32))
-        late_words(KING, 1, 0, tile("king_second0", [P, CH], U32))
-        late_words(THREAT, 1, 0, placed(ring, "threat_second0", [P, CH], U32, 4 * CH * (RING - 2)))
-        late_words(PIECE, 1, 1, placed(early, "piece_second1", [P, CH], U32, 12 * CH))
-        late_words(THREAT, 1, 1, placed(ring, "threat_second1", [P, CH], U32, 4 * CH * (RING - 1)))
+        second = {
+            PIECE: tile("piece_second", [P, EARLY * CH], U32),
+            KING: placed(early, "king_second", [P, EARLY * CH], U32, 12 * CH),
+            THREAT: placed(ring, "threat_second", [P, EARLY * CH], U32, 4 * CH * (RING - EARLY)),
+        }
+        for kind in (PIECE, KING, THREAT):
+            gather_words(kind, 1, second[kind][:], 0, EARLY * CH)
+        for c, kinds in enumerate(((PIECE, KING, THREAT), (PIECE, THREAT, KING))):
+            for kind in kinds:
+                multiply(kind, 1, c, second[kind][:, CH * c : CH * (c + 1)])
         mid_plane = placed(cast, "mid_plane", [P, CH], U8, 0)
         gather_scales(KING, mid_plane[:], EARLY * CH, CH)
         planes[(KING, EARLY)] = mid_plane[:]
-        late_words(KING, 1, 1)
         wo_sgn = placed(early, "wo_sgn", [P, 4, N], BF16, 12 * CH)
         for j in range(4):
             nc.gpsimd.tensor_scalar(
@@ -330,9 +335,11 @@ def tile_list_chess_pattern_evaluation_kernel(
         for c in range(EARLY):
             hidden(c)
 
+        late_piece = ring_tile(U32, LAST + 1 - EARLY)
+        gather_words(PIECE, 0, late_piece[:], EARLY * CH, S - EARLY * CH)
+        multiply_early(PIECE, EARLY, late_piece)
         for c in range(EARLY, LAST + 1):
-            for a in range(PASSES):
-                late_words(PIECE, a, c)
+            late_words(PIECE, 1, c)
             for kind in (THREAT, KING):
                 if (kind, c) not in planes:
                     late_plane(kind, c)

@@ -378,15 +378,21 @@ def tile_list_chess_pattern_evaluation_kernel(
         add_bias(mid_y, halves(banks[2 * EARLY], CH))
         nc.sync.dma_start(out=out_v[:, :, EARLY * CH : LAST * CH], in_=mid_y[:])
 
-        last_bf = placed(rounded, "last_bf", [P, 2, 4 * HALF], BF16, 32 * HALF * EARLY)
-        last_q = [tile("last_q%d" % u, [P, HALF], U32) for u in range(2)]
+        last_bf = [
+            tile("last_bf0", [P, 4 * HALF], BF16),
+            placed(rounded, "last_bf1", [P, 4 * HALF], BF16, 32 * HALF * EARLY + 4 * HALF),
+        ]
+        last_q = [
+            placed(rounded, "last_q0", [P, HALF], U32, 32 * HALF * EARLY),
+            tile("last_q1", [P, HALF], U32),
+        ]
         last_sc = [tile("last_sc%d" % u, [P, HALF], U8) for u in range(2)]
         last_y = [tile("last_y%d" % u, [P, 2, HALF], F32) for u in range(2)]
         for u in range(2):
             flat = capped[u][:].rearrange("p n t -> p (n t)")
-            nc.vector.scalar_tensor_tensor(out=last_bf[:, u, :], in0=flat, scalar=0.0, in1=flat, op0=ALU.max, op1=ALU.mult)
+            nc.vector.scalar_tensor_tensor(out=last_bf[u][:], in0=flat, scalar=0.0, in1=flat, op0=ALU.max, op1=ALU.mult)
         for u in range(2):
-            quantize(last_q[u][:], last_sc[u][:], last_bf[:, u, :])
+            quantize(last_q[u][:], last_sc[u][:], last_bf[u][:])
             evaluate(last_q[u][:], last_sc[u][:], halves(banks[1 + 2 * u], HALF))
         for u in range(2):
             if u == 0:

@@ -191,7 +191,7 @@ def tile_list_chess_pattern_evaluation_kernel(
                     stop=(done + width == 6 * 512),
                 )
 
-        early_planes = {THREAT: EARLY, KING: EARLY}
+        early_planes = {THREAT: LAST, KING: EARLY}
 
         def early_plane(kind):
             plane = placed(early, "early_plane%d" % kind, [P, early_planes[kind] * CH], U8, 4 * CH * kind)

@@ -74,10 +74,11 @@ def tile_list_chess_pattern_evaluation_kernel(
         banks = [ps.tile([P, 512], F32, name="bank%d" % b) for b in range(8)]
 
         nc.vector.memset(tab_sc[:].bitcast(I32), 0)
-        nc.vector.memset(gain_rows[:], 0.0)
         nc.vector.memset(wp_sc_raw[:].bitcast(I32), 0)
         nc.vector.memset(wk_sc_raw[:].bitcast(I32), 0)
         nc.vector.memset(piece_sc1[:].bitcast(I32), 0)
+        nc.vector.memset(gain_rows[:], 0.0)
+        nc.gpsimd.dma_start(out=gain_rows[0:4, :], in_=gain.rearrange("(q t e) -> t q e", t=4, e=8))
         nc.vector.memset(ident[:], 0.0)
         make_identity(nc, ident[:], nomemset=True)
 
@@ -90,26 +91,31 @@ def tile_list_chess_pattern_evaluation_kernel(
         def load_tab(a):
             nc.sync.dma_start(out=tab_w[a][:], in_=tab_words[a].rearrange("p t i -> p (t i)").bitcast(I32))
 
-        def load_packed_rows(dst, scales):
-            for q in range(4):
+        def load_packed_rows(dst, scales, whole):
+            for q in range(whole):
                 nc.sync.dma_start(
                     out=dst[32 * q : 32 * q + 8, :].bitcast(I32), in_=scales[:, 4 * q : 4 * q + 4, :].bitcast(I32)
                 )
+            for q in range(whole, 4):
+                for a in range(PASSES):
+                    row = 32 * q + 4 * a
+                    nc.sync.dma_start(
+                        out=dst[row : row + 4, :].bitcast(I32), in_=scales[a, 4 * q : 4 * q + 4, :].bitcast(I32)
+                    )
 
         nc.sync.dma_start(lists[PIECE][:], offs)
         nc.sync.dma_start(lists[THREAT][:], offs3)
-        nc.sync.dma_start(lists[KING][:], offs2)
-        load_packed_rows(tab_sc, tab_scales)
-        nc.sync.dma_start(out=wp_raw[:], in_=wp_words.rearrange("a p c -> p a c").bitcast(I32))
+        load_packed_rows(tab_sc, tab_scales, 2)
         load_tab(0)
-        nc.sync.dma_start(out=gain_rows[0:4, :], in_=gain.rearrange("(q t e) -> t q e", t=4, e=8))
+        nc.sync.dma_start(lists[KING][:], offs2)
+        nc.sync.dma_start(out=wp_raw[:], in_=wp_words.rearrange("a p c -> p a c").bitcast(I32))
         for q in range(4):
             nc.sync.dma_start(
                 out=wp_sc_raw[32 * q : 32 * q + 4, :].bitcast(I32).rearrange("r (a c) -> r a c", a=PASSES),
                 in_=wp_scales[:, 4 * q : 4 * q + 4, :].rearrange("a r c -> r a c").bitcast(I32),
             )
         load_wt(0)
-        load_packed_rows(wk_sc_raw, wk_scales)
+        load_packed_rows(wk_sc_raw, wk_scales, 4)
         nc.sync.dma_start(out=wk_raw[:], in_=wk_words.rearrange("a p c i -> p a (c i)").bitcast(I32))
         wo_rows = wo.rearrange("(q j e) n -> j q e n", j=4, e=8)
         load_tab(1)
@@ -117,7 +123,7 @@ def tile_list_chess_pattern_evaluation_kernel(
         for j in range(4):
             nc.sync.dma_start(out=wo_raw[j][:], in_=wo_rows[j])
         with nc.allow_non_contiguous_dma(reason="one bias value a partition"):
-            nc.sync.dma_start(out=bias_sb[:], in_=bo.rearrange("(b p) -> p b", p=P))
+            nc.gpsimd.dma_start(out=bias_sb[:], in_=bo.rearrange("(b p) -> p b", p=P))
 
         mag = tile("mag", [P, 4], F32)
         root = tile("root", [P, 4], F32)

@@ -49,8 +49,8 @@ def tile_list_chess_pattern_evaluation_kernel(
         lists = [tile("list%d" % i, [P, S // 16], U16) for i in range(3)]
         tab_sc = tile("tab_sc", [P, T], U8)
         tab_w = [tile("tab_w%d" % a, [P, T], I32) for a in range(PASSES)]
-        wk_sc_raw = tile("wk_sc_raw", [P, H], U8)
-        wk_sc = tile("wk_sc", [P, H], U8)
+        wk_sc_raw = tile("wk_sc_raw", [P, PASSES * H], U8)
+        wk_sc = tile("wk_sc", [P, PASSES * H], U8)
         wp_sc_raw = placed(early, "wp_sc_raw", [P, PASSES * H], U8, 4 * CH * KING)
         wp_sc = tile("wp_sc", [P, PASSES * H], U8)
         piece_sc = tile("piece_sc", [P, S], U8)
@@ -103,19 +103,22 @@ def tile_list_chess_pattern_evaluation_kernel(
                         out=dst[row : row + 4, :].bitcast(I32), in_=scales[a, 4 * q : 4 * q + 4, :].bitcast(I32)
                     )
 
+        def load_side_by_side(dst, scales):
+            for q in range(4):
+                nc.sync.dma_start(
+                    out=dst[32 * q : 32 * q + 4, :].bitcast(I32).rearrange("r (a c) -> r a c", a=PASSES),
+                    in_=scales[:, 4 * q : 4 * q + 4, :].rearrange("a r c -> r a c").bitcast(I32),
+                )
+
         nc.sync.dma_start(lists[PIECE][:], offs)
         nc.sync.dma_start(lists[THREAT][:], offs3)
         load_packed_rows(tab_sc, tab_scales, 2)
         load_tab(0)
         nc.sync.dma_start(lists[KING][:], offs2)
         nc.sync.dma_start(out=wp_raw[:], in_=wp_words.rearrange("a p c -> p a c").bitcast(I32))
-        for q in range(4):
-            nc.sync.dma_start(
-                out=wp_sc_raw[32 * q : 32 * q + 4, :].bitcast(I32).rearrange("r (a c) -> r a c", a=PASSES),
-                in_=wp_scales[:, 4 * q : 4 * q + 4, :].rearrange("a r c -> r a c").bitcast(I32),
-            )
+        load_side_by_side(wp_sc_raw, wp_scales)
         load_wt(0)
-        load_packed_rows(wk_sc_raw, wk_scales, 4)
+        load_side_by_side(wk_sc_raw, wk_scales)
         nc.sync.dma_start(out=wk_raw[:], in_=wk_words.rearrange("a p c i -> p a (c i)").bitcast(I32))
         wo_rows = wo.rearrange("(q j e) n -> j q e n", j=4, e=8)
         load_tab(1)
@@ -168,7 +171,7 @@ def tile_list_chess_pattern_evaluation_kernel(
                 plane = (piece_sc, piece_sc1)[a][:, lo : lo + CH]
             else:
                 plane = planes[(kind, c)][4 * a : P, :]
-            width = HALF if kind == PIECE or c == LAST else CH
+            width = HALF if c == LAST or (kind == PIECE and c == EARLY) else CH
             if c == LAST:
                 steps = [(t, x, 2 * c + x // HALF, t * HALF) for x in (0, HALF) for t in range(4)]
             else:
@@ -181,7 +184,7 @@ def tile_list_chess_pattern_evaluation_kernel(
                     lhsT_sc = wp_sc[:, am]
                 elif kind == KING:
                     lhsT = wk_q[:, am].bitcast(FP8X4)
-                    lhsT_sc = wk_sc[4 * a : P, m]
+                    lhsT_sc = wk_sc[:, am]
                 else:
                     lhsT = wt_q[a][:, m].bitcast(FP8X4)
                     lhsT_sc = wt_sc[a][:, m]
@@ -238,7 +241,7 @@ def tile_list_chess_pattern_evaluation_kernel(
 
         def hidden(c):
             v = placed(scratch, "v%d" % c, [P, 4, CH], F32, 0)
-            w = placed(scratch, "w%d" % c, [P, 4, CH], F32, 16 * CH)
+            w = placed(scratch, "w%d" % c, [P, CH // 4, 4, 4], F32, 16 * CH)
             for b in range(2):
                 nc.scalar.activation(
                     out=v[:, 2 * b : 2 * b + 2, :].rearrange("p t n -> p (t n)"),
@@ -250,8 +253,8 @@ def tile_list_chess_pattern_evaluation_kernel(
             for x in (0, HALF):
                 for t in range(4):
                     nc.scalar.activation(
-                        out=w[:, t, x : x + HALF],
-                        in_=v[:, t, x : x + HALF],
+                        out=w[:, x // 4 : (x + HALF) // 4, t, :],
+                        in_=v[:, t, x : x + HALF].rearrange("p (n i) -> p n i", i=4),
                         func=ACT.Relu,
                         scale=neg_root[:, t : t + 1],
                         bias=root[:, t : t + 1],
@@ -259,7 +262,7 @@ def tile_list_chess_pattern_evaluation_kernel(
             for u in range(2):
                 nc.scalar.activation(
                     out=h_bf[c][u].rearrange("p (n i t) -> p n t i", i=4, t=4),
-                    in_=w[:, :, HALF * u : HALF * (u + 1)].rearrange("p t (n i) -> p n t i", i=4),
+                    in_=w[:, HALF // 4 * u : HALF // 4 * (u + 1)],
                     func=ACT.Square,
                 )
 
@@ -303,8 +306,8 @@ def tile_list_chess_pattern_evaluation_kernel(
         first_king = early_words(KING, 0)
         early_plane(KING)
         nc.gpsimd.tensor_copy(
-            out=wk_sc[:].bitcast(I32).rearrange("p (t q e) -> p t q e", t=4, e=2),
-            in_=wk_sc_raw[:].bitcast(I32).rearrange("p (q t e) -> p t q e", t=4, e=2),
+            out=wk_sc[:].bitcast(I32).rearrange("p (a t q e) -> p a t q e", a=2, t=4, e=2),
+            in_=wk_sc_raw[:].bitcast(I32).rearrange("p (a q t e) -> p a t q e", a=2, t=4, e=2),
         )
         wk_q = tile("wk_q", [P, PASSES * H], I32)
         nc.gpsimd.tensor_copy(

@@ -65,8 +65,7 @@ def tile_list_chess_pattern_evaluation_kernel(
         wk_raw = tile("wk_raw", [P, PASSES, H], I32)
         wp_raw = tile("wp_raw", [P, PASSES, H // 2], I32)
         wp_q = tile("wp_q", [P, PASSES * 2 * H], U8)
-        wo_raw = [tile("wo_raw%d" % j, [P, N], F32) for j in range(4)]
-        wo_bf = tile("wo_bf", [P, 4 * N], BF16)
+        wo_raw = tile("wo_raw", [P, 4, N], F32)
         wo_sc = tile("wo_sc", [P, N], U8)
         gain_rows = tile("gain_rows", [P, P], F32)
         ident = tile("ident", [P, P], F32)
@@ -124,7 +123,7 @@ def tile_list_chess_pattern_evaluation_kernel(
         load_tab(1)
         load_wt(1)
         for j in range(4):
-            nc.sync.dma_start(out=wo_raw[j][:], in_=wo_rows[j])
+            nc.sync.dma_start(out=wo_raw[:, j, :], in_=wo_rows[j])
         with nc.allow_non_contiguous_dma(reason="one bias value a partition"):
             nc.gpsimd.dma_start(out=bias_sb[:], in_=bo.rearrange("(b p) -> p b", p=P))
 
@@ -332,15 +331,14 @@ def tile_list_chess_pattern_evaluation_kernel(
         mid_plane = placed(cast, "mid_plane", [P, CH], U8, 0)
         gather_scales(KING, mid_plane[:], EARLY * CH, CH)
         planes[(KING, EARLY)] = mid_plane[:]
-        wo_sgn = placed(early, "wo_sgn", [P, 4, N], BF16, 12 * CH)
-        for j in range(4):
-            nc.gpsimd.tensor_scalar(
-                out=wo_sgn[:, j, :], in0=wo_raw[j][:], scalar1=sgn[:, j : j + 1], scalar2=0.0, op0=ALU.mult, op1=ALU.add
+        wo_bf = placed(early, "wo_bf", [P, 4 * N], BF16, 12 * CH)
+        for x in (0, HALF):
+            nc.gpsimd.tensor_tensor(
+                out=wo_bf[:, 4 * x : 4 * (x + HALF)].rearrange("p (n j) -> p n j", j=4),
+                in0=wo_raw[:, :, x : x + HALF].rearrange("p j n -> p n j"),
+                in1=sgn[:].unsqueeze(1).to_broadcast([P, HALF, 4]),
+                op=ALU.mult,
             )
-        nc.gpsimd.tensor_copy(
-            out=wo_bf[:].rearrange("p (n i j) -> p n j i", i=4, j=4),
-            in_=wo_sgn[:].rearrange("p j (n i) -> p n j i", i=4),
-        )
         for c in range(EARLY):
             hidden(c)
 

@@ -170,7 +170,7 @@ def tile_list_chess_pattern_evaluation_kernel(
                 plane = (piece_sc, piece_sc1)[a][:, lo : lo + CH]
             else:
                 plane = planes[(kind, c)][4 * a : P, :]
-            width = HALF if c == LAST or (kind == PIECE and c == EARLY) else CH
+            width = HALF if c == LAST else CH
             if c == LAST:
                 steps = [(t, x, 2 * c + x // HALF, t * HALF) for x in (0, HALF) for t in range(4)]
             else:
@@ -386,8 +386,8 @@ def tile_list_chess_pattern_evaluation_kernel(
         nc.sync.dma_start(out=out_v[:, :, EARLY * CH : LAST * CH], in_=mid_y[:])
 
         last_bf = [
-            tile("last_bf0", [P, 4 * HALF], BF16),
-            placed(rounded, "last_bf1", [P, 4 * HALF], BF16, 32 * HALF * EARLY + 4 * HALF),
+            placed(rounded, "last_bf0", [P, 4 * HALF], BF16, 32 * HALF * EARLY + 4 * HALF),
+            placed(rounded, "last_bf1", [P, 4 * HALF], BF16, 16 * HALF * (2 * EARLY + 1)),
         ]
         last_q = [
             placed(rounded, "last_q0", [P, HALF], U32, 32 * HALF * EARLY),

@@ -36,6 +36,7 @@ def tile_list_chess_pattern_evaluation_kernel(
         ring = ctx.enter_context(tc.tile_pool(name="ring", bufs=1))
         early = ctx.enter_context(tc.tile_pool(name="early", bufs=1))
         cast = ctx.enter_context(tc.tile_pool(name="cast", bufs=1))
+        late = ctx.enter_context(tc.tile_pool(name="late", bufs=1))
         scratch = ctx.enter_context(tc.tile_pool(name="scratch", bufs=1))
         rounded = ctx.enter_context(tc.tile_pool(name="rounded", bufs=1))
         ps = ctx.enter_context(tc.psum_pool(name="ps", bufs=1))
@@ -62,10 +63,10 @@ def tile_list_chess_pattern_evaluation_kernel(
         wt_bf = [tile("wt_bf0", [P, 4 * H], BF16), placed(ring, "wt_bf1", [P, 4 * H], BF16, 2 * CH)]
         wt_q = [tile("wt_q%d" % a, [P, H], U32) for a in range(PASSES)]
         wt_sc = [tile("wt_sc%d" % a, [P, H], U8) for a in range(PASSES)]
-        wk_raw = tile("wk_raw", [P, PASSES, H], I32)
+        wk_raw = [placed(late, "wk_raw0", [P, H], I32, 0), tile("wk_raw1", [P, H], I32)]
         wp_raw = tile("wp_raw", [P, PASSES, H // 2], I32)
         wp_q = tile("wp_q", [P, PASSES * 2 * H], U8)
-        wo_raw = tile("wo_raw", [P, 4, N], F32)
+        wo_raw = placed(late, "wo_raw", [P, 4, N], F32, 0)
         wo_sc = tile("wo_sc", [P, N], U8)
         gain_rows = tile("gain_rows", [P, P], F32)
         ident = tile("ident", [P, P], F32)
@@ -86,6 +87,9 @@ def tile_list_chess_pattern_evaluation_kernel(
             width = H // len(wt_raw[a])
             for i, part in enumerate(wt_raw[a]):
                 nc.sync.dma_start(out=part[:], in_=rows[:, :, width * i : width * (i + 1)])
+
+        def load_wk(a):
+            nc.sync.dma_start(out=wk_raw[a][:], in_=wk_words[a].rearrange("p c i -> p (c i)").bitcast(I32))
 
         def load_tab(a):
             nc.sync.dma_start(out=tab_w[a][:], in_=tab_words[a].rearrange("p t i -> p (t i)").bitcast(I32))
@@ -118,12 +122,11 @@ def tile_list_chess_pattern_evaluation_kernel(
         load_side_by_side(wp_sc_raw, wp_scales)
         load_wt(0)
         load_side_by_side(wk_sc_raw, wk_scales)
-        nc.sync.dma_start(out=wk_raw[:], in_=wk_words.rearrange("a p c i -> p a (c i)").bitcast(I32))
+        load_wk(0)
         wo_rows = wo.rearrange("(q j e) n -> j q e n", j=4, e=8)
         load_tab(1)
         load_wt(1)
-        for j in range(4):
-            nc.sync.dma_start(out=wo_raw[:, j, :], in_=wo_rows[j])
+        load_wk(1)
         with nc.allow_non_contiguous_dma(reason="one bias value a partition"):
             nc.gpsimd.dma_start(out=bias_sb[:], in_=bo.rearrange("(b p) -> p b", p=P))
 
@@ -309,10 +312,14 @@ def tile_list_chess_pattern_evaluation_kernel(
             in_=wk_sc_raw[:].bitcast(I32).rearrange("p (a q t e) -> p a t q e", a=2, t=4, e=2),
         )
         wk_q = tile("wk_q", [P, PASSES * H], I32)
-        nc.gpsimd.tensor_copy(
-            out=wk_q[:].rearrange("p (a t q e) -> p a t q e", a=2, t=4, e=8),
-            in_=wk_raw[:].rearrange("p a (q t e) -> p a t q e", t=4, e=8),
-        )
+        for a in range(PASSES):
+            nc.gpsimd.tensor_copy(
+                out=wk_q[:, H * a : H * (a + 1)].rearrange("p (t q e) -> p t q e", t=4, e=8),
+                in_=wk_raw[a][:].rearrange("p (q t e) -> p t q e", t=4, e=8),
+            )
+        for j in range(4):
+            queue = nc.gpsimd if j == 0 else nc.sync
+            queue.dma_start(out=wo_raw[:, j, :], in_=wo_rows[j])
         multiply_early(KING, 0, first_king)
         prepare_wt(0)
         multiply_early(THREAT, 0, first_threat)

@@ -63,8 +63,8 @@ def tile_list_chess_pattern_evaluation_kernel(
         wt_bf = [tile("wt_bf0", [P, 4 * H], BF16), placed(ring, "wt_bf1", [P, 4 * H], BF16, 2 * CH)]
         wt_q = [tile("wt_q%d" % a, [P, H], U32) for a in range(PASSES)]
         wt_sc = [tile("wt_sc%d" % a, [P, H], U8) for a in range(PASSES)]
-        wk_raw = [placed(late, "wk_raw0", [P, H], I32, 0), tile("wk_raw1", [P, H], I32)]
-        wp_raw = tile("wp_raw", [P, PASSES, H // 2], I32)
+        wk_raw = [tile("wk_raw0", [P, H], I32), placed(late, "wk_raw1", [P, H], I32, 0)]
+        wp_raw = [tile("wp_raw%d" % a, [P, H // 2], I32) for a in range(PASSES)]
         wp_q = tile("wp_q", [P, PASSES * 2 * H], U8)
         wo_raw = placed(late, "wo_raw", [P, 4, N], F32, 0)
         wo_sc = tile("wo_sc", [P, N], U8)
@@ -118,7 +118,7 @@ def tile_list_chess_pattern_evaluation_kernel(
         load_packed_rows(tab_sc, tab_scales, 2)
         load_tab(0)
         nc.sync.dma_start(lists[KING][:], offs2)
-        nc.sync.dma_start(out=wp_raw[:], in_=wp_words.rearrange("a p c -> p a c").bitcast(I32))
+        nc.sync.dma_start(out=wp_raw[0][:], in_=wp_words[0].bitcast(I32))
         load_side_by_side(wp_sc_raw, wp_scales)
         load_wt(0)
         load_side_by_side(wk_sc_raw, wk_scales)
@@ -126,6 +126,7 @@ def tile_list_chess_pattern_evaluation_kernel(
         wo_rows = wo.rearrange("(q j e) n -> j q e n", j=4, e=8)
         load_tab(1)
         load_wt(1)
+        nc.sync.dma_start(out=wp_raw[1][:], in_=wp_words[1].bitcast(I32))
         load_wk(1)
         with nc.allow_non_contiguous_dma(reason="one bias value a partition"):
             nc.gpsimd.dma_start(out=bias_sb[:], in_=bo.rearrange("(b p) -> p b", p=P))
@@ -292,10 +293,13 @@ def tile_list_chess_pattern_evaluation_kernel(
                     bias=bias_sb[:, b : b + 1],
                 )
 
-        nc.gpsimd.tensor_copy(
-            out=wp_q[:].bitcast(I32).rearrange("p (a t q e) -> p a t q e", a=2, t=4, e=4),
-            in_=wp_raw[:].rearrange("p a (q t e) -> p a t q e", t=4, e=4),
-        )
+        def deal_words(dealt, raw, run):
+            nc.gpsimd.tensor_copy(
+                out=dealt.rearrange("p (t q e) -> p t q e", t=4, e=run),
+                in_=raw[:].rearrange("p (q t e) -> p t q e", t=4, e=run),
+            )
+
+        deal_words(wp_q[:].bitcast(I32)[:, 0 : H // 2], wp_raw[0], 4)
         gather_scales(PIECE, piece_sc[:], 0, S)
         nc.gpsimd.dma_start(out=piece_sc1[0:100, :].bitcast(I32), in_=piece_sc[4:104, :].bitcast(I32))
         early_plane(THREAT)
@@ -312,13 +316,11 @@ def tile_list_chess_pattern_evaluation_kernel(
             in_=wk_sc_raw[:].bitcast(I32).rearrange("p (a q t e) -> p a t q e", a=2, t=4, e=2),
         )
         wk_q = tile("wk_q", [P, PASSES * H], I32)
-        for a in range(PASSES):
-            nc.gpsimd.tensor_copy(
-                out=wk_q[:, H * a : H * (a + 1)].rearrange("p (t q e) -> p t q e", t=4, e=8),
-                in_=wk_raw[a][:].rearrange("p (q t e) -> p t q e", t=4, e=8),
-            )
+        deal_words(wk_q[:, 0:H], wk_raw[0], 8)
+        deal_words(wp_q[:].bitcast(I32)[:, H // 2 : H], wp_raw[1], 4)
+        deal_words(wk_q[:, H : 2 * H], wk_raw[1], 8)
         for j in range(4):
-            queue = nc.gpsimd if j == 0 else nc.sync
+            queue = nc.gpsimd if j < 2 else nc.sync
             queue.dma_start(out=wo_raw[:, j, :], in_=wo_rows[j])
         multiply_early(KING, 0, first_king)
         prepare_wt(0)

from contextlib import ExitStack

import concourse.mybir as mybir
from concourse.masks import make_identity

K, T, S, H, N = 1024, 2048, 1024, 512, 256
FLOPS = 2 * (3 * K * H * S + H * N * S)

F32 = mybir.dt.float32
BF16 = mybir.dt.bfloat16
I32 = mybir.dt.int32
U32 = mybir.dt.uint32
U16 = mybir.dt.uint16
U8 = mybir.dt.uint8
FP8X4 = mybir.dt.float8_e4m3fn_x4
FP4X4 = mybir.dt.float4_e2m1fn_x4
ACT = mybir.ActivationFunctionType
ALU = mybir.AluOpType

P = 128
PASSES = 2
CH = 256
HALF = CH // 2
LAST = S // CH - 1
EARLY = 2
RING = 7
PIECE, KING, THREAT = 0, 1, 2


def tile_list_chess_pattern_evaluation_kernel(
    tc, tab_words, tab_scales, offs, offs2, offs3, wp_words, wp_scales, wk_words, wk_scales, wt, gain, wo, bo, out
):
    nc = tc.nc
    with ExitStack() as ctx:
        sb = ctx.enter_context(tc.tile_pool(name="sb", bufs=1))
        ring = ctx.enter_context(tc.tile_pool(name="ring", bufs=1))
        early = ctx.enter_context(tc.tile_pool(name="early", bufs=1))
        cast = ctx.enter_context(tc.tile_pool(name="cast", bufs=1))
        late = ctx.enter_context(tc.tile_pool(name="late", bufs=1))
        scratch = ctx.enter_context(tc.tile_pool(name="scratch", bufs=1))
        rounded = ctx.enter_context(tc.tile_pool(name="rounded", bufs=1))
        ps = ctx.enter_context(tc.psum_pool(name="ps", bufs=1))

        def tile(name, shape, dtype):
            return sb.tile(shape, dtype, name=name, align_bytes=64)

        def placed(pool, name, shape, dtype, offset):
            return pool.tile(shape, dtype, name=name, align_bytes=64, offset=offset)

        lists = [tile("list%d" % i, [P, S // 16], U16) for i in range(3)]
        tab_sc = tile("tab_sc", [P, T], U8)
        tab_w = [tile("tab_w%d" % a, [P, T], I32) for a in range(PASSES)]
        wk_sc_raw = tile("wk_sc_raw", [P, PASSES * H], U8)
        wk_sc = tile("wk_sc", [P, PASSES * H], U8)
        wp_sc_raw = placed(early, "wp_sc_raw", [P, PASSES * H], U8, 4 * CH * KING)
        wp_sc = tile("wp_sc", [P, PASSES * H], U8)
        piece_sc = tile("piece_sc", [P, S], U8)
        piece_sc1 = tile("piece_sc1", [P, S], U8)
        wt_raw = [
            [tile("wt_raw0", [P, 4, H], F32)],
            [tile("wt_raw1", [P, 4, H // 2], F32), placed(cast, "wt_raw2", [P, 4, H // 2], F32, 0)],
        ]
        wt_bf = [tile("wt_bf0", [P, 4 * H], BF16), placed(ring, "wt_bf1", [P, 4 * H], BF16, 2 * CH)]
        wt_q = [tile("wt_q%d" % a, [P, H], U32) for a in range(PASSES)]
        wt_sc = [tile("wt_sc%d" % a, [P, H], U8) for a in range(PASSES)]
        wk_raw = [tile("wk_raw0", [P, H], I32), placed(late, "wk_raw1", [P, H], I32, 0)]
        wp_raw = [tile("wp_raw%d" % a, [P, H // 2], I32) for a in range(PASSES)]
        wp_q = tile("wp_q", [P, PASSES * 2 * H], U8)
        wo_raw = placed(late, "wo_raw", [P, 4, N], F32, 0)
        wo_sc = tile("wo_sc", [P, N], U8)
        gain_rows = tile("gain_rows", [P, P], F32)
        ident = tile("ident", [P, P], F32)
        bias_sb = tile("bias_sb", [P, 2], F32)
        banks = [ps.tile([P, 512], F32, name="bank%d" % b) for b in range(8)]

        nc.vector.memset(tab_sc[:].bitcast(I32), 0)
        nc.vector.memset(wp_sc_raw[:].bitcast(I32), 0)
        nc.vector.memset(wk_sc_raw[:].bitcast(I32), 0)
        nc.vector.memset(piece_sc1[:].bitcast(I32), 0)
        nc.vector.memset(gain_rows[:], 0.0)
        nc.gpsimd.dma_start(out=gain_rows[0:4, :], in_=gain.rearrange("(q t e) -> t q e", t=4, e=8))
        nc.vector.memset(ident[:], 0.0)
        make_identity(nc, ident[:], nomemset=True)

        def load_wt(a):
            rows = wt[512 * a : 512 * (a + 1), :].rearrange("(p j) c -> p j c", j=4)
            width = H // len(wt_raw[a])
            for i, part in enumerate(wt_raw[a]):
                nc.sync.dma_start(out=part[:], in_=rows[:, :, width * i : width * (i + 1)])

        def load_wk(a):
            nc.sync.dma_start(out=wk_raw[a][:], in_=wk_words[a].rearrange("p c i -> p (c i)").bitcast(I32))

        def load_tab(a):
            nc.sync.dma_start(out=tab_w[a][:], in_=tab_words[a].rearrange("p t i -> p (t i)").bitcast(I32))

        def load_packed_rows(dst, scales, whole):
            for q in range(whole):
                nc.sync.dma_start(
                    out=dst[32 * q : 32 * q + 8, :].bitcast(I32), in_=scales[:, 4 * q : 4 * q + 4, :].bitcast(I32)
                )
            for q in range(whole, 4):
                for a in range(PASSES):
                    row = 32 * q + 4 * a
                    nc.sync.dma_start(
                        out=dst[row : row + 4, :].bitcast(I32), in_=scales[a, 4 * q : 4 * q + 4, :].bitcast(I32)
                    )

        def load_side_by_side(dst, scales):
            for q in range(4):
                nc.sync.dma_start(
                    out=dst[32 * q : 32 * q + 4, :].bitcast(I32).rearrange("r (a c) -> r a c", a=PASSES),
                    in_=scales[:, 4 * q : 4 * q + 4, :].rearrange("a r c -> r a c").bitcast(I32),
                )

        nc.sync.dma_start(lists[PIECE][:], offs)
        nc.sync.dma_start(lists[THREAT][:], offs3)
        load_packed_rows(tab_sc, tab_scales, 2)
        load_tab(0)
        nc.sync.dma_start(lists[KING][:], offs2)
        nc.sync.dma_start(out=wp_raw[0][:], in_=wp_words[0].bitcast(I32))
        load_side_by_side(wp_sc_raw, wp_scales)
        load_wt(0)
        load_side_by_side(wk_sc_raw, wk_scales)
        load_wk(0)
        wo_rows = wo.rearrange("(q j e) n -> j q e n", j=4, e=8)
        load_tab(1)
        load_wt(1)
        nc.sync.dma_start(out=wp_raw[1][:], in_=wp_words[1].bitcast(I32))
        load_wk(1)
        with nc.allow_non_contiguous_dma(reason="one bias value a partition"):
            nc.gpsimd.dma_start(out=bias_sb[:], in_=bo.rearrange("(b p) -> p b", p=P))

        mag = tile("mag", [P, 4], F32)
        root = tile("root", [P, 4], F32)
        neg_root = tile("neg_root", [P, 4], F32)
        sgn0 = tile("sgn0", [P, 4], F32)
        sgn = tile("sgn", [P, 4], F32)
        nc.tensor.transpose(banks[7][:, 0:P], gain_rows[:], ident[:])
        nc.scalar.activation(out=sgn0[:], in_=banks[7][:, 0:4], func=ACT.Sign)
        nc.scalar.activation(out=mag[:], in_=banks[7][:, 0:4], func=ACT.Abs)
        nc.scalar.activation(out=sgn[:], in_=sgn0[:], func=ACT.Sign, bias=0.5)
        nc.scalar.activation(out=root[:], in_=mag[:], func=ACT.Sqrt)
        nc.scalar.activation(out=neg_root[:], in_=root[:], func=ACT.Copy, scale=-1.0)

        def offsets(kind, start, count):
            return lists[kind][:, start // 16 : (start + count) // 16]

        def gather_scales(kind, dst, start, count):
            nc.vector.tensor_copy(out=dst, in_=tab_sc[:].indirect(offsets(kind, start, count)))

        def gather_words(kind, a, dst, start, count):
            nc.vector.tensor_copy(out=dst, in_=tab_w[a][:].bitcast(U32).indirect(offsets(kind, start, count)))

        def quantize(codes, scales, src):
            nc.vector.quantize_mx(out=codes.bitcast(FP8X4), scales=scales, in_=src)

        def prepare_wt(a):
            width = H // len(wt_raw[a])
            for i, part in enumerate(wt_raw[a]):
                src = part[:].rearrange("p j (q t u i) -> p t q u j i", t=4, u=2, i=4)
                for t in range(4):
                    first = 512 * t + width * i
                    dst = wt_bf[a][:, first : first + width].rearrange("p (q u i j) -> p q u j i", u=2, i=4, j=4)
                    nc.scalar.copy(out=dst, in_=src[:, t])
            quantize(wt_q[a][:], wt_sc[a][:], wt_bf[a][:])

        planes = {}
        columns_done = {}

        def multiply(kind, a, c, words):
            lo = c * CH
            if kind == PIECE:
                plane = (piece_sc, piece_sc1)[a][:, lo : lo + CH]
            else:
                plane = planes[(kind, c)][4 * a : P, :]
            width = HALF if c == LAST else CH
            if c == LAST:
                steps = [(t, x, 2 * c + x // HALF, t * HALF) for x in (0, HALF) for t in range(4)]
            else:
                steps = [(t, x, 2 * c + t // 2, (t % 2) * CH + x) for t in range(4) for x in range(0, CH, width)]
            for t, x, b, col in steps:
                m = slice(128 * t, 128 * (t + 1))
                am = slice(H * a + 128 * t, H * a + 128 * (t + 1))
                if kind == PIECE:
                    lhsT = wp_q[:, 256 * (4 * a + t) : 256 * (4 * a + t + 1)].bitcast(FP4X4)
                    lhsT_sc = wp_sc[:, am]
                elif kind == KING:
                    lhsT = wk_q[:, am].bitcast(FP8X4)
                    lhsT_sc = wk_sc[:, am]
                else:
                    lhsT = wt_q[a][:, m].bitcast(FP8X4)
                    lhsT_sc = wt_sc[a][:, m]
                done = columns_done.get(b, 0)
                columns_done[b] = done + width
                nc.tensor.matmul_mx(
                    out=banks[b][:, col : col + width],
                    lhsT=lhsT,
                    lhsT_scale=lhsT_sc,
                    rhs=words[:, x : x + width].bitcast(FP8X4),
                    rhs_scale=plane[:, x : x + width],
                    start=(done == 0),
                    stop=(done + width == 6 * 512),
                )

        early_planes = {THREAT: LAST, KING: EARLY}

        def early_plane(kind):
            plane = placed(early, "early_plane%d" % kind, [P, early_planes[kind] * CH], U8, 4 * CH * kind)
            gather_scales(kind, plane[:], 0, early_planes[kind] * CH)
            for c in range(early_planes[kind]):
                planes[(kind, c)] = plane[:, CH * c : CH * (c + 1)]

        def early_words(kind, first):
            words = tile("early_words%d_%d" % (kind, first), [P, EARLY * CH], U32)
            gather_words(kind, 0, words[:], first * CH, EARLY * CH)
            return words

        def multiply_early(kind, first, words):
            for i in range(EARLY):
                multiply(kind, 0, first + i, words[:, CH * i : CH * (i + 1)])

        taken = []

        def ring_tile(dtype, buffers=1):
            n = len(taken)
            taken.extend([dtype] * buffers)
            return placed(ring, "ring%d" % n, [P, buffers * CH], dtype, 4 * CH * (n % RING))

        def late_plane(kind, c):
            plane = ring_tile(U8)
            gather_scales(kind, plane[:], c * CH, CH)
            planes[(kind, c)] = plane[:]

        def late_words(kind, a, c):
            words = ring_tile(U32)
            gather_words(kind, a, words[:], c * CH, CH)
            multiply(kind, a, c, words[:])

        early_bf = placed(rounded, "early_bf", [P, EARLY, 2, 4 * HALF], BF16, 0)
        h_bf = [[early_bf[:, c, u, :] for u in range(2)] for c in range(EARLY)]
        h_bf.append([placed(rounded, "mid_bf%d" % u, [P, 4 * HALF], BF16, 16 * HALF * (2 * EARLY + u))[:] for u in range(2)])
        out_v = out.rearrange("(b p) s -> p b s", p=P)

        def hidden(c):
            v = placed(scratch, "v%d" % c, [P, 4, CH], F32, 0)
            w = placed(scratch, "w%d" % c, [P, CH // 4, 4, 4], F32, 16 * CH)
            for b in range(2):
                nc.scalar.activation(
                    out=v[:, 2 * b : 2 * b + 2, :].rearrange("p t n -> p (t n)"),
                    in_=banks[2 * c + b][:],
                    func=ACT.Relu,
                    scale=-1.0,
                    bias=1.0,
                )
            for x in (0, HALF):
                for t in range(4):
                    nc.scalar.activation(
                        out=w[:, x // 4 : (x + HALF) // 4, t, :],
                        in_=v[:, t, x : x + HALF].rearrange("p (n i) -> p n i", i=4),
                        func=ACT.Relu,
                        scale=neg_root[:, t : t + 1],
                        bias=root[:, t : t + 1],
                    )
            for u in range(2):
                nc.scalar.activation(
                    out=h_bf[c][u].rearrange("p (n i t) -> p n t i", i=4, t=4),
                    in_=w[:, HALF // 4 * u : HALF // 4 * (u + 1)],
                    func=ACT.Square,
                )

        def halves(bank, width):
            return [bank[:, width * b : width * (b + 1)] for b in range(2)]

        def evaluate(codes, scales, sums):
            for b in range(2):
                nc.tensor.matmul_mx(
                    out=sums[b],
                    lhsT=wo_q[:, 128 * b : 128 * (b + 1)].bitcast(FP8X4),
                    lhsT_scale=wo_sc[:, 128 * b : 128 * (b + 1)],
                    rhs=codes.bitcast(FP8X4),
                    rhs_scale=scales,
                    start=True,
                    stop=True,
                )

        def add_bias(dst, sums):
            for b in range(2):
                nc.scalar.activation(
                    out=dst[:, b, :],
                    in_=sums[b],
                    func=ACT.Identity,
                    bias=bias_sb[:, b : b + 1],
                )

        def deal_words(dealt, raw, run):
            nc.gpsimd.tensor_copy(
                out=dealt.rearrange("p (t q e) -> p t q e", t=4, e=run),
                in_=raw[:].rearrange("p (q t e) -> p t q e", t=4, e=run),
            )

        deal_words(wp_q[:].bitcast(I32)[:, 0 : H // 2], wp_raw[0], 4)
        gather_scales(PIECE, piece_sc[:], 0, S)
        nc.gpsimd.dma_start(out=piece_sc1[0:100, :].bitcast(I32), in_=piece_sc[4:104, :].bitcast(I32))
        early_plane(THREAT)
        nc.gpsimd.tensor_copy(
            out=wp_sc[:].bitcast(I32).rearrange("p (a t q e) -> p a t q e", a=2, t=4, e=2),
            in_=wp_sc_raw[:].bitcast(I32).rearrange("p (a q t e) -> p a t q e", a=2, t=4, e=2),
        )
        multiply_early(PIECE, 0, early_words(PIECE, 0))
        first_threat = early_words(THREAT, 0)
        first_king = early_words(KING, 0)
        early_plane(KING)
        nc.gpsimd.tensor_copy(
            out=wk_sc[:].bitcast(I32).rearrange("p (a t q e) -> p a t q e", a=2, t=4, e=2),
            in_=wk_sc_raw[:].bitcast(I32).rearrange("p (a q t e) -> p a t q e", a=2, t=4, e=2),
        )
        wk_q = tile("wk_q", [P, PASSES * H], I32)
        deal_words(wk_q[:, 0:H], wk_raw[0], 8)
        deal_words(wp_q[:].bitcast(I32)[:, H // 2 : H], wp_raw[1], 4)
        deal_words(wk_q[:, H : 2 * H], wk_raw[1], 8)
        for j in range(4):
            queue = nc.gpsimd if j < 2 else nc.sync
            queue.dma_start(out=wo_raw[:, j, :], in_=wo_rows[j])
        multiply_early(KING, 0, first_king)
        prepare_wt(0)
        multiply_early(THREAT, 0, first_threat)
        prepare_wt(1)

        second = {
            PIECE: tile("piece_second", [P, EARLY * CH], U32),
            KING: placed(early, "king_second", [P, EARLY * CH], U32, 12 * CH),
            THREAT: placed(ring, "threat_second", [P, EARLY * CH], U32, 4 * CH * (RING - EARLY)),
        }
        for kind in (PIECE, KING, THREAT):
            gather_words(kind, 1, second[kind][:], 0, EARLY * CH)
        for c, kinds in enumerate(((PIECE, KING, THREAT), (PIECE, THREAT, KING))):
            for kind in kinds:
                multiply(kind, 1, c, second[kind][:, CH * c : CH * (c + 1)])
        mid_plane = placed(cast, "mid_plane", [P, CH], U8, 0)
        gather_scales(KING, mid_plane[:], EARLY * CH, CH)
        planes[(KING, EARLY)] = mid_plane[:]
        wo_bf = placed(early, "wo_bf", [P, 4 * N], BF16, 12 * CH)
        for x in (0, HALF):
            nc.gpsimd.tensor_tensor(
                out=wo_bf[:, 4 * x : 4 * (x + HALF)].rearrange("p (n j) -> p n j", j=4),
                in0=wo_raw[:, :, x : x + HALF].rearrange("p j n -> p n j"),
                in1=sgn[:].unsqueeze(1).to_broadcast([P, HALF, 4]),
                op=ALU.mult,
            )
        for c in range(EARLY):
            hidden(c)

        late_piece = ring_tile(U32, LAST + 1 - EARLY)
        gather_words(PIECE, 0, late_piece[:], EARLY * CH, S - EARLY * CH)
        multiply_early(PIECE, EARLY, late_piece)
        for c in range(EARLY, LAST + 1):
            late_words(PIECE, 1, c)
            for kind in (THREAT, KING):
                if (kind, c) not in planes:
                    late_plane(kind, c)
                for a in range(PASSES):
                    late_words(kind, a, c)
        hidden(EARLY)

        early_q = ring_tile(U32, EARLY)
        early_sc = tile("early_sc", [P, EARLY * CH], U8)
        early_y = placed(scratch, "early_y", [P, 2, EARLY * CH], F32, 0)
        quantize(early_q[:], early_sc[:], early_bf[:].rearrange("p c u x -> p (c u x)"))
        wo_q = ring_tile(U32)
        quantize(wo_q[:], wo_sc[:], wo_bf[:])
        early_sums = [banks[0][:], banks[2][:]]
        evaluate(early_q[:], early_sc[:], early_sums)
        add_bias(early_y, early_sums)
        nc.sync.dma_start(out=out_v[:, :, 0 : EARLY * CH], in_=early_y[:])

        capped = [tile("capped%d" % u, [P, HALF, 4], F32) for u in range(2)]
        for u in range(2):
            nc.vector.scalar_tensor_tensor(
                out=capped[u][:],
                in0=banks[2 * LAST + u][:].rearrange("p (t n) -> p n t", t=4),
                scalar=1.0,
                in1=root[:].unsqueeze(1).to_broadcast([P, HALF, 4]),
                op0=ALU.min,
                op1=ALU.mult,
            )
        mid_q = tile("mid_q", [P, CH], U32)
        mid_sc = tile("mid_sc", [P, CH], U8)
        for u in range(2):
            cols = slice(HALF * u, HALF * (u + 1))
            quantize(mid_q[:, cols], mid_sc[:, cols], h_bf[EARLY][u])
        evaluate(mid_q[:], mid_sc[:], halves(banks[2 * EARLY], CH))
        mid_y = tile("mid_y", [P, 2, CH], F32)
        add_bias(mid_y, halves(banks[2 * EARLY], CH))
        nc.sync.dma_start(out=out_v[:, :, EARLY * CH : LAST * CH], in_=mid_y[:])

        last_bf = [
            placed(rounded, "last_bf0", [P, 4 * HALF], BF16, 32 * HALF * EARLY + 4 * HALF),
            placed(rounded, "last_bf1", [P, 4 * HALF], BF16, 16 * HALF * (2 * EARLY + 1)),
        ]
        last_q = [
            placed(rounded, "last_q0", [P, HALF], U32, 32 * HALF * EARLY),
            tile("last_q1", [P, HALF], U32),
        ]
        last_sc = [tile("last_sc%d" % u, [P, HALF], U8) for u in range(2)]
        last_y = [tile("last_y%d" % u, [P, 2, HALF], F32) for u in range(2)]
        for u in range(2):
            flat = capped[u][:].rearrange("p n t -> p (n t)")
            nc.vector.scalar_tensor_tensor(out=last_bf[u][:], in0=flat, scalar=0.0, in1=flat, op0=ALU.max, op1=ALU.mult)
        for u in range(2):
            quantize(last_q[u][:], last_sc[u][:], last_bf[u][:])
            evaluate(last_q[u][:], last_sc[u][:], halves(banks[1 + 2 * u], HALF))
        for u in range(2):
            if u == 0:
                add_bias(last_y[u], halves(banks[1], HALF))
            else:
                for b in range(2):
                    nc.vector.tensor_scalar(
                        out=last_y[u][:, b, :],
                        in0=banks[3][:, HALF * b : HALF * (b + 1)],
                        scalar1=bias_sb[:, b : b + 1],
                        scalar2=None,
                        op0=ALU.add,
                    )
            lo = LAST * CH + HALF * u
            nc.sync.dma_start(out=out_v[:, :, lo : lo + HALF], in_=last_y[u][:])
